import numpy as np, ml_dtypes
CORES = [2,6,10,14,18,22,26,30]
N = 8
BF = ml_dtypes.bfloat16
def gentries(a):
    return np.ascontiguousarray(a.reshape(8, 16, -1).transpose(0, 2, 1)).reshape(8, -1)
def gtable(e):
    e = np.asarray(e); return np.ascontiguousarray(e.reshape(8, -1, 16).transpose(0, 2, 1)).reshape(128, -1).astype(np.int32)
V, H, K, Q, PO, HP = 1536, 1152, 4, 384, 3, 2
W = V + 2 * H
ALL = (N, 8, 16, V)
def bases(rng):
    return rng.integers(32, 65, (1, 1, 16, 1)) * (1 - 2 * rng.integers(0, 2, (1, 1, 16, 1)))
def sky(rng, base, c):
    main = rng.choice(np.array([0, 1, 2]), (N, 8, 1, V), p=np.array([0.45, 0.35, 0.2]))
    camp = np.where(rng.random(ALL) < 0.3, rng.integers(0, 3, ALL), main)
    t = base + np.array([-90, 0, 90])[camp] + np.rint(c * rng.integers(-40, 41, ALL)).astype(np.int64)
    d = np.clip(np.rint(c * rng.integers(32, 129, ALL)), 32, 128).astype(np.int64)
    return t, d, drifts(rng)
def drifts(rng):
    return rng.integers(-256, 257, ALL) * np.where(rng.random((N, 8, 1, V)) < 0.5, 4, 1)
def agree(rng, base, ms):
    m = rng.choice(np.array(ms), (N, 8, 1, V)); off = np.argsort(rng.random(ALL), axis=2) >= m
    far = rng.integers(150, 181, ALL) * (1 - 2 * rng.integers(0, 2, ALL))
    return base + rng.integers(-8, 9, ALL) + np.where(off, far, 0), rng.integers(112, 129, ALL)
def nets(rng):
    o = np.argsort(rng.random((N, 8, V)), axis=-1); place = np.argsort(o, axis=-1)
    mate = np.take_along_axis(o[:, :, None], ((place >> 3) << 3)[:, :, None] + rng.integers(0, 8, (N, 8, K, V)), 3)
    u = rng.random((N, 8, K, V))
    s = np.where(u < 0.55, mate, np.where(u < 0.75, rng.integers(0, V, u.shape), rng.integers(V, W, u.shape)))
    j = rng.integers(0, K, (N, 8, 1, V))
    r = np.where(rng.random((N, 8, V)) < 0.8, np.take_along_axis(s, j, 2)[:, :, 0], rng.integers(0, W, (N, 8, V)))
    return s, r
def ring(rng):
    n = rng.integers(1, HP + 4, V); last = np.add.accumulate(n); i = np.arange(V)
    c = np.searchsorted(last, i, side="right"); first = last[c] - n[c]
    nx = np.where(i + 1 < np.minimum(last[c], V), i + 1, first); o = rng.permutation(V)
    y = np.zeros(V, np.int64); y[o] = o[nx]
    return y
def pack(t, d, f, s, r):
    e = np.ascontiguousarray(s.reshape(N, 8, K, 4, Q).transpose(0, 1, 3, 2, 4)).reshape(N, 8, K * V)
    return {"th": (t * 0.015625).astype(np.float32).astype(BF).reshape(N, 128, V), "dl": (d * 0.0078125).astype(np.float32).astype(BF).reshape(N, 128, V),
            "dr": (f * 0.0000152587890625).astype(np.float32).astype(BF).reshape(N, 128, V), "sl": np.stack([gtable(a) for a in e]), "rf": np.stack([gtable(a) for a in r])}
def setup_inputs(rng):
    t, d, f = sky(rng, bases(rng), 1.0); s, r = nets(rng)
    return pack(t, d, f, s, r)
def setup_inputs_corners(rng):
    base = bases(rng); t, d = agree(rng, base, [16, 16, 16, 15, 9, 9, 8, 8, 1, 0]); tc, dc = agree(rng, base, [16]); f = drifts(rng); s, r = nets(rng)
    calm = ((np.arange(N)[:, None] + np.arange(8)) & 1) == 0
    t = np.where(calm[:, :, None, None], tc, t); d = np.where(calm[:, :, None, None], dc, d)
    pts = np.array([0, V - 1, V, V + H - 1, V + H, W - 1])
    s = np.where(rng.random(s.shape) < 0.2, rng.choice(pts, s.shape), s); u = rng.random(r.shape)
    r = np.where(u < 0.5, rng.choice(pts, r.shape), np.where(u < 0.65, np.arange(V), r))
    for q in range(N):
        for g in range(8):
            if calm[q, g]:
                y = ring(rng); s[q, g, 0] = y; r[q, g] = y
    return pack(t, d, f, s, r)
def setup_inputs_crowd(rng):
    base = bases(rng); t, d, f = sky(rng, base, 1.0); s, r = nets(rng); tc, dc = agree(rng, base, [16, 15])
    kind = (np.arange(N)[:, None] + np.arange(8) + rng.integers(0, 4)) & 3; k = kind[:, :, None, None]
    t = np.where(k < 3, tc, t); d = np.where(k < 3, dc, d)
    one = rng.integers(0, W, (N, 8, 1, 1)); one[N - 1] = V - 1; one[:, 7] = W - 1
    few = rng.integers(0, W, (N, 8, 3)); three = np.take_along_axis(few, rng.integers(0, 3, (N, 8, K * V)), 2).reshape(N, 8, K, V)
    spare = np.arange(K)[:, None] == rng.integers(0, K, (N, 8, 1, V))
    s = np.where(k == 0, one, np.where(k == 1, np.where(spare, s, one), np.where(k == 2, three, s)))
    r = np.where(kind[:, :, None] < 2, one[:, :, 0], r)
    return pack(t, d, f, s, r)
def setup_inputs_ends(rng):
    t, d, f = sky(rng, bases(rng), 1.0); s, r = nets(rng); one = (N, 8, 1, V)
    flip = np.where(rng.random(ALL) < 0.25, -1, 1)
    t = np.where(rng.random(one) < 0.8, 256 * (1 - 2 * rng.integers(0, 2, one)) * flip, t)
    d = np.where(rng.random(one) < 0.8, rng.choice(np.array([32, 128]), ALL), d)
    f = np.where(rng.random(one) < 0.8, 1024 * (1 - 2 * rng.integers(0, 2, ALL)), f)
    s = np.where(rng.random(s.shape) < 0.7, rng.choice(np.array([0, W - 1]), s.shape), s)
    r = np.where(rng.random(r.shape) < 0.7, rng.choice(np.array([0, W - 1]), r.shape), r)
    v = np.arange(V); ix = v[(v % Q < 4) | (v % Q >= Q - 4)]; odd = (ix & 1) == 1; n = (N, 8, len(ix))
    t[..., ix] = np.where(odd, -256, 256); d[..., ix] = 128; f[..., ix] = np.where((ix & 2) == 2, -1024, 1024)
    for j in range(K):
        a, b = rng.choice(ix[odd], n), rng.choice(ix[~odd], n)
        s[:, :, j, ix] = np.where(odd, a, b) if j < K - 1 else np.where(odd, b, a)
    return pack(t, d, f, s, r)
def setup_inputs_spread(rng):
    c = np.exp2(rng.integers(-1, 2, (N, 8, 1, V)).astype(np.float64)); t, d, f = sky(rng, bases(rng), c); s, r = nets(rng)
    f = rng.integers(-256, 257, ALL) * (1 << rng.integers(0, 3, (N, 8, 1, V)))
    s = np.where(rng.random((N, 8, 1, V)) < 0.4, (W * rng.random(s.shape) ** 3).astype(np.int64), s)
    return pack(t, d, f, s, r)
def setup_inputs_ties(rng):
    base = rng.choice(np.array([-64, -32, 32, 64]), (1, 1, 16, 1)); s, r = nets(rng)
    main = rng.integers(-3, 4, (N, 8, 1, V)); t = base + 32 * np.where(rng.random(ALL) < 0.3, rng.integers(-3, 4, ALL), main)
    d = rng.choice(np.array([32, 64, 128]), ALL)
    f = rng.choice(np.array([0, 0, 0, 0, 0, 0, 0, 1, -1, 1024, -1024]), (N, 8, 1, V)) * rng.integers(0, 2, ALL)
    return pack(t, d, f, s, r)
def check_ranges(d):
    bad = []
    for k, lo, hi, u in (("th", -4.0, 4.0, 64.0), ("dl", 0.25, 1.0, 128.0), ("dr", -0.015625, 0.015625, 65536.0)):
        v = np.asarray(d[k]).astype(np.float64)
        if not (np.min(v) >= lo and np.max(v) <= hi): bad.append("range of " + k)
        elif np.any(np.rint(v * u) != v * u): bad.append("multiples of " + k)
    for k in ("sl", "rf"):
        if np.min(d[k]) < 0 or np.max(d[k]) > W - 1: bad.append("range of " + k)
    return bad
def view(a):
    return np.concatenate([a, np.roll(a, -1, axis=0)[..., :H], np.roll(a, -1, axis=1)[..., :H]], axis=3)
def reference(th, dl, dr, sl, rf):
    x, e, f = [a.astype(np.float64).reshape(N, 8, 16, V) for a in (th, dl, dr)]
    S = np.stack([gentries(a) for a in sl]).astype(np.int64).reshape(N, 8, 4, K, Q).transpose(0, 1, 3, 2, 4).reshape(N, 8, K, V)
    R = np.stack([gentries(a) for a in rf]).astype(np.int64)
    away = np.broadcast_to(np.arange(V, W), (N, 8, 2 * H))
    for poll in range(PO):
        ids = np.concatenate([np.arange(Q) + (poll & 1) * Q, np.arange(Q) + (2 + (poll & 1)) * Q])
        xw, ew, Sw = view(x), view(e), view(S); Sp = S[..., ids]; xo, eo = x[..., ids], e[..., ids]
        lo, hi = [], []
        for j in range(K):
            ix = Sp[:, :, j][:, :, None, :]; a = np.take_along_axis(xw, ix, 3); b = np.take_along_axis(ew, ix, 3)
            lo.append(a - b); hi.append(a + b)
        lo.append(xo - eo); hi.append(xo + eo)
        cnt = []
        for a in lo:
            c = np.zeros(a.shape, np.int64)
            for b, h in zip(lo, hi): c += (b <= a) & (a <= h)
            cnt.append(c)
        best = np.maximum.reduce(cnt)
        A = np.maximum.reduce([np.where(c == best, a, -64.0) for c, a in zip(cnt, lo)])
        hold = [(b <= A) & (A <= h) for b, h in zip(lo, hi)]
        B = np.minimum.reduce([np.where(m, h, 64.0) for m, h in zip(hold, hi)])
        n = np.stack([np.add.reduce(m.astype(np.int64), axis=2) for m in hold[:K]], axis=2)
        stay = n >= 9; score = np.where(stay, n, 0); top = np.argmax(score, axis=2); some = np.max(score, axis=2) > 0
        cand = np.take_along_axis(Sp, top[:, :, None], 2)[:, :, 0]
        Rw = np.concatenate([R, away], axis=2); h = cand; meet = h == ids
        for hop in range(HP):
            h = np.take_along_axis(Rw, h, 2); meet = meet | (h == ids)
        veto = some & meet
        fall = ~stay | (veto[:, :, None] & (np.arange(K)[:, None] == top[:, :, None]))
        w = np.where(some & ~meet, cand, R[..., ids]); ww = w[:, :, None]
        nm = np.take_along_axis(Sw, ww, 3)
        new = np.where(ww < V, nm, np.where(ww < V + H, V, V + H) + nm)
        Sn = np.where(fall & ((ww < V) | (nm < H)), new, Sp)
        x = x + f; e = e + 0.0625
        x[..., ids] = A + 0.5 * (B - A); e[..., ids] = 0.5 * (B - A) + 0.0625
        S = np.array(S); S[..., ids] = Sn; R = np.array(R); R[..., ids] = w
    xw, ew = view(x), view(e); y = 0.5 * e
    for j in range(K):
        ix = S[:, :, j][:, :, None, :]; z = np.take_along_axis(xw, ix, 3) - x
        y = y + np.take_along_axis(ew, ix, 3) * np.reciprocal(1.0 + np.exp(-z))
    return {"yt": x.reshape(N, 128, V).astype(np.float32), "yq": y.reshape(N, 128, V).astype(np.float32), "yr": np.asarray(R, np.float32)}

def check_inputs(d):
    bad = list(check_ranges(d))
    if not bad:
        for name, y in reference(**d).items():
            for q in range(N):
                v = np.abs(np.asarray(y[q], np.float64)); s = np.sqrt(np.mean(v * v))
                if v.max() > 11 * s or s < 2.0 ** -2: bad.append('%s of rank %d is uneven or too small' % (name, q))
    return bad

@@ -1,0 +1,729 @@
+import numpy as np
+from concourse.bass import DstId, RemoteDMATransfer
+from concourse.mybir import AluOpType, ActivationFunctionType
+
+Q = 384
+V = 1536
+W = 3840
+RK = 1536
+GR = 2688
+CR, CG, CW = 2400, 4200, 5744
+
+BASE_PE = (1, 1, 1, 1, 1)
+MASK_PE = (1, 1, 1, 1, 1)
+A_PE = (1, 0, 1, 0, 1, 0)
+DVE_G = (2, 0, 0, 0, 0, 0)
+XA = 3
+ACC = False
+NOFF = (0, 0, 0, 0, 0, 0)
+PE_NS = 0.47
+P = {"NET": 70.0, "NETLAT": 2600, "SEED": 14, "AMP": 700.0}
+
+SCRATCH = {}
+for _t in range(4):
+    SCRATCH["wl%d" % _t] = ("sbuf", [128, W], "float32")
+    SCRATCH["wh%d" % _t] = ("sbuf", [128, W], "float32")
+for _t in range(2):
+    SCRATCH["lo%d" % _t] = ("sbuf", [128, 5 * Q], "float32")
+    SCRATCH["hi%d" % _t] = ("sbuf", [128, 5 * Q], "float32")
+    SCRATCH["sf%d" % _t] = ("sbuf", [128, 4, 2, 24], "float32")
+    SCRATCH["su%d" % _t] = ("sbuf", [128, 192], "uint16")
+    SCRATCH["vv%d" % _t] = ("sbuf", [128, 144], "float32")
+for _t in range(3):
+    SCRATCH["land%d" % _t] = ("sbuf", [128, 768], "bfloat16")
+for _n in ("pl0", "pl1", "pk0", "pk1", "pa", "pm0", "pm1", "pc"):
+    SCRATCH[_n] = ("psum", [128, 512], "float32")
+SCRATCH.update({
+    "tb": ("sbuf", [128, GR], "bfloat16"), "db": ("sbuf", [128, GR], "bfloat16"), "fb": ("sbuf", [128, GR], "bfloat16"),
+    "cmp": ("sbuf", [128, (18 + max(NOFF)) * Q], "bfloat16"),
+    "le": ("sbuf", [128, 4 * Q], "bfloat16"), "lt": ("sbuf", [128, 5 * Q], "bfloat16"),
+    "k2": ("sbuf", [128, Q], "float32"), "kk": ("sbuf", [128, Q], "float32"), "bb": ("sbuf", [128, Q], "float32"), "rr": ("sbuf", [128, Q], "bfloat16"),
+    "a1": ("sbuf", [128, Q], "float32"), "a2": ("sbuf", [128, Q], "float32"),
+    "cst": ("sbuf", [128, Q], "bfloat16"),
+    "wc": ("sbuf", [128, CW], "bfloat16"), "gg": ("sbuf", [128, 768], "bfloat16"),
+    "sli": ("sbuf", [128, 2, 2, 4, 24], "int32"), "rfi": ("sbuf", [128, 2, 2, 24], "int32"),
+    "rn": ("sbuf", [128, 2, 2, 24], "float32"), "r2": ("sbuf", [128, 96], "float32"), "rt": ("sbuf", [128, 128], "float32"),
+    "pp": ("sbuf", [128, 10, 2, 2, 24], "bfloat16"),
+    "ph": ("sbuf", [128, 4, 2, 24], "bfloat16"), "pw": ("sbuf", [128, 4, 2, 24], "bfloat16"),
+    "dd": ("sbuf", [128, 144], "float32"), "mh": ("sbuf", [128, 144], "bfloat16"), "mn": ("sbuf", [128, 144], "bfloat16"),
+    "m8": ("sbuf", [128, 128], "bfloat16"), "n8": ("sbuf", [128, 128], "bfloat16"),
+    "m1": ("sbuf", [128, 128], "bfloat16"), "n1": ("sbuf", [128, 128], "bfloat16"),
+    "f1": ("sbuf", [128, 128], "float32"), "fh": ("sbuf", [128, 128], "float32"), "fn": ("sbuf", [128, 128], "float32"),
+    "sel": ("sbuf", [128, 7 * 144], "bfloat16"),
+    "a8": ("sbuf", [128, 8], "float32"), "b8": ("sbuf", [128, 8], "int32"), "c8": ("sbuf", [128, 8], "int32"),
+    "pi": ("sbuf", [128, 4], "int32"), "pj": ("sbuf", [128, 4], "int32"), "pf": ("sbuf", [128, 4], "float32"),
+    "v0": ("sbuf", [128, 144], "float32"),
+    "kb": ("sbuf", [128, 4, 2, 24], "float32"), "key": ("sbuf", [128, 4, 2, 24], "float32"),
+    "fall": ("sbuf", [128, 4, 2, 24], "float32"), "ok": ("sbuf", [128, 4, 2, 24], "float32"),
+    "rb": ("sbuf", [128, 4, 2, 24], "float32"), "rth": ("sbuf", [128, 4, 2, 24], "float32"),
+    "mx": ("sbuf", [128, 2, 2, 24], "float32"), "best": ("sbuf", [128, 2, 24], "float32"), "bi": ("sbuf", [128, 48], "int32"),
+    "ci": ("sbuf", [128, 48], "int32"), "hh": ("sbuf", [128, 144], "float32"), "eq": ("sbuf", [128, 144], "float32"),
+    "off": ("sbuf", [128, 48], "uint16"), "ti": ("sbuf", [128, 48], "int32"),
+})
+for _n in ("some", "fc", "ta", "tc", "veto", "take", "g1", "g2", "gb", "thr", "bv"):
+    SCRATCH[_n] = ("sbuf", [128, 48], "float32")
+for _n in ("cr", "ww"):
+    SCRATCH[_n] = ("sbuf", [128, 2, 24], "float32")
+SEMAPHORES = ["pe", "act", "dve", "pool", "sent"] + ["s%d" % _k for _k in range(140)]
+
+IO = {"th": [128, V], "dl": [128, V], "dr": [128, V], "sl": [128, 384], "rf": [128, 96],
+      "yt": [128, V], "yq": [128, V], "yr": [8, V]}
+AL = AluOpType
+AF = ActivationFunctionType
+S_ = np.s_
+_CACHE = {}
+
+
+def _where(n):
+    return SCRATCH[n][0] if n in SCRATCH else "dram"
+
+
+def _bytes(n):
+    return 2 if n in SCRATCH and SCRATCH[n][2] in ("bfloat16", "uint16") else (2 if n in ("th", "dl", "dr") else 4)
+
+
+def ref(name, idx=None):
+    shape = SCRATCH[name][1] if name in SCRATCH else IO[name]
+    if idx is None:
+        idx = S_[:]
+    key = (name, repr(idx))
+    if key not in _CACHE:
+        free = int(np.prod(shape[1:]))
+        tup = idx if isinstance(idx, tuple) else (idx,)
+        p = np.atleast_1d(np.arange(shape[0])[tup[0]])
+        c = np.arange(free).reshape(shape[1:])[tup[1:]]
+        c = np.atleast_1d(c)
+        _CACHE[key] = (int(p.min()), int(p.max()), int(c.min()), int(c.max()), int(c.size), int(p.size))
+    return {"n": name, "i": idx, "s": _CACHE[key], "ind": None}
+
+
+def cols(name, a, b, step=1):
+    return ref(name, S_[:, a:b] if step == 1 else S_[:, a:b:step])
+
+
+def gath(win, offs):
+    r = dict(win)
+    r["ind"] = offs
+    return r
+
+
+def build():
+    ops = []
+
+    def add(eng, kind, args, reads, writes, cost, lat=0.0, grp=None):
+        rd = []
+        for r in reads:
+            rd.append(r)
+            if r["ind"] is not None:
+                rd.append(r["ind"])
+        ops.append({"e": eng, "k": kind, "a": args, "r": rd, "w": list(writes), "c": cost, "lat": lat, "g": grp, "x": []})
+        return len(ops) - 1
+
+    def nel(out):
+        return out["s"][4]
+
+    def vcost(out, ins, two=False):
+        n = nel(out)
+        if any(r["ind"] is not None for r in ins):
+            return 55 + 1.3 * n
+        k = 2.0 if two and all(_where(r["n"]) == "sbuf" for r in ins) else 1.0
+        return 55 + 0.83 * k * max(n, 32)
+
+    def tt(out, a, b, op):
+        return add("dve", "tt", (out, a, b, op), [a, b], [out], vcost(out, [a, b], True))
+
+    def ts(out, a, s1, s2, op0, op1=None):
+        rd = [a] + [s for s in (s1, s2) if isinstance(s, dict)]
+        return add("dve", "ts", (out, a, s1, s2, op0, op1), rd, [out], vcost(out, [a]))
+
+    def cp(out, a):
+        return add("dve", "cp", (out, a), [a], [out], vcost(out, [a]))
+
+    def ms(out, val):
+        return add("dve", "ms", (out, val), [], [out], 55 + 0.42 * nel(out))
+
+    def act(out, a, bias=0.0, scale=1.0, func="Identity"):
+        return add("act", "act", (out, a, func, bias, scale), [a], [out], 15 + vcost(out, [a]))
+
+    def mm(out, lhs, rhs, start, stop):
+        k = 4 if _bytes(rhs["n"]) == 4 else 1
+        return add("pe", "mm", (out, lhs, rhs, start, stop), [lhs, rhs], [out], 10 + PE_NS * k * max(64, nel(rhs)))
+
+    def iota(out, pat, base, cm):
+        return add("g", "iota", (out, pat, base, cm), [], [out], 130 + 1.7 * nel(out))
+
+    def dma(q, out, a, grp, accum=False):
+        by = nel(out) * out["s"][5] * _bytes(out["n"])
+        rd = [a, out] if accum else [a]
+        return add(q, "dma", (out, a, accum), rd, [out], 900 if q == "g" else 80, 1900 + by / 300.0, grp)
+
+    def send(pairs, grp, own=None, after=()):
+        by = sum(nel(s) * 128 * _bytes(s["n"]) for s, d in pairs)
+        k = add("g", "send", (pairs, grp), [s for s, d in pairs] + list(after), [], 300, 1500 + by / P["NET"], own)
+        a = add("net", "arrive", (len(pairs),), [], [d for s, d in pairs], by / P["NET"], P["NETLAT"], grp)
+        ops[a]["x"].append(k)
+
+    dma("sync", cols("tb", 0, 1152), cols("th", 0, 1152), "ld0")
+    dma("act", cols("db", 0, 1152), cols("dl", 0, 1152), "ld0")
+    dma("sync", ref("sli"), ref("sl"), "ld1")
+    dma("sync", cols("tb", 1152, V), cols("th", 1152, V), "ld2")
+    dma("sync", cols("db", 1152, V), cols("dl", 1152, V), "ld2")
+    dma("sync", cols("fb", 0, V), ref("dr"), "ld3")
+    dma("sync", ref("rfi"), ref("rf"), "ld4")
+    iota(ref("dd"), [[-1, 144]], 0, 1)
+    iota(ref("a8"), [[-16, 8]], 0, 1)
+    iota(ref("pi"), [[0, 4]], 0, 1)
+    iota(ref("v0"), [[0, 3], [768, 2], [16, 24]], 0, 0)
+    for a in range(3):
+        send([(cols("tb", a * Q, a * Q + Q), cols("tb", RK + a * Q, RK + a * Q + Q)),
+              (cols("db", a * Q, a * Q + Q), cols("db", RK + a * Q, RK + a * Q + Q))], "in%d" % a)
+    for n, s in (("mh", 0.5), ("mn", -0.5)):
+        ts(cols(n, 0, 128), cols("dd", 0, 128), 0.0, s, AL.is_equal, AL.mult)
+        ts(cols(n, 128, 144), cols("dd", 128, 144), -128.0, s, AL.is_equal, AL.mult)
+    for n, s in (("f1", 1.0), ("m8", 8.0), ("n8", -8.0), ("m1", 1.0), ("n1", -1.0), ("fh", 0.5)) + ((("fn", -1.0),) if max(NOFF) else ()):
+        ts(ref(n), cols("dd", 0, 128), 0.0, s, AL.is_equal, AL.mult)
+    ms(ref("cst"), 1536.0)
+    ms(ref("sel"), 0.0)
+    ms(ref("wc"), 0.0)
+    ts(ref("b8"), ref("a8"), 0.5, -0.25, AL.mult, AL.add)
+    ts(ref("c8"), ref("a8"), 0.0625, -0.46875, AL.mult, AL.add)
+    for j in range(5):
+        ts(cols("sel", j * 144 + 15, j * 144 + 143, 16), ref("b8"), float(j), None, AL.is_equal)
+    for j, s in ((5, 16384.0), (6, -16384.0)):
+        ts(cols("sel", j * 144 + 15, j * 144 + 143, 16), ref("c8"), 0.0, s, AL.is_equal, AL.mult)
+    ts(ref("pj"), ref("pi"), 15, None, AL.bitwise_and)
+    cp(ref("pf"), ref("pj"))
+    for p in range(2):
+        ts(ref("vv%d" % p), ref("v0"), cols("pf", 0, 1), 384.0 * p, AL.add, AL.add)
+
+    def selv(j, i):
+        return cols("sel", j * 144 + 15 - i, j * 144 + 143 - i)
+
+    for p in range(2):
+        for h in range(2):
+            cp(ref("sf%d" % p, S_[:, :, h, :]), ref("sli", S_[:, h, p, :, :]))
+        cp(ref("su%d" % p), ref("sf%d" % p))
+    cp(ref("rn"), ref("rfi"))
+
+    def parts(p):
+        sf = "sf%d" % p
+        act(ref("ph"), ref(sf))
+        tt(ref("pw"), ref(sf), ref("ph"), AL.subtract)
+        for j in range(4):
+            act(ref("pp", S_[:, 2 * j, :, p, :]), ref("ph", S_[:, j]))
+            act(ref("pp", S_[:, 2 * j + 1, :, p, :]), ref("pw", S_[:, j]))
+        act(ref("pp", S_[:, 8, :, p, :]), ref("rn", S_[:, :, p, :]))
+        tt(ref("pp", S_[:, 9, :, p, :]), ref("rn", S_[:, :, p, :]), ref("pp", S_[:, 8, :, p, :]), AL.subtract)
+
+    def names(t):
+        send([(ref("pp", S_[:, 0:8]), ref("land%d" % t))], "nm%d" % t, "no%d" % t)
+        for k in range(10):
+            dma("sync", ref("wc", S_[k::16, 0:V]), ref("pp", S_[:, k]), "wa%d" % t)
+        dma("sync", ref("wc", S_[0:112, CG:CG + V]), ref("wc", S_[16:128, 0:V]), "wb%d" % t)
+        dma("sync", ref("wc", S_[112:128, CG:CG + V]), ref("wc", S_[0:16, 0:V]), "wb%d" % t)
+        for k in range(8):
+            dma("sync", ref("wc", S_[k::16, CR:CR + V]), cols("land%d" % t, 96 * k, 96 * k + 96), "wc%d" % t)
+
+    banks = ["pl0", "pl1", "pk0", "pk1", "pm0", "pm1", "pa"]
+    nb = [0]
+
+    def w0(dst, src, sh):
+        for nm, m2, f in (("wl0", "mn", cp), ("wh0", "mh", act)):
+            b = cols(banks[nb[0] % 7], 0, Q)
+            nb[0] += 1
+            mm(b, cols("mh", sh, sh + 128), cols("tb", src, src + Q), True, False)
+            mm(b, cols(m2, sh, sh + 128), cols("db", src, src + Q), False, True)
+            f(cols(nm, dst, dst + Q), b)
+
+    for a in range(3):
+        w0(a * Q, a * Q, 0)
+        w0(GR + a * Q, a * Q, 16)
+    w0(3 * Q, 3 * Q, 0)
+    for a in range(3):
+        w0(RK + a * Q, RK + a * Q, 0)
+    parts(0)
+    parts(1)
+    names(0)
+
+    send([(cols("fb", 0, 1152), cols("fb", RK, GR))], "in3", None, [cols("db", GR - Q, GR)])
+
+    def share(views, tag, far=True):
+        if far:
+            send([(cols(n, a * Q, a * Q + Q), cols(n, RK + a * Q, RK + a * Q + Q)) for n, a in views], "x" + tag)
+        for n, a in views:
+            dma("sync", ref(n, S_[0:112, GR + a * Q:GR + a * Q + Q]), ref(n, S_[16:128, a * Q:a * Q + Q]), "y" + tag)
+            dma("sync", ref(n, S_[112:128, GR + a * Q:GR + a * Q + Q]), ref(n, S_[0:16, a * Q:a * Q + Q]), "y" + tag)
+
+    def drift(t, a):
+        c0, c1 = a * Q, a * Q + Q
+        wide = 0.0 if t == 0 else 1.0 / 32
+        if t < 2:
+            for b0 in ((c0, RK + c0) if a < 3 else (c0,)):
+                for n, s in (("wl", -1.0), ("wh", 1.0)):
+                    act(cols("%s%d" % (n, t + 1), b0, b0 + Q), cols("fb", b0, b0 + Q), s * wide, 0.5)
+                    dma("g", cols("%s%d" % (n, t + 1), b0, b0 + Q), cols("%s%d" % (n, t), b0, b0 + Q), "d%d_%d" % (t, b0), True)
+            if a < 3:
+                share([("wl%d" % (t + 1), a), ("wh%d" % (t + 1), a)], "d%d%d" % (t, a), False)
+        else:
+            act(cols("wl3", c0, c1), cols("fb", c0, c1))
+            dma("g", cols("wl3", c0, c1), cols("wl2", c0, c1), "e%d" % a, True)
+            dma("g", cols("wl3", c0, c1), cols("wh2", c0, c1), "f%d" % a, True)
+            dma("sync", cols("yt", c0, c1), cols("wl3", c0, c1), "out")
+            if a < 3:
+                share([("wl3", a), ("wh3", a)], "d%d%d" % (t, a))
+
+    def poll(t, h):
+        p = t % 2
+        a = 2 * h + p
+        ck = 2 * t + h
+        lo, hi = "lo%d" % (ck % 2), "hi%d" % (ck % 2)
+        wl, wh = "wl%d" % t, "wh%d" % t
+        c0, c1 = a * Q, a * Q + Q
+        wide = 0.0 if t == 0 else 1.0 / 32
+
+        def L(j):
+            return cols(lo, j * Q, j * Q + Q)
+
+        def H(j):
+            return cols(hi, j * Q, j * Q + Q)
+
+        act(L(4), cols(wl, c0, c1), -wide)
+        act(H(4), cols(wh, c0, c1), wide)
+        ng = 0
+        for j in range(4):
+            o = cols("su%d" % p, j * 48 + h * 24, j * 48 + h * 24 + 24)
+            for dst, w, b in ((L(j), wl, -wide), (H(j), wh, wide)):
+                if ng % 2 == 0 and ng // 2 < DVE_G[ck]:
+                    ts(dst, gath(ref(w), o), b, None, AL.add)
+                else:
+                    act(dst, gath(ref(w), o), b)
+                ng += 1
+        terms = {i: [] for i in range(5)}
+        slot = [0, 0]
+        kk = ref("kk" if ck % 2 else "k2")
+        order = (4, 0, 1, 2, 3)
+        aside = (4, 0, 1, 2)[:NOFF[ck]]
+        for m, j in enumerate(aside):
+            c = cols("cmp", (18 + m) * Q, (19 + m) * Q)
+            pd = cols("pk1", 0, Q)
+            mm(pd, ref("f1"), L(3), True, False)
+            mm(pd, ref("fn"), H(j), False, True)
+            act(c, pd, -4096.0, 2.0 ** 30, "Sigmoid")
+            terms[3].append(("n8", c))
+        for n, i in enumerate(order):
+            pl = cols(("pl0", "pl1", "pk0", "pk1")[(5 * ck + n) % (3 if max(NOFF) else 4)] if ACC else "pl%d" % (n % 2), 0, Q)
+            if ACC:
+                mm(pl, ref("f1"), L(i), True, False)
+            else:
+                act(pl, L(i))
+            for j in range(5):
+                if j == i or (i == 3 and j in aside):
+                    continue
+                if j in order[n + 1:]:
+                    c = cols("cmp", slot[0] * Q, slot[0] * Q + Q)
+                    slot[0] += 1
+                    near = abs(i - j) <= 2
+                    if i < j:
+                        op, si = (AL.is_le, "m8") if near else (AL.is_gt, "n8")
+                    else:
+                        op, si = (AL.is_ge, "n8") if near else (AL.is_lt, "m8")
+                    tt(c, L(j), pl, op)
+                    terms[i].append((si, c))
+                    terms[j].append(("n8" if si == "m8" else "m8", c))
+                c = cols("cmp", (10 + slot[1] % 8) * Q, (11 + slot[1] % 8) * Q)
+                slot[1] += 1
+                tt(c, H(j), pl, AL.is_lt)
+                terms[i].append(("n8", c))
+            pk = pl if ACC else cols("pk%d" % (n % 2), 0, Q)
+            tl = ([("f1", L(i))] if BASE_PE[n] and not ACC else []) + terms[i]
+            for m, (w, c) in enumerate(tl):
+                mm(pk, ref(w), c, m == 0 and not ACC, m == len(tl) - 1)
+            if BASE_PE[n]:
+                if n == 0:
+                    act(kk, pk)
+            else:
+                tt(kk if n == 0 else pk, L(i), pk, AL.add)
+            if n > 0:
+                tt(kk, kk, pk, AL.max)
+        pa = cols("pa", 0, Q)
+        if A_PE[ck]:
+            act(ref("rr"), kk, 1536.0)
+            mm(pa, ref("m1"), ref("cst"), True, False)
+            mm(pa, ref("n1"), ref("rr"), False, False)
+            mm(pa, ref("f1"), kk, False, True)
+        else:
+            ts(pa, kk, 100663296.0, -100663296.0, AL.add, AL.add)
+            tt(pa, kk, pa, AL.subtract)
+        if t < 2:
+            act(cols("wl%d" % (t + 1), c0, c1), pa)
+            if a < 3:
+                share([("wl%d" % (t + 1), a)], "l%d%d" % (t, a))
+        else:
+            act(ref("a1"), pa)
+            act(ref("a2"), pa, -1.0 / 16)
+        for n, j in enumerate(order):
+            lt = cols("lt", j * Q, j * Q + Q)
+            tt(lt, H(j), pa, AL.is_lt)
+            pm = cols("pm%d" % (n % 2), 0, Q)
+            if MASK_PE[n]:
+                mm(pm, ref("f1"), H(j), True, False)
+                mm(pm, ref("m8"), lt, False, True)
+                if n == 0:
+                    act(ref("bb"), pm)
+            else:
+                act(pm, lt, -8.0, 16.0)
+                tt(ref("bb") if n == 0 else pm, H(j), pm, AL.max)
+            if n > 0:
+                dst = ref("bb") if n < 4 else (cols("wh%d" % (t + 1), c0, c1) if t < 2 else pm)
+                tt(dst, ref("bb"), pm, AL.min)
+        if t == 2:
+            tt(cols("wl3", c0, c1), ref("a1"), pm, AL.add)
+            tt(cols("wh3", c0, c1), pm, ref("a2"), AL.subtract)
+            share([("wl3", a)], "z%d" % a)
+            share([("wh3", a)], "w%d" % a)
+            dma("sync", cols("yt", c0, c1), cols("wl3", c0, c1), "out")
+        else:
+            if a < 3:
+                share([("wh%d" % (t + 1), a)], "h%d%d" % (t, a))
+            if t == 1:
+                tt(cols("wh3", c0, c1), cols("wh2", c0, c1), pa, AL.subtract)
+                act(cols("wh3", c0, c1), cols("wh3", c0, c1), 0.125)
+        for j in range(4):
+            tt(cols("le", j * Q, j * Q + Q), L(j), pa, AL.is_le)
+        pn = cols("pc", h * 96, h * 96 + 96)
+        for i in range(16):
+            mm(pn, selv(5, i), cols("le", i, 4 * Q, 16), i == 0, False)
+        for i in range(16):
+            mm(pn, selv(6, i), cols("lt", i, 4 * Q, 16), False, i == 15)
+        if h == 0:
+            for j in range(4):
+                act(ref("kb", S_[:, j]), ref("sf%d" % p, S_[:, j]), 4096.0 * (3 - j))
+        tt(ref("key", S_[:, :, h, :]), ref("kb", S_[:, :, h, :]), pn, AL.add)
+
+    def lookup(x, extra, rows):
+        ts(ref("ti"), x, 0.0625, -0.46875, AL.mult, AL.add)
+        ts(ref("ta"), ref("ti"), -1535.0 / 96, None, AL.mult)
+        if extra is not None:
+            tt(ref("tc"), x, extra, AL.add)
+            x = ref("tc")
+        tt(ref("ta"), ref("ta"), x, AL.add)
+        ts(ref("off"), ref("ta"), 96.0, 0.25, AL.mult, AL.add)
+        act(ref("gg"), gath(ref("wc"), ref("off")))
+        for n, j in enumerate(rows):
+            for i in range(16):
+                mm(cols("pc", 192 + n * 48, 240 + n * 48), selv(j, i), cols("gg", i, 768, 16), i == 0, i == 15)
+
+    def step(out, x, at, size, scalar):
+        if scalar:
+            act(out, x, 0.5 - at, 1.0, "Sign")
+            act(out, out, 0.0, size, "Relu")
+        else:
+            ts(out, x, at, size, AL.is_ge, AL.mult)
+
+    def control(t):
+        p = t % 2
+        sf = "sf%d" % p
+        nine = 9.0 * 16384
+        rp = ref("rn", S_[:, :, p, :])
+        tt(ref("mx"), ref("key", S_[:, 0:2]), ref("key", S_[:, 2:4]), AL.max)
+        tt(ref("best"), ref("mx", S_[:, 0]), ref("mx", S_[:, 1]), AL.max)
+        cp(ref("bi"), ref("best"))
+        ts(ref("ci"), ref("bi"), 4095, None, AL.bitwise_and)
+        c = cols("hh", 0, 48)
+        lookup(ref("ci"), None, [4])
+        cp(c, ref("ci"))
+        act(ref("fall"), ref("key"), nine - 0.5, -1.0, "Sign")
+        act(ref("fall"), ref("fall"), func="Relu")
+        step(ref("some"), ref("best"), nine, 1.0, True)
+        step(ref("fc"), c, 1536.0, 1536.0, True)
+        tt(ref("cr"), c, rp, AL.subtract)
+        tt(cols("hh", 48, 96), ref("fc"), cols("pc", 192, 240), AL.max)
+        lookup(cols("hh", 48, 96), None, [4])
+        step(ref("fc"), cols("hh", 48, 96), 1536.0, 1536.0, True)
+        tt(cols("hh", 96, 144), ref("fc"), cols("pc", 192, 240), AL.max)
+        tt(ref("eq"), ref("hh"), ref("vv%d" % p), AL.is_equal)
+        tt(ref("veto"), cols("eq", 0, 48), cols("eq", 48, 96), AL.max)
+        tt(ref("veto"), ref("veto"), cols("eq", 96, 144), AL.max)
+        tt(ref("veto"), ref("veto"), ref("some"), AL.mult)
+        tt(ref("take"), ref("some"), ref("veto"), AL.subtract)
+        tt(ref("cr"), ref("cr"), ref("take"), AL.mult)
+        tt(ref("ww"), ref("cr"), rp, AL.add)
+        step(ref("g1"), ref("ww"), 1536.0, 24.0, t < 2)
+        step(ref("g2"), ref("ww"), 2688.0, 18.0, t < 2)
+        tt(ref("gb"), ref("g1"), ref("g2"), AL.add)
+        lookup(ref("ww"), ref("gb"), [0, 1, 2, 3])
+        act(rp, ref("ww"))
+        ts(ref("thr"), ref("gb"), 24.0, -1152.0, AL.is_equal, AL.mult)
+        tt(ref("bv"), ref("best"), ref("veto"), AL.mult)
+        for j in range(4):
+            act(cols("pc", 48 * j, 48 * j + 48), ref("bv"))
+            act(ref("rb", S_[:, j]), ref("gb"), 0.0, 64.0)
+            act(ref("rth", S_[:, j]), ref("thr"), 3840.0)
+        u, nw = cols("pc", 0, 192), cols("pc", 192, 384)
+        tt(u, ref("key"), u, AL.is_equal)
+        tt(ref("fall"), ref("fall"), u, AL.max)
+        tt(nw, ref("rb"), nw, AL.add)
+        tt(u, nw, ref("rth"), AL.is_lt)
+        tt(ref("ok"), u, ref("fall"), AL.mult)
+        tt(nw, nw, ref(sf), AL.subtract)
+        tt(nw, nw, ref("ok"), AL.mult)
+        tt(ref(sf), ref(sf), nw, AL.add)
+        cp(ref("su%d" % p), ref(sf))
+        if t < 2:
+            parts(p)
+            names(t + 1)
+
+    def last(a, n):
+        h, p = a // 2, a % 2
+        c0, c1 = a * Q, a * Q + Q
+        lo, hi = "lo%d" % (n % 2), "hi%d" % (n % 2)
+        ps = cols("pm%d" % (n % 2), 0, Q)
+        mm(ps, ref("fh"), cols("wh3", c0, c1), True, False)
+        sb = ("pl0", "pl1", "pk0", "pk1")
+        own = ref(("k2", "kk", "bb", "a1")[n])
+        dma("sync", own, cols("wl3", c0, c1), "o%d" % n)
+        for j in range(4):
+            o = cols("su%d" % p, j * 48 + h * 24, j * 48 + h * 24 + 24)
+            z, d = cols(lo, j * Q, j * Q + Q), cols(hi, j * Q, j * Q + Q)
+            tt(z, gath(ref("wl3"), o), own, AL.subtract)
+            if j < XA:
+                act(d, gath(ref("wh3"), o))
+                act(cols(sb[j], 0, Q), z, func="Sigmoid")
+                tt(d, d, cols(sb[j], 0, Q), AL.mult)
+            else:
+                act(z, z, func="Sigmoid")
+                tt(d, gath(ref("wh3"), o), z, AL.mult)
+            mm(ps, ref("f1"), d, False, j == 3)
+        y = cols(lo, 4 * Q, 5 * Q)
+        act(y, ps)
+        dma("sync", cols("yq", c0, c1), y, "q%d" % n)
+
+    for t in range(3):
+        for h in range(2):
+            drift(t, 2 * h + 1 - t % 2)
+        poll(t, 0)
+        poll(t, 1)
+        control(t)
+    act(ref("r2"), ref("rn"))
+    mm(ref("pc", S_[0:96, 0:128]), ref("r2"), ref("f1"), True, True)
+    act(ref("rt", S_[0:96, :]), ref("pc", S_[0:96, 0:128]))
+    for k in range(8):
+        dma("sync", ref("yr", S_[k, :]), ref("rt", S_[0:96, 16 * k:16 * k + 16]), "out")
+    for n, a in enumerate((1, 3, 0, 2)):
+        last(a, n)
+    return ops
+
+
+def _meet(a, b):
+    return a[0] <= b[1] and b[0] <= a[1] and a[2] <= b[3] and b[2] <= a[3]
+
+
+def plan():
+    if "plan" in _CACHE:
+        return _CACHE["plan"]
+    ops = build()
+    hist = {}
+    groups = {}
+    for k, o in enumerate(ops):
+        dep = set()
+        for views, wr in ((o["r"], False), (o["w"], True)):
+            for r in views:
+                bank = _where(r["n"]) == "psum"
+                for (m, s, w2) in hist.get(r["n"], []):
+                    if m == k:
+                        continue
+                    if bank and (ops[m]["e"] != o["e"] or o["e"] == "pe"):
+                        dep.add(m)
+                    elif (wr or w2) and _meet(s, r["s"]) and not (o["g"] is not None and ops[m]["g"] == o["g"]):
+                        dep.add(m)
+        for views, wr in ((o["r"], False), (o["w"], True)):
+            for r in views:
+                h = hist.setdefault(r["n"], [])
+                s = r["s"]
+                if _where(r["n"]) == "psum":
+                    if o["e"] == "pe":
+                        h[:] = []
+
+                elif wr and s[5] == s[1] - s[0] + 1 and s[4] == s[3] - s[2] + 1:
+                    h[:] = [e for e in h if e[0] == k or not (s[0] <= e[1][0] and e[1][1] <= s[1] and s[2] <= e[1][2] and e[1][3] <= s[3])]
+                h.append((k, s, wr))
+        o["d"] = dep
+        if o["g"] is not None:
+            groups.setdefault(o["g"], []).append(k)
+    for k, o in enumerate(ops):
+        full = set()
+        for m in o["d"]:
+            if ops[m]["g"] is not None:
+                full.update(groups[ops[m]["g"]])
+            else:
+                full.add(m)
+        o["d"] = sorted(full)
+        o["all"] = sorted(full | set(o["x"]))
+    n = len(ops)
+    succ = [[] for _ in range(n)]
+    for k, o in enumerate(ops):
+        for m in o["all"]:
+            succ[m].append(k)
+    indeg = [len(o["all"]) for o in ops]
+    topo = [k for k in range(n) if indeg[k] == 0]
+    left = list(indeg)
+    for k in topo:
+        for s in succ[k]:
+            left[s] -= 1
+            if left[s] == 0:
+                topo.append(s)
+    assert len(topo) == n
+    pr = [0.0] * n
+    for k in reversed(topo):
+        pr[k] = ops[k]["c"] + ops[k]["lat"] + max([pr[s] + 80 for s in succ[k]] + [0.0])
+    if P["SEED"]:
+        pr = list(np.array(pr) + P["AMP"] * np.random.default_rng(P["SEED"]).random(n))
+    free = {}
+    ready = {}
+    at = [0.0] * n
+    fin = [0.0] * n
+    start = [0.0] * n
+    left = list(indeg)
+    for k in range(n):
+        if left[k] == 0:
+            ready.setdefault(ops[k]["e"], []).append(k)
+    seq = []
+    while len(seq) < n:
+        best = None
+        for e, lst in ready.items():
+            if not lst:
+                continue
+            t0 = max(free.get(e, 0.0), min(at[k] for k in lst))
+            k = max((k for k in lst if at[k] <= t0 + 30), key=lambda k: (pr[k], -k))
+            if best is None or t0 < best[0]:
+                best = (t0, e, k)
+        t0, e, k = best
+        ready[e].remove(k)
+        o = ops[k]
+        start[k] = max(t0, at[k])
+        free[e] = start[k] + o["c"]
+        fin[k] = free[e] + o["lat"]
+        seq.append(k)
+        for s in succ[k]:
+            same = ops[s]["e"] == e == "pe"
+            early = o["k"] == "send" and k in ops[s]["x"]
+            at[s] = max(at[s], (free[e] if early else fin[k]) + (0 if same else 80))
+            left[s] -= 1
+            if left[s] == 0:
+                ready.setdefault(ops[s]["e"], []).append(s)
+    _CACHE["plan"] = (ops, seq, groups, start, fin)
+    return _CACHE["plan"]
+
+
+def rank_program(g, core, T, topo):
+    rank = T.rank_of(core)
+    if rank is None:
+        return
+    n = len(T.cores)
+    prev, nxt = T.cores[(rank - 1) % n], T.cores[(rank + 1) % n]
+    rid, pid = topo.addr(prev)[0:2]
+    eng = topo.engines(core, prev)
+    got = len(topo.engines(nxt, core))
+    ops, seq, groups, start, fin = plan()
+    queue = {"g": g, "pe": g.tensor, "act": g.scalar, "dve": g.vector, "sync": g.sync}
+    gsem = {name: "s%d" % k for k, name in enumerate(sorted(groups))}
+    total = {}
+    for name, ks in groups.items():
+        kind = ops[ks[0]]["k"]
+        total[gsem[name]] = 16 * len(ks) if kind == "dma" else (got if kind == "arrive" else len(eng))
+    count = {}
+    mark = {}
+    clock = {}
+    known = {e: {} for e in queue}
+
+    def ap(r):
+        a = T[r["n"]][r["i"]]
+        if r["ind"] is not None:
+            w = T[r["n"]]
+            a = w[:, 0:w.shape[1]].indirect(ap(r["ind"]))
+        return a
+
+    def val(s):
+        return ap(s) if isinstance(s, dict) else s
+
+    for k in seq:
+        o = ops[k]
+        e, kind, a = o["e"], o["k"], o["a"]
+        if kind == "arrive":
+            mark[k] = (gsem[o["g"]], got)
+            clock[k] = {}
+            continue
+        q = queue[e]
+        need = {}
+        for m in o["d"]:
+            if e == "pe" and ops[m]["e"] == "pe":
+                continue
+            s, v = mark[m]
+            if known[e].get(s, 0) < v:
+                need[s] = max(need.get(s, 0), v)
+        for m in o["d"]:
+            if mark[m][0] in need and mark[m][1] <= need[mark[m][0]]:
+                for s, v in clock[m].items():
+                    if s in need and need[s] <= v and s != mark[m][0]:
+                        need[s] = 0
+        for s in sorted(need):
+            if need[s]:
+                q.wait_ge(T.sem[s], need[s])
+        for m in o["d"]:
+            if e == "pe" and ops[m]["e"] == "pe":
+                continue
+            for s, v in list(clock[m].items()) + [mark[m]]:
+                if known[e].get(s, 0) < v:
+                    known[e][s] = v
+        clock[k] = dict(known[e])
+        if kind == "dma":
+            if a[2]:
+                ins = q.dma_start(ap(a[0]), ap(a[1]), accum_op=AL.add)
+            else:
+                ins = q.dma_start(ap(a[0]), ap(a[1]))
+            ins.then_inc(T.sem[gsem[o["g"]]], 16)
+            mark[k] = (gsem[o["g"]], total[gsem[o["g"]]])
+            continue
+        if kind == "send":
+            pairs, grp = a
+            loc = gsem[o["g"]] if o["g"] is not None else "sent"
+            per = len(eng) // len(pairs)
+            masks = [sum(1 << x for x in eng[m * per:(m + 1) * per]) for m in range(len(pairs))]
+            if len(pairs) == 1:
+                g.remote_dma(ap(pairs[0][1]), ap(pairs[0][0]), T.sem[gsem[grp]], T.sem[loc], pid, rid, masks[0])
+            else:
+                g.remote_dma_fused([RemoteDMATransfer(dst_ids=[DstId(rid=rid, pnc=pid)], dma_engine_mask=masks[m],
+                                                      remote_sem=T.sem[gsem[grp]], src=ap(s), dst=ap(d))
+                                    for m, (s, d) in enumerate(pairs)], local_sem=T.sem[loc])
+            if loc == "sent":
+                total["sent"] = total.get("sent", 0) + len(eng)
+            mark[k] = (loc, len(eng))
+            continue
+        if kind == "tt":
+            ins = q.tensor_tensor(ap(a[0]), ap(a[1]), ap(a[2]), a[3])
+        elif kind == "ts":
+            if a[5] is None:
+                ins = q.tensor_scalar(ap(a[0]), ap(a[1]), val(a[2]), None, a[4])
+            else:
+                ins = q.tensor_scalar(ap(a[0]), ap(a[1]), val(a[2]), val(a[3]), a[4], a[5])
+        elif kind == "cp":
+            ins = q.tensor_copy(ap(a[0]), ap(a[1]))
+        elif kind == "ms":
+            ins = q.memset(ap(a[0]), a[1])
+        elif kind == "act":
+            f = {"Sigmoid": AF.Sigmoid, "Identity": AF.Identity, "Sign": AF.Sign, "Relu": AF.Relu}[a[2]]
+            ins = q.activation(ap(a[0]), ap(a[1]), f, bias=a[3], scale=a[4])
+        elif kind == "mm":
+            ins = q.matmul(ap(a[0]), ap(a[1]), ap(a[2]), a[3], a[4])
+        else:
+            if SCRATCH[a[0]["n"]][2] == "int32":
+                ins = q.iota(ap(a[0]), a[1], a[2], a[3])
+            else:
+                ins = q.iota(ap(a[0]), a[1], a[2], a[3], allow_small_or_imprecise_dtypes=True)
+        s = "pool" if e == "g" else e
+        count[s] = count.get(s, 0) + 1
+        ins.then_inc(T.sem[s], 1)
+        mark[k] = (s, count[s])
+    total.update(count)
+    for s in sorted(total):
+        g.wait_ge(T.sem[s], total[s])

@@ -11,13 +11,15 @@ CR, CG, CW = 2400, 4200, 5744
 
 BASE_PE = (1, 1, 1, 1, 1)
 MASK_PE = (1, 1, 1, 1, 1)
-A_PE = (1, 0, 1, 0, 1, 0)
+A_PE = (2, 2, 2, 2, 2, 2)
 DVE_G = (2, 0, 0, 0, 0, 0)
 XA = 3
 ACC = False
 NOFF = (0, 0, 0, 0, 0, 0)
-PE_NS = 0.47
-P = {"NET": 70.0, "NETLAT": 2600, "SEED": 14, "AMP": 700.0}
+SC = (0, 1, 0)
+VIA = ("in1", "in3", "nm0", "nm1", "nm2", "xd21", "xw0", "xw2")
+PE_NS = 0.45
+P = {"NET": 62.0, "NETLAT": 2200, "SEED": 5, "ITER": 45, "OVH": 35.0}
 
 SCRATCH = {}
 for _t in range(4):
@@ -49,6 +51,7 @@ SCRATCH.update({
     "m8": ("sbuf", [128, 128], "bfloat16"), "n8": ("sbuf", [128, 128], "bfloat16"),
     "m1": ("sbuf", [128, 128], "bfloat16"), "n1": ("sbuf", [128, 128], "bfloat16"),
     "f1": ("sbuf", [128, 128], "float32"), "fh": ("sbuf", [128, 128], "float32"), "fn": ("sbuf", [128, 128], "float32"),
+    "f96": ("sbuf", [128, 128], "float32"), "fm": ("sbuf", [128, 128], "float32"),
     "sel": ("sbuf", [128, 7 * 144], "bfloat16"),
     "a8": ("sbuf", [128, 8], "float32"), "b8": ("sbuf", [128, 8], "int32"), "c8": ("sbuf", [128, 8], "int32"),
     "pi": ("sbuf", [128, 4], "int32"), "pj": ("sbuf", [128, 4], "int32"), "pf": ("sbuf", [128, 4], "float32"),
@@ -57,13 +60,12 @@ SCRATCH.update({
     "fall": ("sbuf", [128, 4, 2, 24], "float32"), "ok": ("sbuf", [128, 4, 2, 24], "float32"),
     "rb": ("sbuf", [128, 4, 2, 24], "float32"), "rth": ("sbuf", [128, 4, 2, 24], "float32"),
     "mx": ("sbuf", [128, 2, 2, 24], "float32"), "best": ("sbuf", [128, 2, 24], "float32"), "bi": ("sbuf", [128, 48], "int32"),
-    "ci": ("sbuf", [128, 48], "int32"), "hh": ("sbuf", [128, 144], "float32"), "eq": ("sbuf", [128, 144], "float32"),
+    "ci": ("sbuf", [128, 48], "int32"), "hh": ("sbuf", [128, 144], "float32"), "eq": ("sbuf", [128, 144], "bfloat16"),
     "off": ("sbuf", [128, 48], "uint16"), "ti": ("sbuf", [128, 48], "int32"),
 })
-for _n in ("some", "fc", "ta", "tc", "veto", "take", "g1", "g2", "gb", "thr", "bv"):
+for _n in ("fc", "ta", "tc", "veto", "take", "g1", "g2", "gb", "thr", "bv", "cr", "ww"):
     SCRATCH[_n] = ("sbuf", [128, 48], "float32")
-for _n in ("cr", "ww"):
-    SCRATCH[_n] = ("sbuf", [128, 2, 24], "float32")
+SCRATCH["some"] = ("sbuf", [128, 48], "bfloat16")
 SEMAPHORES = ["pe", "act", "dve", "pool", "sent"] + ["s%d" % _k for _k in range(140)]
 
 IO = {"th": [128, V], "dl": [128, V], "dr": [128, V], "sl": [128, 384], "rf": [128, 96],
@@ -125,9 +127,9 @@ def build():
     def vcost(out, ins, two=False):
         n = nel(out)
         if any(r["ind"] is not None for r in ins):
-            return 55 + 1.3 * n
+            return P["OVH"] + 1.3 * n
         k = 2.0 if two and all(_where(r["n"]) == "sbuf" for r in ins) else 1.0
-        return 55 + 0.83 * k * max(n, 32)
+        return P["OVH"] + 0.83 * k * max(n, 48)
 
     def tt(out, a, b, op):
         return add("dve", "tt", (out, a, b, op), [a, b], [out], vcost(out, [a, b], True))
@@ -160,11 +162,15 @@ def build():
     def send(pairs, grp, own=None, after=()):
         by = sum(nel(s) * 128 * _bytes(s["n"]) for s, d in pairs)
         k = add("g", "send", (pairs, grp), [s for s, d in pairs] + list(after), [], 300, 1500 + by / P["NET"], own)
-        a = add("net", "arrive", (len(pairs),), [], [d for s, d in pairs], by / P["NET"], P["NETLAT"], grp)
+        by2 = grp in VIA
+        a = add("net2" if by2 else "net", "arrive", (len(pairs),), [], [d for s, d in pairs], by / P["NET"],
+                P["NETLAT"] + (3200 if by2 else 0), grp)
         ops[a]["x"].append(k)
 
-    dma("sync", cols("tb", 0, 1152), cols("th", 0, 1152), "ld0")
-    dma("act", cols("db", 0, 1152), cols("dl", 0, 1152), "ld0")
+    dma("sync", cols("tb", 0, Q), cols("th", 0, Q), "ld0")
+    dma("act", cols("db", 0, Q), cols("dl", 0, Q), "ld0")
+    dma("sync", cols("tb", Q, 1152), cols("th", Q, 1152), "ld5")
+    dma("act", cols("db", Q, 1152), cols("dl", Q, 1152), "ld5")
     dma("sync", ref("sli"), ref("sl"), "ld1")
     dma("sync", cols("tb", 1152, V), cols("th", 1152, V), "ld2")
     dma("sync", cols("db", 1152, V), cols("dl", 1152, V), "ld2")
@@ -180,11 +186,16 @@ def build():
     for n, s in (("mh", 0.5), ("mn", -0.5)):
         ts(cols(n, 0, 128), cols("dd", 0, 128), 0.0, s, AL.is_equal, AL.mult)
         ts(cols(n, 128, 144), cols("dd", 128, 144), -128.0, s, AL.is_equal, AL.mult)
-    for n, s in (("f1", 1.0), ("m8", 8.0), ("n8", -8.0), ("m1", 1.0), ("n1", -1.0), ("fh", 0.5)) + ((("fn", -1.0),) if max(NOFF) else ()):
-        ts(ref(n), cols("dd", 0, 128), 0.0, s, AL.is_equal, AL.mult)
-    ms(ref("cst"), 1536.0)
+    ts(ref("f1"), cols("dd", 0, 128), 0.0, None, AL.is_equal)
+    for n, s in (("m8", 8.0), ("n8", -8.0), ("m1", 1.0), ("fh", 0.5), ("f96", 96.0), ("fm", -1535.0 / 16)) + ((("fn", -1.0),) if max(NOFF) else ()):
+        act(ref(n), ref("f1"), 0.0, s)
+    if 1 in A_PE:
+        act(ref("n1"), ref("f1"), 0.0, -1.0)
+        ms(ref("cst"), 1536.0)
     ms(ref("sel"), 0.0)
-    ms(ref("wc"), 0.0)
+    ms(cols("wc", 0, CW // 8), 0.0)
+    for k in range(1, 8):
+        dma("sync", cols("wc", k * CW // 8, (k + 1) * CW // 8), cols("wc", 0, CW // 8), "zero")
     ts(ref("b8"), ref("a8"), 0.5, -0.25, AL.mult, AL.add)
     ts(ref("c8"), ref("a8"), 0.0625, -0.46875, AL.mult, AL.add)
     for j in range(5):
@@ -346,7 +357,11 @@ def build():
             if n > 0:
                 tt(kk, kk, pk, AL.max)
         pa = cols("pa", 0, Q)
-        if A_PE[ck]:
+        if A_PE[ck] == 2:
+            act(ref("rr"), kk, 1536.0)
+            act(pa, ref("rr"), -1536.0)
+            tt(pa, kk, pa, AL.subtract)
+        elif A_PE[ck]:
             act(ref("rr"), kk, 1536.0)
             mm(pa, ref("m1"), ref("cst"), True, False)
             mm(pa, ref("n1"), ref("rr"), False, False)
@@ -400,14 +415,29 @@ def build():
                 act(ref("kb", S_[:, j]), ref("sf%d" % p, S_[:, j]), 4096.0 * (3 - j))
         tt(ref("key", S_[:, :, h, :]), ref("kb", S_[:, :, h, :]), pn, AL.add)
 
-    def lookup(x, extra, rows):
-        ts(ref("ti"), x, 0.0625, -0.46875, AL.mult, AL.add)
-        ts(ref("ta"), ref("ti"), -1535.0 / 96, None, AL.mult)
-        if extra is not None:
-            tt(ref("tc"), x, extra, AL.add)
-            x = ref("tc")
-        tt(ref("ta"), ref("ta"), x, AL.add)
-        ts(ref("off"), ref("ta"), 96.0, 0.25, AL.mult, AL.add)
+    def down(out, x, unit):
+        big = 1.5 * 2.0 ** 23 * unit
+        act(out, x, 0.5 - unit / 2)
+        act(out, out, big)
+        act(out, out, -big)
+
+    def lookup(x, extra, rows, scalar):
+        if scalar:
+            down(ref("ta"), x, 16.0)
+            po = cols("pc", 384, 432)
+            mm(po, ref("f96"), x, True, False)
+            if extra is not None:
+                mm(po, ref("f96"), extra, False, False)
+            mm(po, ref("fm"), ref("ta"), False, True)
+            ts(ref("off"), po, 0.25, None, AL.add)
+        else:
+            ts(ref("ti"), x, 0.0625, -0.46875, AL.mult, AL.add)
+            ts(ref("ta"), ref("ti"), -1535.0 / 96, None, AL.mult)
+            if extra is not None:
+                tt(ref("tc"), x, extra, AL.add)
+                x = ref("tc")
+            tt(ref("ta"), ref("ta"), x, AL.add)
+            ts(ref("off"), ref("ta"), 96.0, 0.25, AL.mult, AL.add)
         act(ref("gg"), gath(ref("wc"), ref("off")))
         for n, j in enumerate(rows):
             for i in range(16):
@@ -427,38 +457,48 @@ def build():
         rp = ref("rn", S_[:, :, p, :])
         tt(ref("mx"), ref("key", S_[:, 0:2]), ref("key", S_[:, 2:4]), AL.max)
         tt(ref("best"), ref("mx", S_[:, 0]), ref("mx", S_[:, 1]), AL.max)
-        cp(ref("bi"), ref("best"))
-        ts(ref("ci"), ref("bi"), 4095, None, AL.bitwise_and)
         c = cols("hh", 0, 48)
-        lookup(ref("ci"), None, [4])
-        cp(c, ref("ci"))
+        sc = SC[t]
+        if sc:
+            down(ref("tc"), ref("best"), 4096.0)
+            tt(c, ref("best"), ref("tc"), AL.subtract)
+            lookup(c, None, [4], sc)
+        else:
+            cp(ref("bi"), ref("best"))
+            ts(ref("ci"), ref("bi"), 4095, None, AL.bitwise_and)
+            lookup(ref("ci"), None, [4], sc)
+            cp(c, ref("ci"))
         act(ref("fall"), ref("key"), nine - 0.5, -1.0, "Sign")
         act(ref("fall"), ref("fall"), func="Relu")
-        step(ref("some"), ref("best"), nine, 1.0, True)
+        step(ref("some"), ref("best"), nine, 4.0, True)
         step(ref("fc"), c, 1536.0, 1536.0, True)
         tt(ref("cr"), c, rp, AL.subtract)
         tt(cols("hh", 48, 96), ref("fc"), cols("pc", 192, 240), AL.max)
-        lookup(cols("hh", 48, 96), None, [4])
+        lookup(cols("hh", 48, 96), None, [4], sc)
         step(ref("fc"), cols("hh", 48, 96), 1536.0, 1536.0, True)
         tt(cols("hh", 96, 144), ref("fc"), cols("pc", 192, 240), AL.max)
         tt(ref("eq"), ref("hh"), ref("vv%d" % p), AL.is_equal)
-        tt(ref("veto"), cols("eq", 0, 48), cols("eq", 48, 96), AL.max)
-        tt(ref("veto"), ref("veto"), cols("eq", 96, 144), AL.max)
-        tt(ref("veto"), ref("veto"), ref("some"), AL.mult)
-        tt(ref("take"), ref("some"), ref("veto"), AL.subtract)
+        pv = cols("pc", 432, 480)
+        mm(pv, ref("m1"), ref("some"), True, False)
+        for m in range(3):
+            mm(pv, ref("m1"), cols("eq", 48 * m, 48 * m + 48), False, m == 2)
+        act(ref("take"), pv, -4.0, 1.0, "Abs")
+        act(ref("take"), ref("take"), 1.0, -1.0, "Relu")
+        step(ref("veto"), pv, 5.0, 1.0, True)
         tt(ref("cr"), ref("cr"), ref("take"), AL.mult)
         tt(ref("ww"), ref("cr"), rp, AL.add)
         step(ref("g1"), ref("ww"), 1536.0, 24.0, t < 2)
         step(ref("g2"), ref("ww"), 2688.0, 18.0, t < 2)
         tt(ref("gb"), ref("g1"), ref("g2"), AL.add)
-        lookup(ref("ww"), ref("gb"), [0, 1, 2, 3])
+        lookup(ref("ww"), ref("gb"), [0, 1, 2, 3], sc)
         act(rp, ref("ww"))
-        ts(ref("thr"), ref("gb"), 24.0, -1152.0, AL.is_equal, AL.mult)
+        act(ref("thr"), ref("gb"), -24.0, 1.0, "Abs")
+        act(ref("thr"), ref("thr"), 1152.0, -1152.0, "Relu")
         tt(ref("bv"), ref("best"), ref("veto"), AL.mult)
         for j in range(4):
             act(cols("pc", 48 * j, 48 * j + 48), ref("bv"))
             act(ref("rb", S_[:, j]), ref("gb"), 0.0, 64.0)
-            act(ref("rth", S_[:, j]), ref("thr"), 3840.0)
+            act(ref("rth", S_[:, j]), ref("thr"), 3840.0, -1.0)
         u, nw = cols("pc", 0, 192), cols("pc", 192, 384)
         tt(u, ref("key"), u, AL.is_equal)
         tt(ref("fall"), ref("fall"), u, AL.max)
@@ -493,9 +533,13 @@ def build():
             else:
                 act(z, z, func="Sigmoid")
                 tt(d, gath(ref("wh3"), o), z, AL.mult)
-            mm(ps, ref("f1"), d, False, j == 3)
+            if j < 3 or n < 3:
+                mm(ps, ref("f1"), d, False, j == (3 if n < 3 else 2))
         y = cols(lo, 4 * Q, 5 * Q)
-        act(y, ps)
+        if n < 3:
+            act(y, ps)
+        else:
+            tt(y, d, ps, AL.add)
         dma("sync", cols("yq", c0, c1), y, "q%d" % n)
 
     for t in range(3):
@@ -576,57 +620,134 @@ def plan():
     pr = [0.0] * n
     for k in reversed(topo):
         pr[k] = ops[k]["c"] + ops[k]["lat"] + max([pr[s] + 80 for s in succ[k]] + [0.0])
-    if P["SEED"]:
-        pr = list(np.array(pr) + P["AMP"] * np.random.default_rng(P["SEED"]).random(n))
-    free = {}
-    ready = {}
-    at = [0.0] * n
-    fin = [0.0] * n
-    start = [0.0] * n
-    left = list(indeg)
-    for k in range(n):
-        if left[k] == 0:
-            ready.setdefault(ops[k]["e"], []).append(k)
-    seq = []
-    while len(seq) < n:
-        best = None
-        for e, lst in ready.items():
-            if not lst:
-                continue
-            t0 = max(free.get(e, 0.0), min(at[k] for k in lst))
-            k = max((k for k in lst if at[k] <= t0 + 30), key=lambda k: (pr[k], -k))
-            if best is None or t0 < best[0]:
-                best = (t0, e, k)
-        t0, e, k = best
-        ready[e].remove(k)
-        o = ops[k]
-        start[k] = max(t0, at[k])
-        free[e] = start[k] + o["c"]
-        fin[k] = free[e] + o["lat"]
-        seq.append(k)
-        for s in succ[k]:
-            same = ops[s]["e"] == e == "pe"
-            early = o["k"] == "send" and k in ops[s]["x"]
-            at[s] = max(at[s], (free[e] if early else fin[k]) + (0 if same else 80))
-            left[s] -= 1
-            if left[s] == 0:
-                ready.setdefault(ops[s]["e"], []).append(s)
+    eng = [o["e"] for o in ops]
+    cost = [o["c"] for o in ops]
+
+    def lag(m, s):
+        early = ops[m]["k"] == "send" and m in ops[s]["x"]
+        return (0.0 if early else ops[m]["lat"]) + (0.0 if eng[m] == eng[s] == "pe" else 80.0)
+
+    fw = [[(s, lag(k, s)) for s in succ[k]] for k in range(n)]
+    bw = [[(m, lag(m, k)) for m in ops[k]["all"]] for k in range(n)]
+
+    def sched(pr, nxt, first, look):
+        free, ready = {}, {}
+        at = list(first)
+        start = [0.0] * n
+        left = [0] * n
+        for k in range(n):
+            for s, d in nxt[k]:
+                left[s] += 1
+        for k in range(n):
+            if left[k] == 0:
+                ready.setdefault(eng[k], []).append(k)
+        seq = []
+        while len(seq) < n:
+            best = None
+            for e, lst in ready.items():
+                if lst:
+                    t0 = max(free.get(e, 0.0), min([at[k] for k in lst]))
+                    if best is None or t0 < best[0]:
+                        best = (t0, e)
+            t0, e = best
+            k = max([k for k in ready[e] if at[k] <= t0 + look], key=lambda k: pr[k])
+            ready[e].remove(k)
+            start[k] = max(t0, at[k])
+            free[e] = start[k] + cost[k]
+            seq.append(k)
+            for s, d in nxt[k]:
+                if free[e] + d > at[s]:
+                    at[s] = free[e] + d
+                left[s] -= 1
+                if left[s] == 0:
+                    ready.setdefault(eng[s], []).append(s)
+        return seq, start
+
+    alts = []
+    for gat, net, pe in ((1.0, 1.0, 0.94), (1.3, 1.0, 1.0), (0.75, 0.6, 1.0), (1.0, 1.5, 0.94), (1.0, 0.7, 1.07)):
+        c = list(cost)
+        for k, o in enumerate(ops):
+            if o["k"] == "arrive":
+                c[k] *= net
+            elif o["k"] == "mm":
+                c[k] *= pe
+            elif any(r["ind"] is not None for r in o["r"]):
+                c[k] *= gat
+        alts.append(c)
+
+    def score(seq):
+        tot = 0.0
+        for c in alts:
+            free, end = {}, [0.0] * n
+            for k in seq:
+                t0 = free.get(eng[k], 0.0)
+                for m, d in bw[k]:
+                    if end[m] + d > t0:
+                        t0 = end[m] + d
+                free[eng[k]] = end[k] = t0 + c[k]
+            tot += max(end)
+        return tot / len(alts)
+
+    rng = np.random.default_rng(P["SEED"])
+    zero = [0.0] * n
+    tail = [o["lat"] for o in ops]
+    seq, start = sched(pr, fw, zero, 30)
+    best = (score(seq), seq, start)
+    cur = best
+    for it in range(P["ITER"]):
+        amp = (50.0, 300.0, 1000.0)[it % 3]
+        look = (30, 150, 300)[(it // 3) % 3]
+        back = [cur[2][k] + cost[k] + x for k, x in enumerate(amp * rng.random(n))]
+        s2, st2 = sched(back, bw, tail, look)
+        fore = [st2[k] + cost[k] + x for k, x in enumerate(amp * rng.random(n))]
+        seq, start = sched(fore, fw, zero, look)
+        sc = score(seq)
+        if sc < cur[0] + 400.0:
+            cur = (sc, seq, start)
+        if sc < best[0]:
+            best = cur
+    seq, start = best[1], best[2]
+    fin = [start[k] + cost[k] + tail[k] for k in range(n)]
     _CACHE["plan"] = (ops, seq, groups, start, fin)
     return _CACHE["plan"]
 
 
 def rank_program(g, core, T, topo):
     rank = T.rank_of(core)
-    if rank is None:
-        return
     n = len(T.cores)
+    ops, seq, groups, start, fin = plan()
+    gsem = {name: "s%d" % k for k, name in enumerate(sorted(groups))}
+
+    def helper(src, dst):
+        if topo.chip(src) == topo.chip(dst):
+            return None
+        return [c for c in topo.cores_of(src) if c not in T.cores and topo.die(c) != topo.die(src) and topo.may_write(c, dst)][0]
+
+    def fused(to, engines, views, remote, local):
+        r, p = topo.addr(to)[0:2]
+        per = len(engines) // len(views)
+        g.remote_dma_fused([RemoteDMATransfer(dst_ids=[DstId(rid=r, pnc=p)], remote_sem=T.sem[remote], src=s, dst=d,
+                                              dma_engine_mask=sum(1 << x for x in engines[m * per:(m + 1) * per]))
+                            for m, (s, d) in enumerate(views)], local_sem=T.sem[local])
+
+    if rank is None:
+        for r in range(n):
+            src, dst = T.cores[r], T.cores[(r - 1) % n]
+            if helper(src, dst) == core:
+                spare = [x for x in topo.engines(src, core) if x not in topo.engines(src, dst)]
+                out = topo.engines(core, dst)
+                todo = [ops[k]["a"] for k in seq if ops[k]["k"] == "send" and ops[k]["a"][1] in VIA]
+                for pairs, grp in todo:
+                    g.wait_ge(T.sem[gsem[grp]], len(spare))
+                    fused(dst, out, [(T[d["n"]][d["i"]], T[d["n"]][d["i"]]) for s, d in pairs], gsem[grp], "sent")
+                g.wait_ge(T.sem["sent"], len(out) * len(todo))
+        return
     prev, nxt = T.cores[(rank - 1) % n], T.cores[(rank + 1) % n]
     rid, pid = topo.addr(prev)[0:2]
     eng = topo.engines(core, prev)
     got = len(topo.engines(nxt, core))
-    ops, seq, groups, start, fin = plan()
+    via = helper(core, prev)
     queue = {"g": g, "pe": g.tensor, "act": g.scalar, "dve": g.vector, "sync": g.sync}
-    gsem = {name: "s%d" % k for k, name in enumerate(sorted(groups))}
     total = {}
     for name, ks in groups.items():
         kind = ops[ks[0]]["k"]
@@ -689,7 +810,11 @@ def rank_program(g, core, T, topo):
             loc = gsem[o["g"]] if o["g"] is not None else "sent"
             per = len(eng) // len(pairs)
             masks = [sum(1 << x for x in eng[m * per:(m + 1) * per]) for m in range(len(pairs))]
-            if len(pairs) == 1:
+            if grp in VIA and via is not None:
+                spare = [x for x in topo.engines(core, via) if x not in eng]
+                assert len(spare) == len(eng)
+                fused(via, spare, [(ap(s), ap(d)) for s, d in pairs], gsem[grp], loc)
+            elif len(pairs) == 1:
                 g.remote_dma(ap(pairs[0][1]), ap(pairs[0][0]), T.sem[gsem[grp]], T.sem[loc], pid, rid, masks[0])
             else:
                 g.remote_dma_fused([RemoteDMATransfer(dst_ids=[DstId(rid=rid, pnc=pid)], dma_engine_mask=masks[m],
@@ -711,7 +836,7 @@ def rank_program(g, core, T, topo):
         elif kind == "ms":
             ins = q.memset(ap(a[0]), a[1])
         elif kind == "act":
-            f = {"Sigmoid": AF.Sigmoid, "Identity": AF.Identity, "Sign": AF.Sign, "Relu": AF.Relu}[a[2]]
+            f = {"Sigmoid": AF.Sigmoid, "Identity": AF.Identity, "Sign": AF.Sign, "Relu": AF.Relu, "Abs": AF.Abs}[a[2]]
             ins = q.activation(ap(a[0]), ap(a[1]), f, bias=a[3], scale=a[4])
         elif kind == "mm":
             ins = q.matmul(ap(a[0]), ap(a[1]), ap(a[2]), a[3], a[4])

@@ -7,66 +7,74 @@ V = 1536
 W = 3840
 RK = 1536
 GR = 2688
-CR, CG, CW = 2400, 4200, 5744
+CR, CG, CW = 1536, 3072, 4608
 
-BASE_PE = (1, 1, 1, 1, 1)
-MASK_PE = (1, 1, 1, 1, 1)
-A_PE = (2, 2, 2, 2, 2, 2)
-DVE_G = (2, 0, 0, 0, 0, 0)
-XA = 3
-ACC = False
-NOFF = (0, 0, 0, 0, 0, 0)
-SC = (0, 1, 0)
-VIA = ("in1", "in3", "nm0", "nm1", "nm2", "xd21", "xw0", "xw2")
-PE_NS = 0.45
-P = {"NET": 62.0, "NETLAT": 2200, "SEED": 5, "ITER": 45, "OVH": 35.0}
+OPT = {
+    "KEY_ACT": (2, 4, 1, 4, 1, 4),
+    "A_PE": (0, 2, 0, 2, 0, 2),
+    "HL_DMA": (1, 1, 1, 1, 1, 1),
+    "PL": (("pl0", "pl1", "pm0", "pm1", "pl0"), ("pl1", "pl0", "pl1", "pl0", "pl1")),
+    "AFTER": (9, 9, 9),
+    "LISTS": (99, 99),
+    "LE_DMA": (2, 0, 2, 0, 2, 0),
+    "LT_DMA": (0, 0, 0, 0, 0, 0),
+    "MASK_DMA": (0, 0, 0, 0, 0, 0),
+    "MASK_ACT": (5, 4, 5, 4, 5, 4),
+    "OWN_ACT": 4,
+    "ENDS": 0,
+    "LE_FIRST": 0,
+    "DVE_G": (4, 0, 0, 0, 0, 0),
+    "ROWS": ("ZZXX", "ZZZX", "ZZXY", "XYYY"),
+    "VIA": ("in0", "in3", "nm0", "nm1", "nm2", "xd21", "xw0", "xw2", "xz0"),
+}
+P = {"NET": 62.0, "NETLAT": 2200, "SEED": 1, "ITER": 6, "MOVES": 80, "POLISH": 8000, "TEMP": 20.0, "SOON": {},
+     "OVH": 50.0, "LAG": 80.0, "PE": 0.43,
+     "GDMA": 900.0, "DMA": 500.0, "OCC": 0.15, "NEAR": 120.0, "DLAT": 1900.0, "ACC": 2.0, "PAD": (150.0, 0.15, 150.0),
+     "ALTS": ((1.0, 1.0, 1.0, 1.0, 0.0, 0.1, 1.0), (1.2, 1.0, 1.0, 1.0, 0.0, 0.1, 1.25), (0.8, 1.2, 1.0, 1.2, 400.0, 0.25, 1.0))}
 
 SCRATCH = {}
 for _t in range(4):
-    SCRATCH["wl%d" % _t] = ("sbuf", [128, W], "float32")
-    SCRATCH["wh%d" % _t] = ("sbuf", [128, W], "float32")
+    SCRATCH["w%d" % _t] = ("sbuf", [128, 2, W], "float32")
 for _t in range(2):
-    SCRATCH["lo%d" % _t] = ("sbuf", [128, 5 * Q], "float32")
+    SCRATCH["lo%d" % _t] = ("sbuf", [128, 4 * Q], "float32")
     SCRATCH["hi%d" % _t] = ("sbuf", [128, 5 * Q], "float32")
     SCRATCH["sf%d" % _t] = ("sbuf", [128, 4, 2, 24], "float32")
     SCRATCH["su%d" % _t] = ("sbuf", [128, 192], "uint16")
-    SCRATCH["vv%d" % _t] = ("sbuf", [128, 144], "float32")
+    SCRATCH["vv%d" % _t] = ("sbuf", [128, 96], "float32")
+    SCRATCH["kb%d" % _t] = ("sbuf", [128, 4, 2, 24], "float32")
+    SCRATCH["s%d" % (_t + 1)] = ("sbuf", [128, 192], "bfloat16")
 for _t in range(3):
     SCRATCH["land%d" % _t] = ("sbuf", [128, 768], "bfloat16")
 for _n in ("pl0", "pl1", "pk0", "pk1", "pa", "pm0", "pm1", "pc"):
     SCRATCH[_n] = ("psum", [128, 512], "float32")
 SCRATCH.update({
-    "tb": ("sbuf", [128, GR], "bfloat16"), "db": ("sbuf", [128, GR], "bfloat16"), "fb": ("sbuf", [128, GR], "bfloat16"),
-    "cmp": ("sbuf", [128, (18 + max(NOFF)) * Q], "bfloat16"),
-    "le": ("sbuf", [128, 4 * Q], "bfloat16"), "lt": ("sbuf", [128, 5 * Q], "bfloat16"),
-    "k2": ("sbuf", [128, Q], "float32"), "kk": ("sbuf", [128, Q], "float32"), "bb": ("sbuf", [128, Q], "float32"), "rr": ("sbuf", [128, Q], "bfloat16"),
-    "a1": ("sbuf", [128, Q], "float32"), "a2": ("sbuf", [128, Q], "float32"),
-    "cst": ("sbuf", [128, Q], "bfloat16"),
+    "td": ("sbuf", [128, 18 * Q], "bfloat16"), "fb": ("sbuf", [128, 2, GR], "bfloat16"),
+    "cmp": ("sbuf", [128, 25 * Q], "bfloat16"),
+    "k2": ("sbuf", [128, Q], "float32"), "kk": ("sbuf", [128, Q], "float32"), "a0": ("sbuf", [128, Q], "float32"),
+    "rr": ("sbuf", [128, Q], "bfloat16"), "a1": ("sbuf", [128, Q], "float32"), "cst": ("sbuf", [128, Q], "bfloat16"),
     "wc": ("sbuf", [128, CW], "bfloat16"), "gg": ("sbuf", [128, 768], "bfloat16"),
     "sli": ("sbuf", [128, 2, 2, 4, 24], "int32"), "rfi": ("sbuf", [128, 2, 2, 24], "int32"),
     "rn": ("sbuf", [128, 2, 2, 24], "float32"), "r2": ("sbuf", [128, 96], "float32"), "rt": ("sbuf", [128, 128], "float32"),
     "pp": ("sbuf", [128, 10, 2, 2, 24], "bfloat16"),
-    "ph": ("sbuf", [128, 4, 2, 24], "bfloat16"), "pw": ("sbuf", [128, 4, 2, 24], "bfloat16"),
+    "g1": ("sbuf", [128, 48], "bfloat16"), "g2": ("sbuf", [128, 48], "bfloat16"),
     "dd": ("sbuf", [128, 144], "float32"), "mh": ("sbuf", [128, 144], "bfloat16"), "mn": ("sbuf", [128, 144], "bfloat16"),
-    "m8": ("sbuf", [128, 128], "bfloat16"), "n8": ("sbuf", [128, 128], "bfloat16"),
-    "m1": ("sbuf", [128, 128], "bfloat16"), "n1": ("sbuf", [128, 128], "bfloat16"),
-    "f1": ("sbuf", [128, 128], "float32"), "fh": ("sbuf", [128, 128], "float32"), "fn": ("sbuf", [128, 128], "float32"),
+    "m1": ("sbuf", [128, 128], "bfloat16"), "n1": ("sbuf", [128, 128], "bfloat16"), "nh": ("sbuf", [128, 128], "bfloat16"),
+    "f1": ("sbuf", [128, 128], "float32"), "f4": ("sbuf", [128, 128], "float32"), "f8": ("sbuf", [128, 128], "float32"),
     "f96": ("sbuf", [128, 128], "float32"), "fm": ("sbuf", [128, 128], "float32"),
-    "sel": ("sbuf", [128, 7 * 144], "bfloat16"),
+    "sel": ("sbuf", [128, 9 * 144], "bfloat16"),
     "a8": ("sbuf", [128, 8], "float32"), "b8": ("sbuf", [128, 8], "int32"), "c8": ("sbuf", [128, 8], "int32"),
     "pi": ("sbuf", [128, 4], "int32"), "pj": ("sbuf", [128, 4], "int32"), "pf": ("sbuf", [128, 4], "float32"),
-    "v0": ("sbuf", [128, 144], "float32"),
-    "kb": ("sbuf", [128, 4, 2, 24], "float32"), "key": ("sbuf", [128, 4, 2, 24], "float32"),
+    "v0": ("sbuf", [128, 96], "float32"),
+    "dn": ("sbuf", [128, 192], "float32"), "key": ("sbuf", [128, 4, 2, 24], "float32"),
     "fall": ("sbuf", [128, 4, 2, 24], "float32"), "ok": ("sbuf", [128, 4, 2, 24], "float32"),
-    "rb": ("sbuf", [128, 4, 2, 24], "float32"), "rth": ("sbuf", [128, 4, 2, 24], "float32"),
     "mx": ("sbuf", [128, 2, 2, 24], "float32"), "best": ("sbuf", [128, 2, 24], "float32"), "bi": ("sbuf", [128, 48], "int32"),
-    "ci": ("sbuf", [128, 48], "int32"), "hh": ("sbuf", [128, 144], "float32"), "eq": ("sbuf", [128, 144], "bfloat16"),
-    "off": ("sbuf", [128, 48], "uint16"), "ti": ("sbuf", [128, 48], "int32"),
+    "ci": ("sbuf", [128, 48], "int32"), "eq": ("sbuf", [128, 144], "bfloat16"),
+    "off": ("sbuf", [128, 48], "uint16"), "cr": ("sbuf", [128, 48], "float32"), "ww": ("sbuf", [128, 48], "float32"),
+    "some": ("sbuf", [128, 48], "bfloat16"), "take": ("sbuf", [128, 48], "bfloat16"), "p8": ("sbuf", [128, 4], "float32"),
 })
-for _n in ("fc", "ta", "tc", "veto", "take", "g1", "g2", "gb", "thr", "bv", "cr", "ww"):
-    SCRATCH[_n] = ("sbuf", [128, 48], "float32")
-SCRATCH["some"] = ("sbuf", [128, 48], "bfloat16")
-SEMAPHORES = ["pe", "act", "dve", "pool", "sent"] + ["s%d" % _k for _k in range(140)]
+for _n in ("mb", "m20", "mq"):
+    SCRATCH[_n] = ("sbuf", [128, 128], "bfloat16")
+SEMAPHORES = ["pe", "act", "dve", "pool", "sent"] + ["s%d" % _k for _k in range(145)]
 
 IO = {"th": [128, V], "dl": [128, V], "dr": [128, V], "sl": [128, 384], "rf": [128, 96],
       "yt": [128, V], "yq": [128, V], "yr": [8, V]}
@@ -103,22 +111,40 @@ def cols(name, a, b, step=1):
     return ref(name, S_[:, a:b] if step == 1 else S_[:, a:b:step])
 
 
-def gath(win, offs):
-    r = dict(win)
+def win(t, s, a=0, n=10, rows=S_[:]):
+    return ref("w%d" % t, (rows, s, slice(a * Q, (a + n) * Q)))
+
+
+def both(name, a):
+    r = dict(ref(name, S_[:, :, a * Q:a * Q + Q]))
+    r["sub"] = [ref(name, S_[:, s, a * Q:a * Q + Q]) for s in range(2)]
+    return r
+
+
+def blk(name, a, n=1):
+    return cols(name, a * Q, (a + n) * Q)
+
+
+def gath(view, offs):
+    r = dict(view)
     r["ind"] = offs
     return r
 
 
 def build():
     ops = []
+    phase = ["start"]
 
     def add(eng, kind, args, reads, writes, cost, lat=0.0, grp=None):
-        rd = []
+        rd, wr = [], []
         for r in reads:
-            rd.append(r)
+            rd.extend(r.get("sub", [r]))
             if r["ind"] is not None:
                 rd.append(r["ind"])
-        ops.append({"e": eng, "k": kind, "a": args, "r": rd, "w": list(writes), "c": cost, "lat": lat, "g": grp, "x": []})
+        for r in writes:
+            wr.extend(r.get("sub", [r]))
+        ops.append({"e": eng, "k": kind, "a": args, "r": rd, "w": wr, "c": cost, "lat": lat, "g": grp, "x": [], "by": 0.0,
+                    "t": phase[0], "after": []})
         return len(ops) - 1
 
     def nel(out):
@@ -129,7 +155,9 @@ def build():
         if any(r["ind"] is not None for r in ins):
             return P["OVH"] + 1.3 * n
         k = 2.0 if two and all(_where(r["n"]) == "sbuf" for r in ins) else 1.0
-        return P["OVH"] + 0.83 * k * max(n, 48)
+        if not two and all(_bytes(r["n"]) == 2 for r in ins + [out]):
+            k = 0.5
+        return P["OVH"] + 0.83 * max(k * n, 64)
 
     def tt(out, a, b, op):
         return add("dve", "tt", (out, a, b, op), [a, b], [out], vcost(out, [a, b], True))
@@ -145,93 +173,139 @@ def build():
         return add("dve", "ms", (out, val), [], [out], 55 + 0.42 * nel(out))
 
     def act(out, a, bias=0.0, scale=1.0, func="Identity"):
-        return add("act", "act", (out, a, func, bias, scale), [a], [out], 15 + vcost(out, [a]))
+        n = nel(out)
+        c = P["OVH"] + 15 + (1.3 * n if a["ind"] is not None else 0.83 * max(n, 64))
+        return add("act", "act", (out, a, func, bias, scale), [a], [out], c)
 
     def mm(out, lhs, rhs, start, stop):
         k = 4 if _bytes(rhs["n"]) == 4 else 1
-        return add("pe", "mm", (out, lhs, rhs, start, stop), [lhs, rhs], [out], 10 + PE_NS * k * max(64, nel(rhs)))
+        return add("pe", "mm", (out, lhs, rhs, start, stop), [lhs, rhs], [out], 10 + P["PE"] * k * max(64, nel(rhs)))
+
+    def mms(out, terms, start, stop):
+        calls = [(out, w, y, start and m == 0, stop and m == len(terms) - 1) for m, (w, y) in enumerate(terms)]
+        c = sum(10 + P["PE"] * (4 if _bytes(y["n"]) == 4 else 1) * max(64, nel(y)) for w, y in terms)
+        seen = {}
+        for w, y in terms:
+            for r in (w, y):
+                seen.setdefault((r["n"], r["s"][2] // 192, r["s"][3] // 192), r)
+        wide = [cols(r["n"], a * 192, min(b * 192 + 192, SCRATCH[r["n"]][1][1])) if len(SCRATCH[r["n"]][1]) == 2 else ref(r["n"])
+                for (nm, a, b), r in seen.items()]
+        return add("pe", "mms", calls, wide, [out], c)
 
     def iota(out, pat, base, cm):
         return add("g", "iota", (out, pat, base, cm), [], [out], 130 + 1.7 * nel(out))
 
     def dma(q, out, a, grp, accum=False):
-        by = nel(out) * out["s"][5] * _bytes(out["n"])
+        ns = nel(out) * out["s"][5] * _bytes(out["n"]) * (P["ACC"] if accum else 1) / P["DMA"]
         rd = [a, out] if accum else [a]
-        return add(q, "dma", (out, a, accum), rd, [out], 900 if q == "g" else 80, 1900 + by / 300.0, grp)
+        k = add(q, "dma", (out, a, accum), rd, [out], P["GDMA"] if q == "g" else 80, P["DLAT"] + ns, grp)
+        ops[k]["by"] = ns
+        return k
 
     def send(pairs, grp, own=None, after=()):
         by = sum(nel(s) * 128 * _bytes(s["n"]) for s, d in pairs)
         k = add("g", "send", (pairs, grp), [s for s, d in pairs] + list(after), [], 300, 1500 + by / P["NET"], own)
-        by2 = grp in VIA
+        by2 = grp in OPT["VIA"]
+        ops[k]["by"] = P["OCC"] * by / (P["NEAR"] if by2 else P["NET"])
         a = add("net2" if by2 else "net", "arrive", (len(pairs),), [], [d for s, d in pairs], by / P["NET"],
                 P["NETLAT"] + (3200 if by2 else 0), grp)
         ops[a]["x"].append(k)
+        return k
 
-    dma("sync", cols("tb", 0, Q), cols("th", 0, Q), "ld0")
-    dma("act", cols("db", 0, Q), cols("dl", 0, Q), "ld0")
-    dma("sync", cols("tb", Q, 1152), cols("th", Q, 1152), "ld5")
-    dma("act", cols("db", Q, 1152), cols("dl", Q, 1152), "ld5")
+    dma("sync", blk("td", 0), blk("th", 0), "ld0")
+    dma("act", blk("td", 7), blk("dl", 0), "ld0")
+    dma("sync", blk("td", 1, 2), blk("th", 1, 2), "ld5")
+    dma("act", blk("td", 8, 2), blk("dl", 1, 2), "ld5")
     dma("sync", ref("sli"), ref("sl"), "ld1")
-    dma("sync", cols("tb", 1152, V), cols("th", 1152, V), "ld2")
-    dma("sync", cols("db", 1152, V), cols("dl", 1152, V), "ld2")
-    dma("sync", cols("fb", 0, V), ref("dr"), "ld3")
     dma("sync", ref("rfi"), ref("rf"), "ld4")
     iota(ref("dd"), [[-1, 144]], 0, 1)
     iota(ref("a8"), [[-16, 8]], 0, 1)
     iota(ref("pi"), [[0, 4]], 0, 1)
-    iota(ref("v0"), [[0, 3], [768, 2], [16, 24]], 0, 0)
-    for a in range(3):
-        send([(cols("tb", a * Q, a * Q + Q), cols("tb", RK + a * Q, RK + a * Q + Q)),
-              (cols("db", a * Q, a * Q + Q), cols("db", RK + a * Q, RK + a * Q + Q))], "in%d" % a)
-    for n, s in (("mh", 0.5), ("mn", -0.5)):
+    iota(ref("v0"), [[0, 2], [48, 2], [1, 24]], 0, 0)
+    first = [send([(blk("td", a), blk("td", 4 + a)), (blk("td", 7 + a), blk("td", 11 + a))], "in%d" % a, "io%d" % a)
+             for a in range(3)]
+    for k in (dma("sync", blk("td", 3), blk("th", 3), "ld2"), dma("sync", blk("td", 10), blk("dl", 3), "ld2"),
+              dma("sync", ref("fb", S_[:, 0, 0:V]), ref("dr"), "ld3")):
+        ops[k]["after"].append(first[0])
+    for n, s in (("mh", 1.0 / 16), ("mn", -1.0 / 16)):
         ts(cols(n, 0, 128), cols("dd", 0, 128), 0.0, s, AL.is_equal, AL.mult)
         ts(cols(n, 128, 144), cols("dd", 128, 144), -128.0, s, AL.is_equal, AL.mult)
     ts(ref("f1"), cols("dd", 0, 128), 0.0, None, AL.is_equal)
-    for n, s in (("m8", 8.0), ("n8", -8.0), ("m1", 1.0), ("fh", 0.5), ("f96", 96.0), ("fm", -1535.0 / 16)) + ((("fn", -1.0),) if max(NOFF) else ()):
+    for n, s in (("m1", 1.0), ("n1", -1.0), ("nh", -0.5), ("f4", 4.0), ("f8", 8.0), ("f96", 96.0), ("fm", -1535.0 / 16),
+                 ("mb", 2.0 ** 21), ("m20", 20.0), ("mq", -0.75)):
         act(ref(n), ref("f1"), 0.0, s)
-    if 1 in A_PE:
-        act(ref("n1"), ref("f1"), 0.0, -1.0)
-        ms(ref("cst"), 1536.0)
+    ms(ref("cst"), 192.0)
     ms(ref("sel"), 0.0)
-    ms(cols("wc", 0, CW // 8), 0.0)
-    for k in range(1, 8):
-        dma("sync", cols("wc", k * CW // 8, (k + 1) * CW // 8), cols("wc", 0, CW // 8), "zero")
     ts(ref("b8"), ref("a8"), 0.5, -0.25, AL.mult, AL.add)
     ts(ref("c8"), ref("a8"), 0.0625, -0.46875, AL.mult, AL.add)
     for j in range(5):
         ts(cols("sel", j * 144 + 15, j * 144 + 143, 16), ref("b8"), float(j), None, AL.is_equal)
-    for j, s in ((5, 16384.0), (6, -16384.0)):
+    for j, s in ((5, 32768.0), (6, -32768.0), (7, 16384.0), (8, -16384.0)):
         ts(cols("sel", j * 144 + 15, j * 144 + 143, 16), ref("c8"), 0.0, s, AL.is_equal, AL.mult)
     ts(ref("pj"), ref("pi"), 15, None, AL.bitwise_and)
-    cp(ref("pf"), ref("pj"))
+    ts(ref("pf"), ref("pj"), 96.0, None, AL.mult)
+    ts(ref("p8"), ref("pj"), 8.0, float(CR), AL.is_equal, AL.mult)
+    for k in range(4):
+        ts(blk("wc", 3 * k, 3), blk("td", 0, 3), 0.0, cols("p8", 0, 1), AL.mult, AL.add)
     for p in range(2):
-        ts(ref("vv%d" % p), ref("v0"), cols("pf", 0, 1), 384.0 * p, AL.add, AL.add)
+        ts(ref("vv%d" % p), ref("v0"), cols("pf", 0, 1), 24.0 * p, AL.add, AL.add)
 
     def selv(j, i):
         return cols("sel", j * 144 + 15 - i, j * 144 + 143 - i)
 
+    phase[0] = "lists"
     for p in range(2):
         for h in range(2):
             cp(ref("sf%d" % p, S_[:, :, h, :]), ref("sli", S_[:, h, p, :, :]))
         cp(ref("su%d" % p), ref("sf%d" % p))
-    cp(ref("rn"), ref("rfi"))
+    cp(ref("r2"), ref("rfi"))
+
+    def step(out, x, at, size):
+        act(out, x, 0.5 - at, 1.0, "Sign")
+        act(out, out, 0.0, size, "Relu")
+
+    def place(x, m):
+        down, big = cols("dn", 0, m), 1.5 * 2.0 ** 27
+        act(down, x, -7.5)
+        act(down, down, big)
+        act(down, down, -big)
+        step(cols("s1", 0, m), x, RK, CR - RK // 16)
+        step(cols("s2", 0, m), x, GR, CG - GR // 16 - CR + RK // 16)
+        po = cols("pc", 0, m)
+        mm(po, ref("f96"), x, True, False)
+        mm(po, ref("fm"), down, False, False)
+        mm(po, ref("m1"), cols("s1", 0, m), False, False)
+        mm(po, ref("m1"), cols("s2", 0, m), False, True)
+
+    def keybase(t):
+        phase[0] = "base%d" % t
+        place(ref("sf%d" % (t % 2)), 192)
+        for j in range(4):
+            for h in range(2):
+                signs = min(OPT["LE_DMA"][2 * t + h], 1) - OPT["LT_DMA"][2 * t + h]
+                act(ref("kb%d" % (t % 2), S_[:, j, h, :]), cols("pc", 48 * j + 24 * h, 48 * j + 24 * h + 24),
+                    8192.0 * (3 - j) + 262144.0 * signs)
+
+    place(ref("r2"), 96)
+    act(ref("rn"), cols("pc", 0, 96))
+    keybase(0)
+    keybase(1)
 
     def parts(p):
         sf = "sf%d" % p
-        act(ref("ph"), ref(sf))
-        tt(ref("pw"), ref(sf), ref("ph"), AL.subtract)
-        for j in range(4):
-            act(ref("pp", S_[:, 2 * j, :, p, :]), ref("ph", S_[:, j]))
-            act(ref("pp", S_[:, 2 * j + 1, :, p, :]), ref("pw", S_[:, j]))
         act(ref("pp", S_[:, 8, :, p, :]), ref("rn", S_[:, :, p, :]))
         tt(ref("pp", S_[:, 9, :, p, :]), ref("rn", S_[:, :, p, :]), ref("pp", S_[:, 8, :, p, :]), AL.subtract)
+        act(ref("pp", S_[:, 0:8:2, :, p, :]), ref(sf))
+        return tt(ref("pp", S_[:, 1:8:2, :, p, :]), ref(sf), ref("pp", S_[:, 0:8:2, :, p, :]), AL.subtract)
 
     def names(t):
+        phase[0] = "names%d" % t
         send([(ref("pp", S_[:, 0:8]), ref("land%d" % t))], "nm%d" % t, "no%d" % t)
         for k in range(10):
             dma("sync", ref("wc", S_[k::16, 0:V]), ref("pp", S_[:, k]), "wa%d" % t)
-        dma("sync", ref("wc", S_[0:112, CG:CG + V]), ref("wc", S_[16:128, 0:V]), "wb%d" % t)
-        dma("sync", ref("wc", S_[112:128, CG:CG + V]), ref("wc", S_[0:16, 0:V]), "wb%d" % t)
+        for k in range(8):
+            n = 16 * ((k + 1) % 8)
+            dma("sync", ref("wc", S_[16 * k:16 * k + 8, CG:CG + V]), ref("wc", S_[n:n + 8, 0:V]), "wb%d" % t)
         for k in range(8):
             dma("sync", ref("wc", S_[k::16, CR:CR + V]), cols("land%d" % t, 96 * k, 96 * k + 96), "wc%d" % t)
 
@@ -239,308 +313,396 @@ def build():
     nb = [0]
 
     def w0(dst, src, sh):
-        for nm, m2, f in (("wl0", "mn", cp), ("wh0", "mh", act)):
+        for s, m2, f in ((0, "mn", cp), (1, "mh", act)):
             b = cols(banks[nb[0] % 7], 0, Q)
             nb[0] += 1
-            mm(b, cols("mh", sh, sh + 128), cols("tb", src, src + Q), True, False)
-            mm(b, cols(m2, sh, sh + 128), cols("db", src, src + Q), False, True)
-            f(cols(nm, dst, dst + Q), b)
+            mm(b, cols("mh", sh, sh + 128), blk("td", src), True, False)
+            mm(b, cols(m2, sh, sh + 128), blk("td", 7 + src), False, True)
+            f(win(0, s, dst, 1), b)
 
+    phase[0] = "own"
     for a in range(3):
-        w0(a * Q, a * Q, 0)
-        w0(GR + a * Q, a * Q, 16)
-    w0(3 * Q, 3 * Q, 0)
+        w0(a, a, 0)
+        w0(7 + a, a, 16)
+    w0(3, 3, 0)
+    phase[0] = "far"
     for a in range(3):
-        w0(RK + a * Q, RK + a * Q, 0)
+        w0(4 + a, 4 + a, 0)
+    phase[0] = "parts"
     parts(0)
     parts(1)
     names(0)
+    phase[0] = "drift"
 
-    send([(cols("fb", 0, 1152), cols("fb", RK, GR))], "in3", None, [cols("db", GR - Q, GR)])
+    ts(ref("fb", S_[:, 0, 0:V]), ref("fb", S_[:, 0, 0:V]), 1.0 / 16, None, AL.mult)
+    send([(ref("fb", S_[:, 0, 0:1152]), ref("fb", S_[:, 0, RK:GR]))], "in3", "io3", [blk("td", 13)])
+    dma("sync", ref("fb", S_[:, 1, 0:V]), ref("fb", S_[:, 0, 0:V]), "fo")
+    dma("sync", ref("fb", S_[:, 1, RK:GR]), ref("fb", S_[:, 0, RK:GR]), "ff")
 
-    def share(views, tag, far=True):
+    def share(t, views, tag, far=True):
         if far:
-            send([(cols(n, a * Q, a * Q + Q), cols(n, RK + a * Q, RK + a * Q + Q)) for n, a in views], "x" + tag)
-        for n, a in views:
-            dma("sync", ref(n, S_[0:112, GR + a * Q:GR + a * Q + Q]), ref(n, S_[16:128, a * Q:a * Q + Q]), "y" + tag)
-            dma("sync", ref(n, S_[112:128, GR + a * Q:GR + a * Q + Q]), ref(n, S_[0:16, a * Q:a * Q + Q]), "y" + tag)
+            send([(win(t, s, a, 1), win(t, s, 4 + a, 1)) for s, a in views], "x" + tag)
+        for s, a in views:
+            dma("sync", win(t, s, 7 + a, 1, S_[0:112]), win(t, s, a, 1, S_[16:128]), "y" + tag)
+            dma("sync", win(t, s, 7 + a, 1, S_[112:128]), win(t, s, a, 1, S_[0:16]), "y" + tag)
 
     def drift(t, a):
-        c0, c1 = a * Q, a * Q + Q
-        wide = 0.0 if t == 0 else 1.0 / 32
+        phase[0] = "drift%d%d" % (t, a)
         if t < 2:
-            for b0 in ((c0, RK + c0) if a < 3 else (c0,)):
-                for n, s in (("wl", -1.0), ("wh", 1.0)):
-                    act(cols("%s%d" % (n, t + 1), b0, b0 + Q), cols("fb", b0, b0 + Q), s * wide, 0.5)
-                    dma("g", cols("%s%d" % (n, t + 1), b0, b0 + Q), cols("%s%d" % (n, t), b0, b0 + Q), "d%d_%d" % (t, b0), True)
+            for b in ((a, 4 + a) if a < 3 else (a,)):
+                dma("sync", both("w%d" % (t + 1), b), both("w%d" % t, b), "c%d_%d" % (t, b))
+                dma("g", both("w%d" % (t + 1), b), both("fb", b), "d%d_%d" % (t, b), True)
             if a < 3:
-                share([("wl%d" % (t + 1), a), ("wh%d" % (t + 1), a)], "d%d%d" % (t, a), False)
+                share(t + 1, [(0, a), (1, a)], "d%d%d" % (t, a), False)
         else:
-            act(cols("wl3", c0, c1), cols("fb", c0, c1))
-            dma("g", cols("wl3", c0, c1), cols("wl2", c0, c1), "e%d" % a, True)
-            dma("g", cols("wl3", c0, c1), cols("wh2", c0, c1), "f%d" % a, True)
-            dma("sync", cols("yt", c0, c1), cols("wl3", c0, c1), "out")
+            act(win(3, 0, a, 1), ref("fb", S_[:, 0, a * Q:a * Q + Q]), 0.0, 2.0)
+            dma("g", win(3, 0, a, 1), win(2, 0, a, 1), "e%d" % a, True)
+            dma("g", win(3, 0, a, 1), win(2, 1, a, 1), "f%d" % a, True)
+            theta(a)
             if a < 3:
-                share([("wl3", a), ("wh3", a)], "d%d%d" % (t, a))
+                share(3, [(0, a), (1, a)], "d%d%d" % (t, a))
+
+    def theta(a):
+        y = win(1, a // 2, 7 + a % 2, 1)
+        act(y, win(3, 0, a, 1), 0.0, 8.0)
+        dma("sync", blk("yt", a), y, "out")
+
+    done = [None, None]
 
     def poll(t, h):
         p = t % 2
         a = 2 * h + p
         ck = 2 * t + h
-        lo, hi = "lo%d" % (ck % 2), "hi%d" % (ck % 2)
-        wl, wh = "wl%d" % t, "wh%d" % t
-        c0, c1 = a * Q, a * Q + Q
-        wide = 0.0 if t == 0 else 1.0 / 32
+        lo, hi = "lo%d" % h, "hi%d" % h
+        c2 = t / 128.0
+        eps = 2.0 ** -21
+        hl_dma, le_dma, lt_dma, mask_dma = [OPT[n][ck] for n in ("HL_DMA", "LE_DMA", "LT_DMA", "MASK_DMA")]
+        lt0, le0 = 5 * h, 10 + 4 * h
+        ends = ck == 5 and OPT["ENDS"]
+        assert not ends or (OPT["MASK_ACT"][ck] >= 4 and not (le_dma or lt_dma or mask_dma))
 
         def L(j):
-            return cols(lo, j * Q, j * Q + Q)
+            return blk(lo, j) if j < 4 else win(t, 0, a, 1)
 
         def H(j):
-            return cols(hi, j * Q, j * Q + Q)
+            return blk(hi, j + 1) if j < 4 else win(t, 1, a, 1)
 
-        act(L(4), cols(wl, c0, c1), -wide)
-        act(H(4), cols(wh, c0, c1), wide)
+        def LT(j):
+            return blk("td", lt0 + (j + 1) % 5)
+
+        phase[0] = "gather%d" % ck
+        if lt_dma or hl_dma:
+            dma("sync", blk(hi, 0), H(4), "o%d" % ck)
         ng = 0
-        for j in range(4):
+        for j in ((3, 0, 1, 2) if hl_dma else range(4)):
             o = cols("su%d" % p, j * 48 + h * 24, j * 48 + h * 24 + 24)
-            for dst, w, b in ((L(j), wl, -wide), (H(j), wh, wide)):
-                if ng % 2 == 0 and ng // 2 < DVE_G[ck]:
-                    ts(dst, gath(ref(w), o), b, None, AL.add)
+            for dst, s, b in ((L(j), 0, -c2), (H(j), 1, 0.0)):
+                if ng % 2 == 0 and ng // 2 < OPT["DVE_G"][ck]:
+                    ts(dst, gath(win(t, s), o), b, None, AL.add)
                 else:
-                    act(dst, gath(ref(w), o), b)
+                    act(dst, gath(win(t, s), o), b)
                 ng += 1
         terms = {i: [] for i in range(5)}
+        if hl_dma:
+            phase[0] = "aside%d" % ck
+            xt, x0 = (3, 0) if t == 0 else (0, 5)
+            act(win(xt, h, x0, 1), L(3), 0.0, -1.0)
+            for m in range(1, 4):
+                dma("sync", win(xt, h, x0 + m, 1), win(xt, h, x0, 1), "g%d" % ck)
+            dma("g", win(xt, h, x0, 4), blk(hi, 0, 4), "j%d" % ck, True)
+            for m in (0, 2):
+                act(blk("cmp", 18 + m, 2), win(xt, h, x0 + m, 2), -eps, -1.0, "Sign")
         slot = [0, 0]
-        kk = ref("kk" if ck % 2 else "k2")
+        kk = ref("kk" if h else "k2")
         order = (4, 0, 1, 2, 3)
-        aside = (4, 0, 1, 2)[:NOFF[ck]]
-        for m, j in enumerate(aside):
-            c = cols("cmp", (18 + m) * Q, (19 + m) * Q)
-            pd = cols("pk1", 0, Q)
-            mm(pd, ref("f1"), L(3), True, False)
-            mm(pd, ref("fn"), H(j), False, True)
-            act(c, pd, -4096.0, 2.0 ** 30, "Sigmoid")
-            terms[3].append(("n8", c))
         for n, i in enumerate(order):
-            pl = cols(("pl0", "pl1", "pk0", "pk1")[(5 * ck + n) % (3 if max(NOFF) else 4)] if ACC else "pl%d" % (n % 2), 0, Q)
-            if ACC:
-                mm(pl, ref("f1"), L(i), True, False)
-            else:
-                act(pl, L(i))
+            phase[0] = "key%d_%d" % (ck, n)
+            aside = hl_dma and i == 3
+            pl = cols(OPT["PL"][h][n], 0, Q)
+            if not aside:
+                act(pl, L(i), -c2 if i == 4 else 0.0)
             for j in range(5):
-                if j == i or (i == 3 and j in aside):
+                if j == i:
                     continue
                 if j in order[n + 1:]:
-                    c = cols("cmp", slot[0] * Q, slot[0] * Q + Q)
+                    c = blk("cmp", slot[0])
                     slot[0] += 1
                     near = abs(i - j) <= 2
                     if i < j:
-                        op, si = (AL.is_le, "m8") if near else (AL.is_gt, "n8")
+                        op, si = (AL.is_le, "m1") if near else (AL.is_gt, "n1")
                     else:
-                        op, si = (AL.is_ge, "n8") if near else (AL.is_lt, "m8")
+                        op, si = (AL.is_ge, "n1") if near else (AL.is_lt, "m1")
                     tt(c, L(j), pl, op)
                     terms[i].append((si, c))
-                    terms[j].append(("n8" if si == "m8" else "m8", c))
-                c = cols("cmp", (10 + slot[1] % 8) * Q, (11 + slot[1] % 8) * Q)
-                slot[1] += 1
-                tt(c, H(j), pl, AL.is_lt)
-                terms[i].append(("n8", c))
-            pk = pl if ACC else cols("pk%d" % (n % 2), 0, Q)
-            tl = ([("f1", L(i))] if BASE_PE[n] and not ACC else []) + terms[i]
-            for m, (w, c) in enumerate(tl):
-                mm(pk, ref(w), c, m == 0 and not ACC, m == len(tl) - 1)
-            if BASE_PE[n]:
-                if n == 0:
-                    act(kk, pk)
+                    terms[j].append(("n1" if si == "m1" else "m1", c))
+                if aside:
+                    terms[i].append(("nh", blk("cmp", 18 + (j + 1) % 5)))
+                else:
+                    if j == 4:
+                        c = blk("cmp", 22 + i if i < 3 else 18)
+                    else:
+                        c = blk("cmp", 10 + slot[1] % 8)
+                        slot[1] += 1
+                    m = tt(c, H(j), pl, AL.is_lt)
+                    terms[i].append(("n1", c))
+                    if h == 1 and n == OPT["AFTER"][t]:
+                        ops[m]["x"].append(done[0])
+                    if t and 5 * h + n == OPT["LISTS"][t - 1]:
+                        ops[m]["x"].append(done[1])
+            pk = cols("pk%d" % (n % 2), 0, Q)
+            byact = n >= 5 - OPT["KEY_ACT"][ck] or aside
+            if byact:
+                mm(pk, ref("m1"), ref("cst"), True, False)
+                act(pk, L(i), -c2 if i == 4 else (-2.0 if aside else 0.0))
             else:
-                tt(kk if n == 0 else pk, L(i), pk, AL.add)
-            if n > 0:
+                mm(pk, ref("f1"), L(i), True, False)
+            for m, (w, c) in enumerate(terms[i]):
+                mm(pk, ref(w), c, False, m == len(terms[i]) - 1)
+            if n == 0:
+                act(kk, pk, 0.0 if byact else -c2)
+            else:
                 tt(kk, kk, pk, AL.max)
+        phase[0] = "low%d" % ck
         pa = cols("pa", 0, Q)
-        if A_PE[ck] == 2:
-            act(ref("rr"), kk, 1536.0)
-            act(pa, ref("rr"), -1536.0)
-            tt(pa, kk, pa, AL.subtract)
-        elif A_PE[ck]:
-            act(ref("rr"), kk, 1536.0)
+        if OPT["A_PE"][ck] == 1:
+            act(ref("rr"), kk, 192.0)
+            mm(pa, ref("f1"), kk, True, False)
+            act(ref("rr"), ref("rr"), -192.0)
+            mm(pa, ref("n1"), ref("rr"), False, True)
+        elif OPT["A_PE"][ck] == 3:
+            act(ref("rr"), kk, 192.0)
             mm(pa, ref("m1"), ref("cst"), True, False)
             mm(pa, ref("n1"), ref("rr"), False, False)
             mm(pa, ref("f1"), kk, False, True)
-        else:
-            ts(pa, kk, 100663296.0, -100663296.0, AL.add, AL.add)
+        elif OPT["A_PE"][ck] == 0:
+            act(ref("rr"), kk, 192.0)
+            act(pa, ref("rr"), -192.0)
             tt(pa, kk, pa, AL.subtract)
+        else:
+            ts(pa, kk, 1.5 * 2.0 ** 23, -1.5 * 2.0 ** 23, AL.add, AL.add)
+            tt(pa, kk, pa, AL.subtract)
+        if lt_dma:
+            k = 1.0 - c2 if t < 2 else 1.0 + 1.0 / 128
+        else:
+            k = (0.0, 1.0 / 64, 1.0 / 128)[t]
+        st = 2 if t == 0 else 0
+        na = win(st, h, 0, 1)
+        ncopy = 5 if lt_dma else (4 if le_dma else 1)
+        if lt_dma:
+            act(na, pa, k, -1.0)
         if t < 2:
-            act(cols("wl%d" % (t + 1), c0, c1), pa)
+            act(win(t + 1, 0, a, 1), pa, c2)
             if a < 3:
-                share([("wl%d" % (t + 1), a)], "l%d%d" % (t, a))
-        else:
+                share(t + 1, [(0, a)], "l%d%d" % (t, a))
+        elif lt_dma:
+            act(win(3, 0, a, 1), pa, c2 - 1.0 / 128, 2.0)
+        elif ends:
             act(ref("a1"), pa)
-            act(ref("a2"), pa, -1.0 / 16)
-        for n, j in enumerate(order):
-            lt = cols("lt", j * Q, j * Q + Q)
-            tt(lt, H(j), pa, AL.is_lt)
-            pm = cols("pm%d" % (n % 2), 0, Q)
-            if MASK_PE[n]:
-                mm(pm, ref("f1"), H(j), True, False)
-                mm(pm, ref("m8"), lt, False, True)
-                if n == 0:
-                    act(ref("bb"), pm)
-            else:
-                act(pm, lt, -8.0, 16.0)
-                tt(ref("bb") if n == 0 else pm, H(j), pm, AL.max)
-            if n > 0:
-                dst = ref("bb") if n < 4 else (cols("wh%d" % (t + 1), c0, c1) if t < 2 else pm)
-                tt(dst, ref("bb"), pm, AL.min)
-        if t == 2:
-            tt(cols("wl3", c0, c1), ref("a1"), pm, AL.add)
-            tt(cols("wh3", c0, c1), pm, ref("a2"), AL.subtract)
-            share([("wl3", a)], "z%d" % a)
-            share([("wh3", a)], "w%d" % a)
-            dma("sync", cols("yt", c0, c1), cols("wl3", c0, c1), "out")
+            send([(ref("a1"), win(3, 0, 4 + a, 1))], "xa")
+            act(cols("pm0", 0, Q), pa, 1.0 / 128)
         else:
-            if a < 3:
-                share([("wh%d" % (t + 1), a)], "h%d%d" % (t, a))
-            if t == 1:
-                tt(cols("wh3", c0, c1), cols("wh2", c0, c1), pa, AL.subtract)
-                act(cols("wh3", c0, c1), cols("wh3", c0, c1), 0.125)
-        for j in range(4):
-            tt(cols("le", j * Q, j * Q + Q), L(j), pa, AL.is_le)
-        pn = cols("pc", h * 96, h * 96 + 96)
-        for i in range(16):
-            mm(pn, selv(5, i), cols("le", i, 4 * Q, 16), i == 0, False)
-        for i in range(16):
-            mm(pn, selv(6, i), cols("lt", i, 4 * Q, 16), False, i == 15)
-        if h == 0:
+            act(ref("a%d" % h), pa, c2)
+        if not lt_dma and (le_dma or t > 0) and not ends:
+            act(na, pa, k, -1.0)
+        if le_dma == 2 and not lt_dma:
+            ncopy = 1
+        for m in range(1, ncopy):
+            dma("sync", win(st, h, m, 1), na, "n%d" % ck)
+        phase[0] = "high%d" % ck
+        wnew = win(t + 1, 1, a, 1)
+        pm = cols("pm%d" % h, 0, Q)
+        if lt_dma:
+            dma("g", ref(hi), win(st, h, 0, 5), "t%d" % ck, True)
+            act(blk("td", lt0, 5), ref(hi), k - eps, -1.0, "Sign")
+            dma("g", ref(hi), blk("td", lt0, 5), "m%d" % ck, True)
+            mm(pm, ref("f1"), blk(hi, 0), True, True)
             for j in range(4):
-                act(ref("kb", S_[:, j]), ref("sf%d" % p, S_[:, j]), 4096.0 * (3 - j))
-        tt(ref("key", S_[:, :, h, :]), ref("kb", S_[:, :, h, :]), pn, AL.add)
-
-    def down(out, x, unit):
-        big = 1.5 * 2.0 ** 23 * unit
-        act(out, x, 0.5 - unit / 2)
-        act(out, out, big)
-        act(out, out, -big)
-
-    def lookup(x, extra, rows, scalar):
-        if scalar:
-            down(ref("ta"), x, 16.0)
-            po = cols("pc", 384, 432)
-            mm(po, ref("f96"), x, True, False)
-            if extra is not None:
-                mm(po, ref("f96"), extra, False, False)
-            mm(po, ref("fm"), ref("ta"), False, True)
-            ts(ref("off"), po, 0.25, None, AL.add)
+                done[0] = tt(pm if j < 3 else wnew, H(j), pm, AL.min)
+            if t == 1:
+                act(win(3, 1, a, 1), wnew, 1.0 / 64 + c2)
+            if t < 2:
+                dma("g", wnew, win(t + 1, 0, a, 1), "b%d" % ck, True)
+            else:
+                dma("g", win(3, 0, a, 1), wnew, "b%d" % ck, True)
         else:
-            ts(ref("ti"), x, 0.0625, -0.46875, AL.mult, AL.add)
-            ts(ref("ta"), ref("ti"), -1535.0 / 96, None, AL.mult)
-            if extra is not None:
-                tt(ref("tc"), x, extra, AL.add)
-                x = ref("tc")
-            tt(ref("ta"), ref("ta"), x, AL.add)
-            ts(ref("off"), ref("ta"), 96.0, 0.25, AL.mult, AL.add)
-        act(ref("gg"), gath(ref("wc"), ref("off")))
+            if mask_dma:
+                for j in range(4):
+                    tt(LT(j), H(j), pa, AL.is_lt)
+                dma("g", blk(hi, 1, 4), blk("td", lt0 + 1, 4), "m%d" % ck, True)
+                tt(LT(4), H(4), pa, AL.is_lt)
+                mm(pm, ref("f1"), H(4), True, False)
+                mm(pm, ref("m1"), LT(4), False, True)
+                for j in range(4):
+                    done[0] = tt(pm if j < 3 or t == 2 else wnew, H(j), pm, AL.min)
+            else:
+                for n, j in enumerate(order):
+                    tt(LT(j), H(j), pa, AL.is_lt)
+                    if h:
+                        pm = cols((("pm1", "pl0", "pk1", "pl1", "pk0"), ("pm1", "pl1", "pl0", "pk1", "pk0"))[hl_dma][n], 0, Q)
+                    else:
+                        pm = cols("pm%d" % (n % 2), 0, Q)
+                    if n >= 5 - OPT["MASK_ACT"][ck]:
+                        mm(pm, ref("m1"), ref("cst"), True, False)
+                        act(pm, H(j), c2 if ends and n else 0.0)
+                    else:
+                        mm(pm, ref("f1"), H(j), True, False)
+                    mm(pm, ref("m1"), LT(j), False, True)
+                    if n == 0:
+                        act(kk, pm, c2 if ends else 0.0)
+                    else:
+                        done[0] = tt(kk if n < 4 or ends else (wnew if t < 2 else pm), kk, pm, AL.min)
+            if ends:
+                send([(kk, win(3, 1, 4 + a, 1))], "xb")
+                tt(win(3, 0, a, 1), kk, pa, AL.add)
+                tt(wnew, kk, cols("pm0", 0, Q), AL.subtract)
+                act(cols("pl0", 0, Q), win(3, 0, 4 + a, 1))
+                act(cols("pl1", 0, Q), win(3, 0, 4 + a, 1), 1.0 / 128)
+                tt(win(3, 0, 4 + a, 1), win(3, 1, 4 + a, 1), cols("pl0", 0, Q), AL.add)
+                tt(win(3, 1, 4 + a, 1), win(3, 1, 4 + a, 1), cols("pl1", 0, Q), AL.subtract)
+            elif t == 2:
+                tt(win(3, 0, a, 1), ref("a%d" % h), pm, AL.add)
+                tt(wnew, na, pm, AL.add)
+            if t == 1:
+                dma("sync", win(3, 1, a, 1), wnew, "u%d" % ck)
+                dma("g", win(3, 1, a, 1), na, "v%d" % ck, True)
+        if t == 2:
+            share(3, [(0, a)], "z%d" % a, not ends)
+            share(3, [(1, a)], "w%d" % a, not ends)
+            theta(a)
+        elif a < 3:
+            share(t + 1, [(1, a)], "h%d%d" % (t, a))
+        phase[0] = "hold%d" % ck
+        if le_dma:
+            if ncopy == 1:
+                for j in range(4):
+                    dma("g", L(j), na, "k%d_%d" % (ck, j // 2), True)
+            else:
+                dma("g", ref(lo), win(st, h, 0, 4), "k%d" % ck, True)
+            for j in (0, 2):
+                act(blk("td", le0 + j, 2), blk(lo, j, 2), k + eps, -1.0, "Sign")
+        else:
+            for j in range(4):
+                tt(blk("td", le0 + j), L(j), pa, AL.is_le)
+        pn = cols("pc", h * 96, h * 96 + 96)
+        sums = [[(selv(7 if le_dma else 5, i), cols("td", le0 * Q + i, (le0 + 4) * Q, 16)) for i in range(16)],
+                [(selv(8 if lt_dma else 6, i), cols("td", (lt0 + 1) * Q + i, (lt0 + 5) * Q, 16)) for i in range(16)]]
+        if le_dma or not OPT["LE_FIRST"]:
+            sums.reverse()
+        for m in range(4):
+            mms(pn, sums[m // 2][8 * (m % 2):8 * (m % 2) + 8], m == 0, m == 3)
+        tt(ref("key", S_[:, :, h, :]), ref("kb%d" % p, S_[:, :, h, :]), pn, AL.add)
+
+    def lookup(x, rows, at, more=()):
+        phase[0] += "+"
+        cp(ref("off"), x)
+        act(ref("gg"), gath(cols("wc", 0, CW), ref("off")))
         for n, j in enumerate(rows):
-            for i in range(16):
-                mm(cols("pc", 192 + n * 48, 240 + n * 48), selv(j, i), cols("gg", i, 768, 16), i == 0, i == 15)
-
-    def step(out, x, at, size, scalar):
-        if scalar:
-            act(out, x, 0.5 - at, 1.0, "Sign")
-            act(out, out, 0.0, size, "Relu")
-        else:
-            ts(out, x, at, size, AL.is_ge, AL.mult)
+            terms = [(selv(j, i), cols("gg", i, 768, 16)) for i in range(16)] + [(ref("m1"), y) for y in more]
+            mms(cols("pc", at + n * 48, at + 48 + n * 48), terms, True, True)
 
     def control(t):
         p = t % 2
-        sf = "sf%d" % p
-        nine = 9.0 * 16384
+        sf, vv = "sf%d" % p, "vv%d" % p
+        phase[0] = "vote%d" % t
+        nine = 9.0 * 32768
         rp = ref("rn", S_[:, :, p, :])
+        side = "pk0" if t == 2 else "pc"
         tt(ref("mx"), ref("key", S_[:, 0:2]), ref("key", S_[:, 2:4]), AL.max)
         tt(ref("best"), ref("mx", S_[:, 0]), ref("mx", S_[:, 1]), AL.max)
-        c = cols("hh", 0, 48)
-        sc = SC[t]
-        if sc:
-            down(ref("tc"), ref("best"), 4096.0)
-            tt(c, ref("best"), ref("tc"), AL.subtract)
-            lookup(c, None, [4], sc)
-        else:
-            cp(ref("bi"), ref("best"))
-            ts(ref("ci"), ref("bi"), 4095, None, AL.bitwise_and)
-            lookup(ref("ci"), None, [4], sc)
-            cp(c, ref("ci"))
+        cp(ref("bi"), ref("best"))
+        ts(ref("ci"), ref("bi"), 8191, None, AL.bitwise_and)
+        lookup(ref("ci"), [4], 192)
         act(ref("fall"), ref("key"), nine - 0.5, -1.0, "Sign")
-        act(ref("fall"), ref("fall"), func="Relu")
-        step(ref("some"), ref("best"), nine, 4.0, True)
-        step(ref("fc"), c, 1536.0, 1536.0, True)
-        tt(ref("cr"), c, rp, AL.subtract)
-        tt(cols("hh", 48, 96), ref("fc"), cols("pc", 192, 240), AL.max)
-        lookup(cols("hh", 48, 96), None, [4], sc)
-        step(ref("fc"), cols("hh", 48, 96), 1536.0, 1536.0, True)
-        tt(cols("hh", 96, 144), ref("fc"), cols("pc", 192, 240), AL.max)
-        tt(ref("eq"), ref("hh"), ref("vv%d" % p), AL.is_equal)
+        act(ref("some"), ref("best"), 0.5 - nine, 1.0, "Sign")
+        tt(cols("eq", 0, 48), ref("ci"), cols(vv, 0, 48), AL.is_equal)
+        tt(ref("cr"), ref("ci"), rp, AL.subtract)
+        lookup(cols("pc", 192, 240), [4], 240)
+        tt(cols("eq", 48, 144), ref(vv), cols("pc", 192, 288), AL.is_equal)
         pv = cols("pc", 432, 480)
-        mm(pv, ref("m1"), ref("some"), True, False)
-        for m in range(3):
-            mm(pv, ref("m1"), cols("eq", 48 * m, 48 * m + 48), False, m == 2)
-        act(ref("take"), pv, -4.0, 1.0, "Abs")
-        act(ref("take"), ref("take"), 1.0, -1.0, "Relu")
-        step(ref("veto"), pv, 5.0, 1.0, True)
+        mms(pv, [(ref("m1"), ref("some"))] + [(ref("n1"), cols("eq", 48 * m, 48 * m + 48)) for m in range(3)], True, True)
+        act(ref("take"), pv, func="Relu")
         tt(ref("cr"), ref("cr"), ref("take"), AL.mult)
         tt(ref("ww"), ref("cr"), rp, AL.add)
-        step(ref("g1"), ref("ww"), 1536.0, 24.0, t < 2)
-        step(ref("g2"), ref("ww"), 2688.0, 18.0, t < 2)
-        tt(ref("gb"), ref("g1"), ref("g2"), AL.add)
-        lookup(ref("ww"), ref("gb"), [0, 1, 2, 3], sc)
+        step(ref("g1"), ref("ww"), CR, RK)
+        step(ref("g2"), ref("ww"), CG, GR - RK)
+        lookup(ref("ww"), [0, 1, 2, 3], 192, (ref("g1"), ref("g2")))
         act(rp, ref("ww"))
-        act(ref("thr"), ref("gb"), -24.0, 1.0, "Abs")
-        act(ref("thr"), ref("thr"), 1152.0, -1152.0, "Relu")
-        tt(ref("bv"), ref("best"), ref("veto"), AL.mult)
+        u, nw = cols(side, 0, 192), cols("pc", 192, 384)
         for j in range(4):
-            act(cols("pc", 48 * j, 48 * j + 48), ref("bv"))
-            act(ref("rb", S_[:, j]), ref("gb"), 0.0, 64.0)
-            act(ref("rth", S_[:, j]), ref("thr"), 3840.0, -1.0)
-        u, nw = cols("pc", 0, 192), cols("pc", 192, 384)
+            mms(cols(side, 48 * j, 48 * j + 48), [(ref("f1"), ref("best")), (ref("mb"), ref("take"))], True, True)
         tt(u, ref("key"), u, AL.is_equal)
         tt(ref("fall"), ref("fall"), u, AL.max)
-        tt(nw, ref("rb"), nw, AL.add)
-        tt(u, nw, ref("rth"), AL.is_lt)
-        tt(ref("ok"), u, ref("fall"), AL.mult)
+        for j in range(4):
+            mms(cols(side, 48 * j, 48 * j + 48), [(ref("m20"), cols("cst", 0, 48)), (ref("mq"), ref("g1")), (ref("m1"), ref("g2"))],
+                True, True)
+        tt(ref("fall"), ref("fall"), u, AL.mult)
+        tt(ref("ok"), ref("fall"), nw, AL.is_gt)
         tt(nw, nw, ref(sf), AL.subtract)
-        tt(nw, nw, ref("ok"), AL.mult)
+        tt(nw, ref("ok"), nw, AL.mult)
         tt(ref(sf), ref(sf), nw, AL.add)
         cp(ref("su%d" % p), ref(sf))
         if t < 2:
-            parts(p)
+            done[1] = parts(p)
             names(t + 1)
+        if t == 0:
+            keybase(2)
 
     def last(a, n):
         h, p = a // 2, a % 2
-        c0, c1 = a * Q, a * Q + Q
-        lo, hi = "lo%d" % (n % 2), "hi%d" % (n % 2)
-        ps = cols("pm%d" % (n % 2), 0, Q)
-        mm(ps, ref("fh"), cols("wh3", c0, c1), True, False)
-        sb = ("pl0", "pl1", "pk0", "pk1")
-        own = ref(("k2", "kk", "bb", "a1")[n])
-        dma("sync", own, cols("wl3", c0, c1), "o%d" % n)
-        for j in range(4):
-            o = cols("su%d" % p, j * 48 + h * 24, j * 48 + h * 24 + 24)
-            z, d = cols(lo, j * Q, j * Q + Q), cols(hi, j * Q, j * Q + Q)
-            tt(z, gath(ref("wl3"), o), own, AL.subtract)
-            if j < XA:
-                act(d, gath(ref("wh3"), o))
-                act(cols(sb[j], 0, Q), z, func="Sigmoid")
+        phase[0] = "sum%d" % n
+        kinds = OPT["ROWS"][n]
+        nz = kinds.count("Z")
+
+        def zt(j, m=1):
+            return blk("lo%d" % n, j, m) if n < 2 else win(2, n - 2, 3 + j, m)
+
+        def dt(j):
+            return blk("hi%d" % n, j) if n < 2 else win(1, n - 2, 3 + j, 1)
+
+        ps = cols(("pm0", "pm1", "pa", "pk1")[n], 0, Q)
+        if n < OPT["OWN_ACT"]:
+            mm(ps, ref("m1"), ref("cst"), True, False)
+            act(ps, win(3, 1, a, 1), 0.0, 4.0)
+        else:
+            mm(ps, ref("f4"), win(3, 1, a, 1), True, False)
+        sb = ("pl0", "pl1", "pl0", "pl1")
+        one = win(2, n, 7, 1) if n < 2 else win(0, n - 2, 5, 1)
+        for m in range(max(nz, 1)):
+            dma("sync", win(2, n, 7 + m, 1) if n < 2 else win(0, n - 2, 5 + m, 1), win(3, 0, a, 1), "p%d" % n)
+
+        def offs(j):
+            return cols("su%d" % p, j * 48 + h * 24, j * 48 + h * 24 + 24)
+
+        if nz:
+            assert kinds[:nz] == "Z" * nz
+            for j in range(nz):
+                act(zt(j), gath(win(3, 0), offs(j)), 0.0, -1.0)
+            src = win(2, n, 7, nz) if n < 2 else win(0, n - 2, 5, nz)
+            dma("g", zt(0, nz), src, "r%d" % n, True)
+            act(zt(0, nz), zt(0, nz), 0.0, -8.0, "Sigmoid")
+        rows = list(range(nz, 4)) + list(range(nz))
+        direct = n == 3 and kinds[rows[3]] == "Y"
+        for m, j in enumerate(rows):
+            z, d = zt(j), dt(j)
+            end = direct and m == 3
+            if kinds[j] != "Z":
+                tt(z, gath(win(3, 0), offs(j)), one, AL.subtract)
+            if kinds[j] == "Y":
+                act(d, gath(win(3, 1), offs(j)), 0.0, 8.0 if end else 1.0)
+                act(cols(sb[j], 0, Q), z, 0.0, 8.0, "Sigmoid")
                 tt(d, d, cols(sb[j], 0, Q), AL.mult)
             else:
-                act(z, z, func="Sigmoid")
-                tt(d, gath(ref("wh3"), o), z, AL.mult)
-            if j < 3 or n < 3:
-                mm(ps, ref("f1"), d, False, j == (3 if n < 3 else 2))
-        y = cols(lo, 4 * Q, 5 * Q)
-        if n < 3:
-            act(y, ps)
-        else:
+                if kinds[j] == "X":
+                    act(z, z, 0.0, 8.0, "Sigmoid")
+                tt(d, gath(win(3, 1), offs(j)), z, AL.mult)
+            if not end:
+                mm(ps, ref("f8"), d, False, m == (2 if direct else 3))
+        y = blk("hi%d" % (n % 2), 4)
+        if direct:
             tt(y, d, ps, AL.add)
-        dma("sync", cols("yq", c0, c1), y, "q%d" % n)
+        else:
+            act(y, ps)
+        dma("sync", blk("yq", a), y, "q%d" % n)
 
     for t in range(3):
         for h in range(2):
@@ -548,8 +710,14 @@ def build():
         poll(t, 0)
         poll(t, 1)
         control(t)
-    act(ref("r2"), ref("rn"))
-    mm(ref("pc", S_[0:96, 0:128]), ref("r2"), ref("f1"), True, True)
+    phase[0] = "refs"
+    act(cols("s1", 0, 96), ref("rn"), 192.0 - 0.495, 1.0 / 96)
+    act(ref("r2"), ref("rn"), 0.0, 16.0)
+    act(cols("dn", 0, 96), cols("s1", 0, 96), 192.0 * 1535, -1535.0)
+    step(cols("dn", 96, 192), ref("rn"), CR, RK - CR // 96)
+    step(cols("dd", 0, 96), ref("rn"), CG, GR - RK - CR // 96)
+    for m, x in enumerate((ref("r2"), cols("dn", 0, 96), cols("dn", 96, 192), cols("dd", 0, 96))):
+        mm(ref("pc", S_[0:96, 0:128]), x, ref("f1"), m == 0, m == 3)
     act(ref("rt", S_[0:96, :]), ref("pc", S_[0:96, 0:128]))
     for k in range(8):
         dma("sync", ref("yr", S_[k, :]), ref("rt", S_[0:96, 16 * k:16 * k + 16]), "out")
@@ -587,11 +755,10 @@ def plan():
                 if _where(r["n"]) == "psum":
                     if o["e"] == "pe":
                         h[:] = []
-
                 elif wr and s[5] == s[1] - s[0] + 1 and s[4] == s[3] - s[2] + 1:
                     h[:] = [e for e in h if e[0] == k or not (s[0] <= e[1][0] and e[1][1] <= s[1] and s[2] <= e[1][2] and e[1][3] <= s[3])]
                 h.append((k, s, wr))
-        o["d"] = dep
+        o["d"] = dep | set(o["after"])
         if o["g"] is not None:
             groups.setdefault(o["g"], []).append(k)
     for k, o in enumerate(ops):
@@ -622,12 +789,15 @@ def plan():
         pr[k] = ops[k]["c"] + ops[k]["lat"] + max([pr[s] + 80 for s in succ[k]] + [0.0])
     eng = [o["e"] for o in ops]
     cost = [o["c"] for o in ops]
+    moved = [o["by"] for o in ops]
 
     def lag(m, s):
         early = ops[m]["k"] == "send" and m in ops[s]["x"]
-        return (0.0 if early else ops[m]["lat"]) + (0.0 if eng[m] == eng[s] == "pe" else 80.0)
+        return (0.0 if early else ops[m]["lat"]) + (0.0 if eng[m] == eng[s] == "pe" else P["LAG"])
 
-    fw = [[(s, lag(k, s)) for s in succ[k]] for k in range(n)]
+    pad = [P["PAD"][0] + P["PAD"][1] * o["by"] if o["k"] == "dma" else (P["PAD"][2] if o["k"] == "arrive" else 0.0) for o in ops]
+    fw = [[(s, lag(k, s) + pad[k]) for s in succ[k]] for k in range(n)]
+    bk = [[(m, lag(m, k) + pad[m]) for m in ops[k]["all"]] for k in range(n)]
     bw = [[(m, lag(m, k)) for m in ops[k]["all"]] for k in range(n)]
 
     def sched(pr, nxt, first, look):
@@ -641,7 +811,7 @@ def plan():
         for k in range(n):
             if left[k] == 0:
                 ready.setdefault(eng[k], []).append(k)
-        seq = []
+        seq, line = [], 0.0
         while len(seq) < n:
             best = None
             for e, lst in ready.items():
@@ -653,61 +823,141 @@ def plan():
             k = max([k for k in ready[e] if at[k] <= t0 + look], key=lambda k: pr[k])
             ready[e].remove(k)
             start[k] = max(t0, at[k])
-            free[e] = start[k] + cost[k]
+            free[e] = end = start[k] + cost[k]
+            if moved[k] and nxt is fw:
+                end = max(end, line)
+                line = end + moved[k] * (1.0 + P["PAD"][1])
             seq.append(k)
             for s, d in nxt[k]:
-                if free[e] + d > at[s]:
-                    at[s] = free[e] + d
+                if end + d > at[s]:
+                    at[s] = end + d
                 left[s] -= 1
                 if left[s] == 0:
                     ready.setdefault(eng[s], []).append(s)
         return seq, start
 
     alts = []
-    for gat, net, pe in ((1.0, 1.0, 0.94), (1.3, 1.0, 1.0), (0.75, 0.6, 1.0), (1.0, 1.5, 0.94), (1.0, 0.7, 1.07)):
-        c = list(cost)
+    for gat, net, pe, slow, late, share, work in P["ALTS"]:
+        c, mv, more = list(cost), list(moved), [0.0] * n
         for k, o in enumerate(ops):
             if o["k"] == "arrive":
                 c[k] *= net
-            elif o["k"] == "mm":
-                c[k] *= pe
-            elif any(r["ind"] is not None for r in o["r"]):
-                c[k] *= gat
-        alts.append(c)
+            elif o["k"] == "send":
+                mv[k] *= share * net / P["OCC"]
+            elif o["k"] == "dma":
+                mv[k] *= slow
+                more[k] = late + mv[k] - moved[k]
+            else:
+                c[k] *= work * (pe if o["e"] == "pe" else (gat if any(r["ind"] is not None for r in o["r"]) else 1.0))
+        alts.append((c, mv, more, work))
+
+    names = sorted(set(eng))
+    en = [names.index(e) for e in eng]
+
+    def timed(seq, alt):
+        c, mv, more, work = alt
+        free, prev, end, held, line = [0.0] * len(names), [-1] * len(names), [0.0] * n, [-1] * n, []
+        for k in seq:
+            e = en[k]
+            t0, by = free[e], prev[e]
+            for m, d in bw[k]:
+                if end[m] + d > t0:
+                    t0, by = end[m] + d, m
+            held[k], prev[e] = by, k
+            free[e] = end[k] = t0 = t0 + c[k]
+            if mv[k]:
+                at = len(line)
+                while at and line[at - 1][1] > t0:
+                    at -= 1
+                while at < len(line) and line[at][0] < t0 + mv[k]:
+                    t0 = max(t0, line[at][1])
+                    at += 1
+                line.insert(at, (t0, t0 + mv[k]))
+                end[k] = t0 + more[k]
+        return end, held
 
     def score(seq):
-        tot = 0.0
-        for c in alts:
-            free, end = {}, [0.0] * n
-            for k in seq:
-                t0 = free.get(eng[k], 0.0)
-                for m, d in bw[k]:
-                    if end[m] + d > t0:
-                        t0 = end[m] + d
-                free[eng[k]] = end[k] = t0 + c[k]
-            tot += max(end)
-        return tot / len(alts)
+        tot = [max(timed(seq, alt)[0]) / alt[3] for alt in alts]
+        _CACHE["ends"] = tot
+        return sum(tot) / len(alts)
+
+    def polish(seq, rounds):
+        now = score(seq)
+        best = (now, seq)
+        for it in range(rounds):
+            if it % 8 == 0:
+                end, held = timed(seq, alts[int(rng.integers(len(alts)))])
+                k, chain = max(range(n), key=lambda x: end[x]), []
+                while k >= 0:
+                    m = held[k]
+                    if m >= 0 and en[m] == en[k] and m not in needs[k]:
+                        chain.append(k)
+                    k = m
+                pos = [0] * n
+                for i, k in enumerate(seq):
+                    pos[k] = i
+            v = chain[int(rng.integers(len(chain)))]
+            hop, i = int(rng.geometric(0.4)), pos[v]
+            while hop and i > 0:
+                i -= 1
+                if en[seq[i]] == en[v]:
+                    hop -= 1
+            take, todo = {v}, [v]
+            while todo:
+                for m in needs[todo.pop()]:
+                    if pos[m] >= i and m not in take:
+                        take.add(m)
+                        todo.append(m)
+            if seq[i] in take or len(take) > 12:
+                continue
+            mid = seq[i:pos[v] + 1]
+            new = seq[:i] + [k for k in mid if k in take] + [k for k in mid if k not in take] + seq[pos[v] + 1:]
+            sc = score(new)
+            if sc < now + P["TEMP"] * (1.0 - it / rounds) * rng.random():
+                seq, now = new, sc
+                for j in range(i, pos[v] + 1):
+                    pos[seq[j]] = j
+                if now < best[0]:
+                    best = (now, seq)
+        return best[1]
+
+    needs = [set(o["all"]) for o in ops]
 
     rng = np.random.default_rng(P["SEED"])
     zero = [0.0] * n
     tail = [o["lat"] for o in ops]
+    pr = [x + P["SOON"].get(o["t"], 0.0) for x, o in zip(pr, ops)]
     seq, start = sched(pr, fw, zero, 30)
-    best = (score(seq), seq, start)
+    best = (score(seq), seq, start, pr, 30)
     cur = best
     for it in range(P["ITER"]):
         amp = (50.0, 300.0, 1000.0)[it % 3]
         look = (30, 150, 300)[(it // 3) % 3]
         back = [cur[2][k] + cost[k] + x for k, x in enumerate(amp * rng.random(n))]
-        s2, st2 = sched(back, bw, tail, look)
-        fore = [st2[k] + cost[k] + x for k, x in enumerate(amp * rng.random(n))]
+        s2, st2 = sched(back, bk, tail, look)
+        fore = [st2[k] + cost[k] + x + P["SOON"].get(ops[k]["t"], 0.0) for k, x in enumerate(amp * rng.random(n))]
         seq, start = sched(fore, fw, zero, look)
         sc = score(seq)
         if sc < cur[0] + 400.0:
-            cur = (sc, seq, start)
+            cur = (sc, seq, start, fore, look)
         if sc < best[0]:
             best = cur
-    seq, start = best[1], best[2]
+    tags = sorted(set(o["t"] for o in ops))
+    for it in range(P["MOVES"]):
+        tag = tags[int(rng.integers(len(tags)))]
+        by = float(rng.choice([-1.0, 1.0]) * rng.choice([200.0, 500.0, 1200.0, 3000.0]))
+        look = best[4] if rng.random() < 0.8 else int(rng.choice([30, 150, 300, 600]))
+        who = (None, "act", "dve", "pe", "g")[int(rng.integers(5))]
+        fore = [x + by if o["t"] == tag and who in (None, o["e"]) else x for x, o in zip(best[3], ops)]
+        seq, start = sched(fore, fw, zero, look)
+        sc = score(seq)
+        if sc < best[0]:
+            best = (sc, seq, start, fore, look)
+    seq = _CACHE["fix"] if "fix" in _CACHE else polish(best[1], P["POLISH"])
+    end = timed(seq, alts[0])[0]
+    start = [end[k] - cost[k] for k in range(n)]
     fin = [start[k] + cost[k] + tail[k] for k in range(n)]
+    _CACHE["score"] = score(seq)
     _CACHE["plan"] = (ops, seq, groups, start, fin)
     return _CACHE["plan"]
 
@@ -736,7 +986,7 @@ def rank_program(g, core, T, topo):
             if helper(src, dst) == core:
                 spare = [x for x in topo.engines(src, core) if x not in topo.engines(src, dst)]
                 out = topo.engines(core, dst)
-                todo = [ops[k]["a"] for k in seq if ops[k]["k"] == "send" and ops[k]["a"][1] in VIA]
+                todo = [ops[k]["a"] for k in seq if ops[k]["k"] == "send" and ops[k]["a"][1] in OPT["VIA"]]
                 for pairs, grp in todo:
                     g.wait_ge(T.sem[gsem[grp]], len(spare))
                     fused(dst, out, [(T[d["n"]][d["i"]], T[d["n"]][d["i"]]) for s, d in pairs], gsem[grp], "sent")
@@ -760,8 +1010,7 @@ def rank_program(g, core, T, topo):
     def ap(r):
         a = T[r["n"]][r["i"]]
         if r["ind"] is not None:
-            w = T[r["n"]]
-            a = w[:, 0:w.shape[1]].indirect(ap(r["ind"]))
+            a = a.indirect(ap(r["ind"]))
         return a
 
     def val(s):
@@ -780,6 +1029,7 @@ def rank_program(g, core, T, topo):
             if e == "pe" and ops[m]["e"] == "pe":
                 continue
             s, v = mark[m]
+            assert s != "sent"
             if known[e].get(s, 0) < v:
                 need[s] = max(need.get(s, 0), v)
         for m in o["d"]:
@@ -810,7 +1060,7 @@ def rank_program(g, core, T, topo):
             loc = gsem[o["g"]] if o["g"] is not None else "sent"
             per = len(eng) // len(pairs)
             masks = [sum(1 << x for x in eng[m * per:(m + 1) * per]) for m in range(len(pairs))]
-            if grp in VIA and via is not None:
+            if grp in OPT["VIA"] and via is not None:
                 spare = [x for x in topo.engines(core, via) if x not in eng]
                 assert len(spare) == len(eng)
                 fused(via, spare, [(ap(s), ap(d)) for s, d in pairs], gsem[grp], loc)
@@ -840,6 +1090,9 @@ def rank_program(g, core, T, topo):
             ins = q.activation(ap(a[0]), ap(a[1]), f, bias=a[3], scale=a[4])
         elif kind == "mm":
             ins = q.matmul(ap(a[0]), ap(a[1]), ap(a[2]), a[3], a[4])
+        elif kind == "mms":
+            for c in a:
+                ins = q.matmul(ap(c[0]), ap(c[1]), ap(c[2]), c[3], c[4])
         else:
             if SCRATCH[a[0]["n"]][2] == "int32":
                 ins = q.iota(ap(a[0]), a[1], a[2], a[3])

import numpy as np
from concourse.bass import DstId, RemoteDMATransfer
from concourse.mybir import AluOpType, ActivationFunctionType

Q = 384
V = 1536
W = 3840
RK = 1536
GR = 2688
CR, CG, CW = 1536, 3072, 4608

OPT = {
    "KEY_ACT": (2, 4, 1, 4, 1, 4),
    "A_PE": (0, 2, 0, 2, 0, 2),
    "HL_DMA": (1, 1, 1, 1, 1, 1),
    "PL": (("pl0", "pl1", "pm0", "pm1", "pl0"), ("pl1", "pl0", "pl1", "pl0", "pl1")),
    "AFTER": (9, 9, 9),
    "LISTS": (99, 99),
    "LE_DMA": (2, 0, 2, 0, 2, 0),
    "LT_DMA": (0, 0, 0, 0, 0, 0),
    "MASK_DMA": (0, 0, 0, 0, 0, 0),
    "MASK_ACT": (5, 4, 5, 4, 5, 4),
    "OWN_ACT": 4,
    "ENDS": 0,
    "LE_FIRST": 0,
    "DVE_G": (4, 0, 0, 0, 0, 0),
    "ROWS": ("ZZXX", "ZZZX", "ZZXY", "XYYY"),
    "VIA": ("in0", "in3", "nm0", "nm1", "nm2", "xd21", "xw0", "xw2", "xz0"),
}
P = {"NET": 62.0, "NETLAT": 2200, "SEED": 1, "ITER": 6, "MOVES": 80, "POLISH": 8000, "TEMP": 20.0, "SOON": {},
     "OVH": 50.0, "LAG": 80.0, "PE": 0.43,
     "GDMA": 900.0, "DMA": 500.0, "OCC": 0.15, "NEAR": 120.0, "DLAT": 1900.0, "ACC": 2.0, "PAD": (150.0, 0.15, 150.0),
     "ALTS": ((1.0, 1.0, 1.0, 1.0, 0.0, 0.1, 1.0), (1.2, 1.0, 1.0, 1.0, 0.0, 0.1, 1.25), (0.8, 1.2, 1.0, 1.2, 400.0, 0.25, 1.0))}

SCRATCH = {}
for _t in range(4):
    SCRATCH["w%d" % _t] = ("sbuf", [128, 2, W], "float32")
for _t in range(2):
    SCRATCH["lo%d" % _t] = ("sbuf", [128, 4 * Q], "float32")
    SCRATCH["hi%d" % _t] = ("sbuf", [128, 5 * Q], "float32")
    SCRATCH["sf%d" % _t] = ("sbuf", [128, 4, 2, 24], "float32")
    SCRATCH["su%d" % _t] = ("sbuf", [128, 192], "uint16")
    SCRATCH["vv%d" % _t] = ("sbuf", [128, 96], "float32")
    SCRATCH["kb%d" % _t] = ("sbuf", [128, 4, 2, 24], "float32")
    SCRATCH["s%d" % (_t + 1)] = ("sbuf", [128, 192], "bfloat16")
for _t in range(3):
    SCRATCH["land%d" % _t] = ("sbuf", [128, 768], "bfloat16")
for _n in ("pl0", "pl1", "pk0", "pk1", "pa", "pm0", "pm1", "pc"):
    SCRATCH[_n] = ("psum", [128, 512], "float32")
SCRATCH.update({
    "td": ("sbuf", [128, 18 * Q], "bfloat16"), "fb": ("sbuf", [128, 2, GR], "bfloat16"),
    "cmp": ("sbuf", [128, 25 * Q], "bfloat16"),
    "k2": ("sbuf", [128, Q], "float32"), "kk": ("sbuf", [128, Q], "float32"), "a0": ("sbuf", [128, Q], "float32"),
    "rr": ("sbuf", [128, Q], "bfloat16"), "a1": ("sbuf", [128, Q], "float32"), "cst": ("sbuf", [128, Q], "bfloat16"),
    "wc": ("sbuf", [128, CW], "bfloat16"), "gg": ("sbuf", [128, 768], "bfloat16"),
    "sli": ("sbuf", [128, 2, 2, 4, 24], "int32"), "rfi": ("sbuf", [128, 2, 2, 24], "int32"),
    "rn": ("sbuf", [128, 2, 2, 24], "float32"), "r2": ("sbuf", [128, 96], "float32"), "rt": ("sbuf", [128, 128], "float32"),
    "pp": ("sbuf", [128, 10, 2, 2, 24], "bfloat16"),
    "g1": ("sbuf", [128, 48], "bfloat16"), "g2": ("sbuf", [128, 48], "bfloat16"),
    "dd": ("sbuf", [128, 144], "float32"), "mh": ("sbuf", [128, 144], "bfloat16"), "mn": ("sbuf", [128, 144], "bfloat16"),
    "m1": ("sbuf", [128, 128], "bfloat16"), "n1": ("sbuf", [128, 128], "bfloat16"), "nh": ("sbuf", [128, 128], "bfloat16"),
    "f1": ("sbuf", [128, 128], "float32"), "f4": ("sbuf", [128, 128], "float32"), "f8": ("sbuf", [128, 128], "float32"),
    "f96": ("sbuf", [128, 128], "float32"), "fm": ("sbuf", [128, 128], "float32"),
    "sel": ("sbuf", [128, 9 * 144], "bfloat16"),
    "a8": ("sbuf", [128, 8], "float32"), "b8": ("sbuf", [128, 8], "int32"), "c8": ("sbuf", [128, 8], "int32"),
    "pi": ("sbuf", [128, 4], "int32"), "pj": ("sbuf", [128, 4], "int32"), "pf": ("sbuf", [128, 4], "float32"),
    "v0": ("sbuf", [128, 96], "float32"),
    "dn": ("sbuf", [128, 192], "float32"), "key": ("sbuf", [128, 4, 2, 24], "float32"),
    "fall": ("sbuf", [128, 4, 2, 24], "float32"), "ok": ("sbuf", [128, 4, 2, 24], "float32"),
    "mx": ("sbuf", [128, 2, 2, 24], "float32"), "best": ("sbuf", [128, 2, 24], "float32"), "bi": ("sbuf", [128, 48], "int32"),
    "ci": ("sbuf", [128, 48], "int32"), "eq": ("sbuf", [128, 144], "bfloat16"),
    "off": ("sbuf", [128, 48], "uint16"), "cr": ("sbuf", [128, 48], "float32"), "ww": ("sbuf", [128, 48], "float32"),
    "some": ("sbuf", [128, 48], "bfloat16"), "take": ("sbuf", [128, 48], "bfloat16"), "p8": ("sbuf", [128, 4], "float32"),
})
for _n in ("mb", "m20", "mq"):
    SCRATCH[_n] = ("sbuf", [128, 128], "bfloat16")
SEMAPHORES = ["pe", "act", "dve", "pool", "sent"] + ["s%d" % _k for _k in range(145)]

IO = {"th": [128, V], "dl": [128, V], "dr": [128, V], "sl": [128, 384], "rf": [128, 96],
      "yt": [128, V], "yq": [128, V], "yr": [8, V]}
AL = AluOpType
AF = ActivationFunctionType
S_ = np.s_
_CACHE = {}


def _where(n):
    return SCRATCH[n][0] if n in SCRATCH else "dram"


def _bytes(n):
    return 2 if n in SCRATCH and SCRATCH[n][2] in ("bfloat16", "uint16") else (2 if n in ("th", "dl", "dr") else 4)


def ref(name, idx=None):
    shape = SCRATCH[name][1] if name in SCRATCH else IO[name]
    if idx is None:
        idx = S_[:]
    key = (name, repr(idx))
    if key not in _CACHE:
        free = int(np.prod(shape[1:]))
        tup = idx if isinstance(idx, tuple) else (idx,)
        p = np.atleast_1d(np.arange(shape[0])[tup[0]])
        c = np.arange(free).reshape(shape[1:])[tup[1:]]
        c = np.atleast_1d(c)
        _CACHE[key] = (int(p.min()), int(p.max()), int(c.min()), int(c.max()), int(c.size), int(p.size))
    return {"n": name, "i": idx, "s": _CACHE[key], "ind": None}


def cols(name, a, b, step=1):
    return ref(name, S_[:, a:b] if step == 1 else S_[:, a:b:step])


def win(t, s, a=0, n=10, rows=S_[:]):
    return ref("w%d" % t, (rows, s, slice(a * Q, (a + n) * Q)))


def both(name, a):
    r = dict(ref(name, S_[:, :, a * Q:a * Q + Q]))
    r["sub"] = [ref(name, S_[:, s, a * Q:a * Q + Q]) for s in range(2)]
    return r


def blk(name, a, n=1):
    return cols(name, a * Q, (a + n) * Q)


def gath(view, offs):
    r = dict(view)
    r["ind"] = offs
    return r


def build():
    ops = []
    phase = ["start"]

    def add(eng, kind, args, reads, writes, cost, lat=0.0, grp=None):
        rd, wr = [], []
        for r in reads:
            rd.extend(r.get("sub", [r]))
            if r["ind"] is not None:
                rd.append(r["ind"])
        for r in writes:
            wr.extend(r.get("sub", [r]))
        ops.append({"e": eng, "k": kind, "a": args, "r": rd, "w": wr, "c": cost, "lat": lat, "g": grp, "x": [], "by": 0.0,
                    "t": phase[0], "after": []})
        return len(ops) - 1

    def nel(out):
        return out["s"][4]

    def vcost(out, ins, two=False):
        n = nel(out)
        if any(r["ind"] is not None for r in ins):
            return P["OVH"] + 1.3 * n
        k = 2.0 if two and all(_where(r["n"]) == "sbuf" for r in ins) else 1.0
        if not two and all(_bytes(r["n"]) == 2 for r in ins + [out]):
            k = 0.5
        return P["OVH"] + 0.83 * max(k * n, 64)

    def tt(out, a, b, op):
        return add("dve", "tt", (out, a, b, op), [a, b], [out], vcost(out, [a, b], True))

    def ts(out, a, s1, s2, op0, op1=None):
        rd = [a] + [s for s in (s1, s2) if isinstance(s, dict)]
        return add("dve", "ts", (out, a, s1, s2, op0, op1), rd, [out], vcost(out, [a]))

    def cp(out, a):
        return add("dve", "cp", (out, a), [a], [out], vcost(out, [a]))

    def ms(out, val):
        return add("dve", "ms", (out, val), [], [out], 55 + 0.42 * nel(out))

    def act(out, a, bias=0.0, scale=1.0, func="Identity"):
        n = nel(out)
        c = P["OVH"] + 15 + (1.3 * n if a["ind"] is not None else 0.83 * max(n, 64))
        return add("act", "act", (out, a, func, bias, scale), [a], [out], c)

    def mm(out, lhs, rhs, start, stop):
        k = 4 if _bytes(rhs["n"]) == 4 else 1
        return add("pe", "mm", (out, lhs, rhs, start, stop), [lhs, rhs], [out], 10 + P["PE"] * k * max(64, nel(rhs)))

    def mms(out, terms, start, stop):
        calls = [(out, w, y, start and m == 0, stop and m == len(terms) - 1) for m, (w, y) in enumerate(terms)]
        c = sum(10 + P["PE"] * (4 if _bytes(y["n"]) == 4 else 1) * max(64, nel(y)) for w, y in terms)
        seen = {}
        for w, y in terms:
            for r in (w, y):
                seen.setdefault((r["n"], r["s"][2] // 192, r["s"][3] // 192), r)
        wide = [cols(r["n"], a * 192, min(b * 192 + 192, SCRATCH[r["n"]][1][1])) if len(SCRATCH[r["n"]][1]) == 2 else ref(r["n"])
                for (nm, a, b), r in seen.items()]
        return add("pe", "mms", calls, wide, [out], c)

    def iota(out, pat, base, cm):
        return add("g", "iota", (out, pat, base, cm), [], [out], 130 + 1.7 * nel(out))

    def dma(q, out, a, grp, accum=False):
        ns = nel(out) * out["s"][5] * _bytes(out["n"]) * (P["ACC"] if accum else 1) / P["DMA"]
        rd = [a, out] if accum else [a]
        k = add(q, "dma", (out, a, accum), rd, [out], P["GDMA"] if q == "g" else 80, P["DLAT"] + ns, grp)
        ops[k]["by"] = ns
        return k

    def send(pairs, grp, own=None, after=()):
        by = sum(nel(s) * 128 * _bytes(s["n"]) for s, d in pairs)
        k = add("g", "send", (pairs, grp), [s for s, d in pairs] + list(after), [], 300, 1500 + by / P["NET"], own)
        by2 = grp in OPT["VIA"]
        ops[k]["by"] = P["OCC"] * by / (P["NEAR"] if by2 else P["NET"])
        a = add("net2" if by2 else "net", "arrive", (len(pairs),), [], [d for s, d in pairs], by / P["NET"],
                P["NETLAT"] + (3200 if by2 else 0), grp)
        ops[a]["x"].append(k)
        return k

    dma("sync", blk("td", 0), blk("th", 0), "ld0")
    dma("act", blk("td", 7), blk("dl", 0), "ld0")
    dma("sync", blk("td", 1, 2), blk("th", 1, 2), "ld5")
    dma("act", blk("td", 8, 2), blk("dl", 1, 2), "ld5")
    dma("sync", ref("sli"), ref("sl"), "ld1")
    dma("sync", ref("rfi"), ref("rf"), "ld4")
    iota(ref("dd"), [[-1, 144]], 0, 1)
    iota(ref("a8"), [[-16, 8]], 0, 1)
    iota(ref("pi"), [[0, 4]], 0, 1)
    iota(ref("v0"), [[0, 2], [48, 2], [1, 24]], 0, 0)
    first = [send([(blk("td", a), blk("td", 4 + a)), (blk("td", 7 + a), blk("td", 11 + a))], "in%d" % a, "io%d" % a)
             for a in range(3)]
    for k in (dma("sync", blk("td", 3), blk("th", 3), "ld2"), dma("sync", blk("td", 10), blk("dl", 3), "ld2"),
              dma("sync", ref("fb", S_[:, 0, 0:V]), ref("dr"), "ld3")):
        ops[k]["after"].append(first[0])
    for n, s in (("mh", 1.0 / 16), ("mn", -1.0 / 16)):
        ts(cols(n, 0, 128), cols("dd", 0, 128), 0.0, s, AL.is_equal, AL.mult)
        ts(cols(n, 128, 144), cols("dd", 128, 144), -128.0, s, AL.is_equal, AL.mult)
    ts(ref("f1"), cols("dd", 0, 128), 0.0, None, AL.is_equal)
    for n, s in (("m1", 1.0), ("n1", -1.0), ("nh", -0.5), ("f4", 4.0), ("f8", 8.0), ("f96", 96.0), ("fm", -1535.0 / 16),
                 ("mb", 2.0 ** 21), ("m20", 20.0), ("mq", -0.75)):
        act(ref(n), ref("f1"), 0.0, s)
    ms(ref("cst"), 192.0)
    ms(ref("sel"), 0.0)
    ts(ref("b8"), ref("a8"), 0.5, -0.25, AL.mult, AL.add)
    ts(ref("c8"), ref("a8"), 0.0625, -0.46875, AL.mult, AL.add)
    for j in range(5):
        ts(cols("sel", j * 144 + 15, j * 144 + 143, 16), ref("b8"), float(j), None, AL.is_equal)
    for j, s in ((5, 32768.0), (6, -32768.0), (7, 16384.0), (8, -16384.0)):
        ts(cols("sel", j * 144 + 15, j * 144 + 143, 16), ref("c8"), 0.0, s, AL.is_equal, AL.mult)
    ts(ref("pj"), ref("pi"), 15, None, AL.bitwise_and)
    ts(ref("pf"), ref("pj"), 96.0, None, AL.mult)
    ts(ref("p8"), ref("pj"), 8.0, float(CR), AL.is_equal, AL.mult)
    for k in range(4):
        ts(blk("wc", 3 * k, 3), blk("td", 0, 3), 0.0, cols("p8", 0, 1), AL.mult, AL.add)
    for p in range(2):
        ts(ref("vv%d" % p), ref("v0"), cols("pf", 0, 1), 24.0 * p, AL.add, AL.add)

    def selv(j, i):
        return cols("sel", j * 144 + 15 - i, j * 144 + 143 - i)

    phase[0] = "lists"
    for p in range(2):
        for h in range(2):
            cp(ref("sf%d" % p, S_[:, :, h, :]), ref("sli", S_[:, h, p, :, :]))
        cp(ref("su%d" % p), ref("sf%d" % p))
    cp(ref("r2"), ref("rfi"))

    def step(out, x, at, size):
        act(out, x, 0.5 - at, 1.0, "Sign")
        act(out, out, 0.0, size, "Relu")

    def place(x, m):
        down, big = cols("dn", 0, m), 1.5 * 2.0 ** 27
        act(down, x, -7.5)
        act(down, down, big)
        act(down, down, -big)
        step(cols("s1", 0, m), x, RK, CR - RK // 16)
        step(cols("s2", 0, m), x, GR, CG - GR // 16 - CR + RK // 16)
        po = cols("pc", 0, m)
        mm(po, ref("f96"), x, True, False)
        mm(po, ref("fm"), down, False, False)
        mm(po, ref("m1"), cols("s1", 0, m), False, False)
        mm(po, ref("m1"), cols("s2", 0, m), False, True)

    def keybase(t):
        phase[0] = "base%d" % t
        place(ref("sf%d" % (t % 2)), 192)
        for j in range(4):
            for h in range(2):
                signs = min(OPT["LE_DMA"][2 * t + h], 1) - OPT["LT_DMA"][2 * t + h]
                act(ref("kb%d" % (t % 2), S_[:, j, h, :]), cols("pc", 48 * j + 24 * h, 48 * j + 24 * h + 24),
                    8192.0 * (3 - j) + 262144.0 * signs)

    place(ref("r2"), 96)
    act(ref("rn"), cols("pc", 0, 96))
    keybase(0)
    keybase(1)

    def parts(p):
        sf = "sf%d" % p
        act(ref("pp", S_[:, 8, :, p, :]), ref("rn", S_[:, :, p, :]))
        tt(ref("pp", S_[:, 9, :, p, :]), ref("rn", S_[:, :, p, :]), ref("pp", S_[:, 8, :, p, :]), AL.subtract)
        act(ref("pp", S_[:, 0:8:2, :, p, :]), ref(sf))
        return tt(ref("pp", S_[:, 1:8:2, :, p, :]), ref(sf), ref("pp", S_[:, 0:8:2, :, p, :]), AL.subtract)

    def names(t):
        phase[0] = "names%d" % t
        send([(ref("pp", S_[:, 0:8]), ref("land%d" % t))], "nm%d" % t, "no%d" % t)
        for k in range(10):
            dma("sync", ref("wc", S_[k::16, 0:V]), ref("pp", S_[:, k]), "wa%d" % t)
        for k in range(8):
            n = 16 * ((k + 1) % 8)
            dma("sync", ref("wc", S_[16 * k:16 * k + 8, CG:CG + V]), ref("wc", S_[n:n + 8, 0:V]), "wb%d" % t)
        for k in range(8):
            dma("sync", ref("wc", S_[k::16, CR:CR + V]), cols("land%d" % t, 96 * k, 96 * k + 96), "wc%d" % t)

    banks = ["pl0", "pl1", "pk0", "pk1", "pm0", "pm1", "pa"]
    nb = [0]

    def w0(dst, src, sh):
        for s, m2, f in ((0, "mn", cp), (1, "mh", act)):
            b = cols(banks[nb[0] % 7], 0, Q)
            nb[0] += 1
            mm(b, cols("mh", sh, sh + 128), blk("td", src), True, False)
            mm(b, cols(m2, sh, sh + 128), blk("td", 7 + src), False, True)
            f(win(0, s, dst, 1), b)

    phase[0] = "own"
    for a in range(3):
        w0(a, a, 0)
        w0(7 + a, a, 16)
    w0(3, 3, 0)
    phase[0] = "far"
    for a in range(3):
        w0(4 + a, 4 + a, 0)
    phase[0] = "parts"
    parts(0)
    parts(1)
    names(0)
    phase[0] = "drift"

    ts(ref("fb", S_[:, 0, 0:V]), ref("fb", S_[:, 0, 0:V]), 1.0 / 16, None, AL.mult)
    send([(ref("fb", S_[:, 0, 0:1152]), ref("fb", S_[:, 0, RK:GR]))], "in3", "io3", [blk("td", 13)])
    dma("sync", ref("fb", S_[:, 1, 0:V]), ref("fb", S_[:, 0, 0:V]), "fo")
    dma("sync", ref("fb", S_[:, 1, RK:GR]), ref("fb", S_[:, 0, RK:GR]), "ff")

    def share(t, views, tag, far=True):
        if far:
            send([(win(t, s, a, 1), win(t, s, 4 + a, 1)) for s, a in views], "x" + tag)
        for s, a in views:
            dma("sync", win(t, s, 7 + a, 1, S_[0:112]), win(t, s, a, 1, S_[16:128]), "y" + tag)
            dma("sync", win(t, s, 7 + a, 1, S_[112:128]), win(t, s, a, 1, S_[0:16]), "y" + tag)

    def drift(t, a):
        phase[0] = "drift%d%d" % (t, a)
        if t < 2:
            for b in ((a, 4 + a) if a < 3 else (a,)):
                dma("sync", both("w%d" % (t + 1), b), both("w%d" % t, b), "c%d_%d" % (t, b))
                dma("g", both("w%d" % (t + 1), b), both("fb", b), "d%d_%d" % (t, b), True)
            if a < 3:
                share(t + 1, [(0, a), (1, a)], "d%d%d" % (t, a), False)
        else:
            act(win(3, 0, a, 1), ref("fb", S_[:, 0, a * Q:a * Q + Q]), 0.0, 2.0)
            dma("g", win(3, 0, a, 1), win(2, 0, a, 1), "e%d" % a, True)
            dma("g", win(3, 0, a, 1), win(2, 1, a, 1), "f%d" % a, True)
            theta(a)
            if a < 3:
                share(3, [(0, a), (1, a)], "d%d%d" % (t, a))

    def theta(a):
        y = win(1, a // 2, 7 + a % 2, 1)
        act(y, win(3, 0, a, 1), 0.0, 8.0)
        dma("sync", blk("yt", a), y, "out")

    done = [None, None]

    def poll(t, h):
        p = t % 2
        a = 2 * h + p
        ck = 2 * t + h
        lo, hi = "lo%d" % h, "hi%d" % h
        c2 = t / 128.0
        eps = 2.0 ** -21
        hl_dma, le_dma, lt_dma, mask_dma = [OPT[n][ck] for n in ("HL_DMA", "LE_DMA", "LT_DMA", "MASK_DMA")]
        lt0, le0 = 5 * h, 10 + 4 * h
        ends = ck == 5 and OPT["ENDS"]
        assert not ends or (OPT["MASK_ACT"][ck] >= 4 and not (le_dma or lt_dma or mask_dma))

        def L(j):
            return blk(lo, j) if j < 4 else win(t, 0, a, 1)

        def H(j):
            return blk(hi, j + 1) if j < 4 else win(t, 1, a, 1)

        def LT(j):
            return blk("td", lt0 + (j + 1) % 5)

        phase[0] = "gather%d" % ck
        if lt_dma or hl_dma:
            dma("sync", blk(hi, 0), H(4), "o%d" % ck)
        ng = 0
        for j in ((3, 0, 1, 2) if hl_dma else range(4)):
            o = cols("su%d" % p, j * 48 + h * 24, j * 48 + h * 24 + 24)
            for dst, s, b in ((L(j), 0, -c2), (H(j), 1, 0.0)):
                if ng % 2 == 0 and ng // 2 < OPT["DVE_G"][ck]:
                    ts(dst, gath(win(t, s), o), b, None, AL.add)
                else:
                    act(dst, gath(win(t, s), o), b)
                ng += 1
        terms = {i: [] for i in range(5)}
        if hl_dma:
            phase[0] = "aside%d" % ck
            xt, x0 = (3, 0) if t == 0 else (0, 5)
            act(win(xt, h, x0, 1), L(3), 0.0, -1.0)
            for m in range(1, 4):
                dma("sync", win(xt, h, x0 + m, 1), win(xt, h, x0, 1), "g%d" % ck)
            dma("g", win(xt, h, x0, 4), blk(hi, 0, 4), "j%d" % ck, True)
            for m in (0, 2):
                act(blk("cmp", 18 + m, 2), win(xt, h, x0 + m, 2), -eps, -1.0, "Sign")
        slot = [0, 0]
        kk = ref("kk" if h else "k2")
        order = (4, 0, 1, 2, 3)
        for n, i in enumerate(order):
            phase[0] = "key%d_%d" % (ck, n)
            aside = hl_dma and i == 3
            pl = cols(OPT["PL"][h][n], 0, Q)
            if not aside:
                act(pl, L(i), -c2 if i == 4 else 0.0)
            for j in range(5):
                if j == i:
                    continue
                if j in order[n + 1:]:
                    c = blk("cmp", slot[0])
                    slot[0] += 1
                    near = abs(i - j) <= 2
                    if i < j:
                        op, si = (AL.is_le, "m1") if near else (AL.is_gt, "n1")
                    else:
                        op, si = (AL.is_ge, "n1") if near else (AL.is_lt, "m1")
                    tt(c, L(j), pl, op)
                    terms[i].append((si, c))
                    terms[j].append(("n1" if si == "m1" else "m1", c))
                if aside:
                    terms[i].append(("nh", blk("cmp", 18 + (j + 1) % 5)))
                else:
                    if j == 4:
                        c = blk("cmp", 22 + i if i < 3 else 18)
                    else:
                        c = blk("cmp", 10 + slot[1] % 8)
                        slot[1] += 1
                    m = tt(c, H(j), pl, AL.is_lt)
                    terms[i].append(("n1", c))
                    if h == 1 and n == OPT["AFTER"][t]:
                        ops[m]["x"].append(done[0])
                    if t and 5 * h + n == OPT["LISTS"][t - 1]:
                        ops[m]["x"].append(done[1])
            pk = cols("pk%d" % (n % 2), 0, Q)
            byact = n >= 5 - OPT["KEY_ACT"][ck] or aside
            if byact:
                mm(pk, ref("m1"), ref("cst"), True, False)
                act(pk, L(i), -c2 if i == 4 else (-2.0 if aside else 0.0))
            else:
                mm(pk, ref("f1"), L(i), True, False)
            for m, (w, c) in enumerate(terms[i]):
                mm(pk, ref(w), c, False, m == len(terms[i]) - 1)
            if n == 0:
                act(kk, pk, 0.0 if byact else -c2)
            else:
                tt(kk, kk, pk, AL.max)
        phase[0] = "low%d" % ck
        pa = cols("pa", 0, Q)
        if OPT["A_PE"][ck] == 1:
            act(ref("rr"), kk, 192.0)
            mm(pa, ref("f1"), kk, True, False)
            act(ref("rr"), ref("rr"), -192.0)
            mm(pa, ref("n1"), ref("rr"), False, True)
        elif OPT["A_PE"][ck] == 3:
            act(ref("rr"), kk, 192.0)
            mm(pa, ref("m1"), ref("cst"), True, False)
            mm(pa, ref("n1"), ref("rr"), False, False)
            mm(pa, ref("f1"), kk, False, True)
        elif OPT["A_PE"][ck] == 0:
            act(ref("rr"), kk, 192.0)
            act(pa, ref("rr"), -192.0)
            tt(pa, kk, pa, AL.subtract)
        else:
            ts(pa, kk, 1.5 * 2.0 ** 23, -1.5 * 2.0 ** 23, AL.add, AL.add)
            tt(pa, kk, pa, AL.subtract)
        if lt_dma:
            k = 1.0 - c2 if t < 2 else 1.0 + 1.0 / 128
        else:
            k = (0.0, 1.0 / 64, 1.0 / 128)[t]
        st = 2 if t == 0 else 0
        na = win(st, h, 0, 1)
        ncopy = 5 if lt_dma else (4 if le_dma else 1)
        if lt_dma:
            act(na, pa, k, -1.0)
        if t < 2:
            act(win(t + 1, 0, a, 1), pa, c2)
            if a < 3:
                share(t + 1, [(0, a)], "l%d%d" % (t, a))
        elif lt_dma:
            act(win(3, 0, a, 1), pa, c2 - 1.0 / 128, 2.0)
        elif ends:
            act(ref("a1"), pa)
            send([(ref("a1"), win(3, 0, 4 + a, 1))], "xa")
            act(cols("pm0", 0, Q), pa, 1.0 / 128)
        else:
            act(ref("a%d" % h), pa, c2)
        if not lt_dma and (le_dma or t > 0) and not ends:
            act(na, pa, k, -1.0)
        if le_dma == 2 and not lt_dma:
            ncopy = 1
        for m in range(1, ncopy):
            dma("sync", win(st, h, m, 1), na, "n%d" % ck)
        phase[0] = "high%d" % ck
        wnew = win(t + 1, 1, a, 1)
        pm = cols("pm%d" % h, 0, Q)
        if lt_dma:
            dma("g", ref(hi), win(st, h, 0, 5), "t%d" % ck, True)
            act(blk("td", lt0, 5), ref(hi), k - eps, -1.0, "Sign")
            dma("g", ref(hi), blk("td", lt0, 5), "m%d" % ck, True)
            mm(pm, ref("f1"), blk(hi, 0), True, True)
            for j in range(4):
                done[0] = tt(pm if j < 3 else wnew, H(j), pm, AL.min)
            if t == 1:
                act(win(3, 1, a, 1), wnew, 1.0 / 64 + c2)
            if t < 2:
                dma("g", wnew, win(t + 1, 0, a, 1), "b%d" % ck, True)
            else:
                dma("g", win(3, 0, a, 1), wnew, "b%d" % ck, True)
        else:
            if mask_dma:
                for j in range(4):
                    tt(LT(j), H(j), pa, AL.is_lt)
                dma("g", blk(hi, 1, 4), blk("td", lt0 + 1, 4), "m%d" % ck, True)
                tt(LT(4), H(4), pa, AL.is_lt)
                mm(pm, ref("f1"), H(4), True, False)
                mm(pm, ref("m1"), LT(4), False, True)
                for j in range(4):
                    done[0] = tt(pm if j < 3 or t == 2 else wnew, H(j), pm, AL.min)
            else:
                for n, j in enumerate(order):
                    tt(LT(j), H(j), pa, AL.is_lt)
                    if h:
                        pm = cols((("pm1", "pl0", "pk1", "pl1", "pk0"), ("pm1", "pl1", "pl0", "pk1", "pk0"))[hl_dma][n], 0, Q)
                    else:
                        pm = cols("pm%d" % (n % 2), 0, Q)
                    if n >= 5 - OPT["MASK_ACT"][ck]:
                        mm(pm, ref("m1"), ref("cst"), True, False)
                        act(pm, H(j), c2 if ends and n else 0.0)
                    else:
                        mm(pm, ref("f1"), H(j), True, False)
                    mm(pm, ref("m1"), LT(j), False, True)
                    if n == 0:
                        act(kk, pm, c2 if ends else 0.0)
                    else:
                        done[0] = tt(kk if n < 4 or ends else (wnew if t < 2 else pm), kk, pm, AL.min)
            if ends:
                send([(kk, win(3, 1, 4 + a, 1))], "xb")
                tt(win(3, 0, a, 1), kk, pa, AL.add)
                tt(wnew, kk, cols("pm0", 0, Q), AL.subtract)
                act(cols("pl0", 0, Q), win(3, 0, 4 + a, 1))
                act(cols("pl1", 0, Q), win(3, 0, 4 + a, 1), 1.0 / 128)
                tt(win(3, 0, 4 + a, 1), win(3, 1, 4 + a, 1), cols("pl0", 0, Q), AL.add)
                tt(win(3, 1, 4 + a, 1), win(3, 1, 4 + a, 1), cols("pl1", 0, Q), AL.subtract)
            elif t == 2:
                tt(win(3, 0, a, 1), ref("a%d" % h), pm, AL.add)
                tt(wnew, na, pm, AL.add)
            if t == 1:
                dma("sync", win(3, 1, a, 1), wnew, "u%d" % ck)
                dma("g", win(3, 1, a, 1), na, "v%d" % ck, True)
        if t == 2:
            share(3, [(0, a)], "z%d" % a, not ends)
            share(3, [(1, a)], "w%d" % a, not ends)
            theta(a)
        elif a < 3:
            share(t + 1, [(1, a)], "h%d%d" % (t, a))
        phase[0] = "hold%d" % ck
        if le_dma:
            if ncopy == 1:
                for j in range(4):
                    dma("g", L(j), na, "k%d_%d" % (ck, j // 2), True)
            else:
                dma("g", ref(lo), win(st, h, 0, 4), "k%d" % ck, True)
            for j in (0, 2):
                act(blk("td", le0 + j, 2), blk(lo, j, 2), k + eps, -1.0, "Sign")
        else:
            for j in range(4):
                tt(blk("td", le0 + j), L(j), pa, AL.is_le)
        pn = cols("pc", h * 96, h * 96 + 96)
        sums = [[(selv(7 if le_dma else 5, i), cols("td", le0 * Q + i, (le0 + 4) * Q, 16)) for i in range(16)],
                [(selv(8 if lt_dma else 6, i), cols("td", (lt0 + 1) * Q + i, (lt0 + 5) * Q, 16)) for i in range(16)]]
        if le_dma or not OPT["LE_FIRST"]:
            sums.reverse()
        for m in range(4):
            mms(pn, sums[m // 2][8 * (m % 2):8 * (m % 2) + 8], m == 0, m == 3)
        tt(ref("key", S_[:, :, h, :]), ref("kb%d" % p, S_[:, :, h, :]), pn, AL.add)

    def lookup(x, rows, at, more=()):
        phase[0] += "+"
        cp(ref("off"), x)
        act(ref("gg"), gath(cols("wc", 0, CW), ref("off")))
        for n, j in enumerate(rows):
            terms = [(selv(j, i), cols("gg", i, 768, 16)) for i in range(16)] + [(ref("m1"), y) for y in more]
            mms(cols("pc", at + n * 48, at + 48 + n * 48), terms, True, True)

    def control(t):
        p = t % 2
        sf, vv = "sf%d" % p, "vv%d" % p
        phase[0] = "vote%d" % t
        nine = 9.0 * 32768
        rp = ref("rn", S_[:, :, p, :])
        side = "pk0" if t == 2 else "pc"
        tt(ref("mx"), ref("key", S_[:, 0:2]), ref("key", S_[:, 2:4]), AL.max)
        tt(ref("best"), ref("mx", S_[:, 0]), ref("mx", S_[:, 1]), AL.max)
        cp(ref("bi"), ref("best"))
        ts(ref("ci"), ref("bi"), 8191, None, AL.bitwise_and)
        lookup(ref("ci"), [4], 192)
        act(ref("fall"), ref("key"), nine - 0.5, -1.0, "Sign")
        act(ref("some"), ref("best"), 0.5 - nine, 1.0, "Sign")
        tt(cols("eq", 0, 48), ref("ci"), cols(vv, 0, 48), AL.is_equal)
        tt(ref("cr"), ref("ci"), rp, AL.subtract)
        lookup(cols("pc", 192, 240), [4], 240)
        tt(cols("eq", 48, 144), ref(vv), cols("pc", 192, 288), AL.is_equal)
        pv = cols("pc", 432, 480)
        mms(pv, [(ref("m1"), ref("some"))] + [(ref("n1"), cols("eq", 48 * m, 48 * m + 48)) for m in range(3)], True, True)
        act(ref("take"), pv, func="Relu")
        tt(ref("cr"), ref("cr"), ref("take"), AL.mult)
        tt(ref("ww"), ref("cr"), rp, AL.add)
        step(ref("g1"), ref("ww"), CR, RK)
        step(ref("g2"), ref("ww"), CG, GR - RK)
        lookup(ref("ww"), [0, 1, 2, 3], 192, (ref("g1"), ref("g2")))
        act(rp, ref("ww"))
        u, nw = cols(side, 0, 192), cols("pc", 192, 384)
        for j in range(4):
            mms(cols(side, 48 * j, 48 * j + 48), [(ref("f1"), ref("best")), (ref("mb"), ref("take"))], True, True)
        tt(u, ref("key"), u, AL.is_equal)
        tt(ref("fall"), ref("fall"), u, AL.max)
        for j in range(4):
            mms(cols(side, 48 * j, 48 * j + 48), [(ref("m20"), cols("cst", 0, 48)), (ref("mq"), ref("g1")), (ref("m1"), ref("g2"))],
                True, True)
        tt(ref("fall"), ref("fall"), u, AL.mult)
        tt(ref("ok"), ref("fall"), nw, AL.is_gt)
        tt(nw, nw, ref(sf), AL.subtract)
        tt(nw, ref("ok"), nw, AL.mult)
        tt(ref(sf), ref(sf), nw, AL.add)
        cp(ref("su%d" % p), ref(sf))
        if t < 2:
            done[1] = parts(p)
            names(t + 1)
        if t == 0:
            keybase(2)

    def last(a, n):
        h, p = a // 2, a % 2
        phase[0] = "sum%d" % n
        kinds = OPT["ROWS"][n]
        nz = kinds.count("Z")

        def zt(j, m=1):
            return blk("lo%d" % n, j, m) if n < 2 else win(2, n - 2, 3 + j, m)

        def dt(j):
            return blk("hi%d" % n, j) if n < 2 else win(1, n - 2, 3 + j, 1)

        ps = cols(("pm0", "pm1", "pa", "pk1")[n], 0, Q)
        if n < OPT["OWN_ACT"]:
            mm(ps, ref("m1"), ref("cst"), True, False)
            act(ps, win(3, 1, a, 1), 0.0, 4.0)
        else:
            mm(ps, ref("f4"), win(3, 1, a, 1), True, False)
        sb = ("pl0", "pl1", "pl0", "pl1")
        one = win(2, n, 7, 1) if n < 2 else win(0, n - 2, 5, 1)
        for m in range(max(nz, 1)):
            dma("sync", win(2, n, 7 + m, 1) if n < 2 else win(0, n - 2, 5 + m, 1), win(3, 0, a, 1), "p%d" % n)

        def offs(j):
            return cols("su%d" % p, j * 48 + h * 24, j * 48 + h * 24 + 24)

        if nz:
            assert kinds[:nz] == "Z" * nz
            for j in range(nz):
                act(zt(j), gath(win(3, 0), offs(j)), 0.0, -1.0)
            src = win(2, n, 7, nz) if n < 2 else win(0, n - 2, 5, nz)
            dma("g", zt(0, nz), src, "r%d" % n, True)
            act(zt(0, nz), zt(0, nz), 0.0, -8.0, "Sigmoid")
        rows = list(range(nz, 4)) + list(range(nz))
        direct = n == 3 and kinds[rows[3]] == "Y"
        for m, j in enumerate(rows):
            z, d = zt(j), dt(j)
            end = direct and m == 3
            if kinds[j] != "Z":
                tt(z, gath(win(3, 0), offs(j)), one, AL.subtract)
            if kinds[j] == "Y":
                act(d, gath(win(3, 1), offs(j)), 0.0, 8.0 if end else 1.0)
                act(cols(sb[j], 0, Q), z, 0.0, 8.0, "Sigmoid")
                tt(d, d, cols(sb[j], 0, Q), AL.mult)
            else:
                if kinds[j] == "X":
                    act(z, z, 0.0, 8.0, "Sigmoid")
                tt(d, gath(win(3, 1), offs(j)), z, AL.mult)
            if not end:
                mm(ps, ref("f8"), d, False, m == (2 if direct else 3))
        y = blk("hi%d" % (n % 2), 4)
        if direct:
            tt(y, d, ps, AL.add)
        else:
            act(y, ps)
        dma("sync", blk("yq", a), y, "q%d" % n)

    for t in range(3):
        for h in range(2):
            drift(t, 2 * h + 1 - t % 2)
        poll(t, 0)
        poll(t, 1)
        control(t)
    phase[0] = "refs"
    act(cols("s1", 0, 96), ref("rn"), 192.0 - 0.495, 1.0 / 96)
    act(ref("r2"), ref("rn"), 0.0, 16.0)
    act(cols("dn", 0, 96), cols("s1", 0, 96), 192.0 * 1535, -1535.0)
    step(cols("dn", 96, 192), ref("rn"), CR, RK - CR // 96)
    step(cols("dd", 0, 96), ref("rn"), CG, GR - RK - CR // 96)
    for m, x in enumerate((ref("r2"), cols("dn", 0, 96), cols("dn", 96, 192), cols("dd", 0, 96))):
        mm(ref("pc", S_[0:96, 0:128]), x, ref("f1"), m == 0, m == 3)
    act(ref("rt", S_[0:96, :]), ref("pc", S_[0:96, 0:128]))
    for k in range(8):
        dma("sync", ref("yr", S_[k, :]), ref("rt", S_[0:96, 16 * k:16 * k + 16]), "out")
    for n, a in enumerate((1, 3, 0, 2)):
        last(a, n)
    return ops


def _meet(a, b):
    return a[0] <= b[1] and b[0] <= a[1] and a[2] <= b[3] and b[2] <= a[3]


def plan():
    if "plan" in _CACHE:
        return _CACHE["plan"]
    ops = build()
    hist = {}
    groups = {}
    for k, o in enumerate(ops):
        dep = set()
        for views, wr in ((o["r"], False), (o["w"], True)):
            for r in views:
                bank = _where(r["n"]) == "psum"
                for (m, s, w2) in hist.get(r["n"], []):
                    if m == k:
                        continue
                    if bank and (ops[m]["e"] != o["e"] or o["e"] == "pe"):
                        dep.add(m)
                    elif (wr or w2) and _meet(s, r["s"]) and not (o["g"] is not None and ops[m]["g"] == o["g"]):
                        dep.add(m)
        for views, wr in ((o["r"], False), (o["w"], True)):
            for r in views:
                h = hist.setdefault(r["n"], [])
                s = r["s"]
                if _where(r["n"]) == "psum":
                    if o["e"] == "pe":
                        h[:] = []
                elif wr and s[5] == s[1] - s[0] + 1 and s[4] == s[3] - s[2] + 1:
                    h[:] = [e for e in h if e[0] == k or not (s[0] <= e[1][0] and e[1][1] <= s[1] and s[2] <= e[1][2] and e[1][3] <= s[3])]
                h.append((k, s, wr))
        o["d"] = dep | set(o["after"])
        if o["g"] is not None:
            groups.setdefault(o["g"], []).append(k)
    for k, o in enumerate(ops):
        full = set()
        for m in o["d"]:
            if ops[m]["g"] is not None:
                full.update(groups[ops[m]["g"]])
            else:
                full.add(m)
        o["d"] = sorted(full)
        o["all"] = sorted(full | set(o["x"]))
    n = len(ops)
    succ = [[] for _ in range(n)]
    for k, o in enumerate(ops):
        for m in o["all"]:
            succ[m].append(k)
    indeg = [len(o["all"]) for o in ops]
    topo = [k for k in range(n) if indeg[k] == 0]
    left = list(indeg)
    for k in topo:
        for s in succ[k]:
            left[s] -= 1
            if left[s] == 0:
                topo.append(s)
    assert len(topo) == n
    pr = [0.0] * n
    for k in reversed(topo):
        pr[k] = ops[k]["c"] + ops[k]["lat"] + max([pr[s] + 80 for s in succ[k]] + [0.0])
    eng = [o["e"] for o in ops]
    cost = [o["c"] for o in ops]
    moved = [o["by"] for o in ops]

    def lag(m, s):
        early = ops[m]["k"] == "send" and m in ops[s]["x"]
        return (0.0 if early else ops[m]["lat"]) + (0.0 if eng[m] == eng[s] == "pe" else P["LAG"])

    pad = [P["PAD"][0] + P["PAD"][1] * o["by"] if o["k"] == "dma" else (P["PAD"][2] if o["k"] == "arrive" else 0.0) for o in ops]
    fw = [[(s, lag(k, s) + pad[k]) for s in succ[k]] for k in range(n)]
    bk = [[(m, lag(m, k) + pad[m]) for m in ops[k]["all"]] for k in range(n)]
    bw = [[(m, lag(m, k)) for m in ops[k]["all"]] for k in range(n)]

    def sched(pr, nxt, first, look):
        free, ready = {}, {}
        at = list(first)
        start = [0.0] * n
        left = [0] * n
        for k in range(n):
            for s, d in nxt[k]:
                left[s] += 1
        for k in range(n):
            if left[k] == 0:
                ready.setdefault(eng[k], []).append(k)
        seq, line = [], 0.0
        while len(seq) < n:
            best = None
            for e, lst in ready.items():
                if lst:
                    t0 = max(free.get(e, 0.0), min([at[k] for k in lst]))
                    if best is None or t0 < best[0]:
                        best = (t0, e)
            t0, e = best
            k = max([k for k in ready[e] if at[k] <= t0 + look], key=lambda k: pr[k])
            ready[e].remove(k)
            start[k] = max(t0, at[k])
            free[e] = end = start[k] + cost[k]
            if moved[k] and nxt is fw:
                end = max(end, line)
                line = end + moved[k] * (1.0 + P["PAD"][1])
            seq.append(k)
            for s, d in nxt[k]:
                if end + d > at[s]:
                    at[s] = end + d
                left[s] -= 1
                if left[s] == 0:
                    ready.setdefault(eng[s], []).append(s)
        return seq, start

    alts = []
    for gat, net, pe, slow, late, share, work in P["ALTS"]:
        c, mv, more = list(cost), list(moved), [0.0] * n
        for k, o in enumerate(ops):
            if o["k"] == "arrive":
                c[k] *= net
            elif o["k"] == "send":
                mv[k] *= share * net / P["OCC"]
            elif o["k"] == "dma":
                mv[k] *= slow
                more[k] = late + mv[k] - moved[k]
            else:
                c[k] *= work * (pe if o["e"] == "pe" else (gat if any(r["ind"] is not None for r in o["r"]) else 1.0))
        alts.append((c, mv, more, work))

    names = sorted(set(eng))
    en = [names.index(e) for e in eng]

    def timed(seq, alt):
        c, mv, more, work = alt
        free, prev, end, held, line = [0.0] * len(names), [-1] * len(names), [0.0] * n, [-1] * n, []
        for k in seq:
            e = en[k]
            t0, by = free[e], prev[e]
            for m, d in bw[k]:
                if end[m] + d > t0:
                    t0, by = end[m] + d, m
            held[k], prev[e] = by, k
            free[e] = end[k] = t0 = t0 + c[k]
            if mv[k]:
                at = len(line)
                while at and line[at - 1][1] > t0:
                    at -= 1
                while at < len(line) and line[at][0] < t0 + mv[k]:
                    t0 = max(t0, line[at][1])
                    at += 1
                line.insert(at, (t0, t0 + mv[k]))
                end[k] = t0 + more[k]
        return end, held

    def score(seq):
        tot = [max(timed(seq, alt)[0]) / alt[3] for alt in alts]
        _CACHE["ends"] = tot
        return sum(tot) / len(alts)

    def polish(seq, rounds):
        now = score(seq)
        best = (now, seq)
        for it in range(rounds):
            if it % 8 == 0:
                end, held = timed(seq, alts[int(rng.integers(len(alts)))])
                k, chain = max(range(n), key=lambda x: end[x]), []
                while k >= 0:
                    m = held[k]
                    if m >= 0 and en[m] == en[k] and m not in needs[k]:
                        chain.append(k)
                    k = m
                pos = [0] * n
                for i, k in enumerate(seq):
                    pos[k] = i
            v = chain[int(rng.integers(len(chain)))]
            hop, i = int(rng.geometric(0.4)), pos[v]
            while hop and i > 0:
                i -= 1
                if en[seq[i]] == en[v]:
                    hop -= 1
            take, todo = {v}, [v]
            while todo:
                for m in needs[todo.pop()]:
                    if pos[m] >= i and m not in take:
                        take.add(m)
                        todo.append(m)
            if seq[i] in take or len(take) > 12:
                continue
            mid = seq[i:pos[v] + 1]
            new = seq[:i] + [k for k in mid if k in take] + [k for k in mid if k not in take] + seq[pos[v] + 1:]
            sc = score(new)
            if sc < now + P["TEMP"] * (1.0 - it / rounds) * rng.random():
                seq, now = new, sc
                for j in range(i, pos[v] + 1):
                    pos[seq[j]] = j
                if now < best[0]:
                    best = (now, seq)
        return best[1]

    needs = [set(o["all"]) for o in ops]

    rng = np.random.default_rng(P["SEED"])
    zero = [0.0] * n
    tail = [o["lat"] for o in ops]
    pr = [x + P["SOON"].get(o["t"], 0.0) for x, o in zip(pr, ops)]
    seq, start = sched(pr, fw, zero, 30)
    best = (score(seq), seq, start, pr, 30)
    cur = best
    for it in range(P["ITER"]):
        amp = (50.0, 300.0, 1000.0)[it % 3]
        look = (30, 150, 300)[(it // 3) % 3]
        back = [cur[2][k] + cost[k] + x for k, x in enumerate(amp * rng.random(n))]
        s2, st2 = sched(back, bk, tail, look)
        fore = [st2[k] + cost[k] + x + P["SOON"].get(ops[k]["t"], 0.0) for k, x in enumerate(amp * rng.random(n))]
        seq, start = sched(fore, fw, zero, look)
        sc = score(seq)
        if sc < cur[0] + 400.0:
            cur = (sc, seq, start, fore, look)
        if sc < best[0]:
            best = cur
    tags = sorted(set(o["t"] for o in ops))
    for it in range(P["MOVES"]):
        tag = tags[int(rng.integers(len(tags)))]
        by = float(rng.choice([-1.0, 1.0]) * rng.choice([200.0, 500.0, 1200.0, 3000.0]))
        look = best[4] if rng.random() < 0.8 else int(rng.choice([30, 150, 300, 600]))
        who = (None, "act", "dve", "pe", "g")[int(rng.integers(5))]
        fore = [x + by if o["t"] == tag and who in (None, o["e"]) else x for x, o in zip(best[3], ops)]
        seq, start = sched(fore, fw, zero, look)
        sc = score(seq)
        if sc < best[0]:
            best = (sc, seq, start, fore, look)
    seq = _CACHE["fix"] if "fix" in _CACHE else polish(best[1], P["POLISH"])
    end = timed(seq, alts[0])[0]
    start = [end[k] - cost[k] for k in range(n)]
    fin = [start[k] + cost[k] + tail[k] for k in range(n)]
    _CACHE["score"] = score(seq)
    _CACHE["plan"] = (ops, seq, groups, start, fin)
    return _CACHE["plan"]


def rank_program(g, core, T, topo):
    rank = T.rank_of(core)
    n = len(T.cores)
    ops, seq, groups, start, fin = plan()
    gsem = {name: "s%d" % k for k, name in enumerate(sorted(groups))}

    def helper(src, dst):
        if topo.chip(src) == topo.chip(dst):
            return None
        return [c for c in topo.cores_of(src) if c not in T.cores and topo.die(c) != topo.die(src) and topo.may_write(c, dst)][0]

    def fused(to, engines, views, remote, local):
        r, p = topo.addr(to)[0:2]
        per = len(engines) // len(views)
        g.remote_dma_fused([RemoteDMATransfer(dst_ids=[DstId(rid=r, pnc=p)], remote_sem=T.sem[remote], src=s, dst=d,
                                              dma_engine_mask=sum(1 << x for x in engines[m * per:(m + 1) * per]))
                            for m, (s, d) in enumerate(views)], local_sem=T.sem[local])

    if rank is None:
        for r in range(n):
            src, dst = T.cores[r], T.cores[(r - 1) % n]
            if helper(src, dst) == core:
                spare = [x for x in topo.engines(src, core) if x not in topo.engines(src, dst)]
                out = topo.engines(core, dst)
                todo = [ops[k]["a"] for k in seq if ops[k]["k"] == "send" and ops[k]["a"][1] in OPT["VIA"]]
                for pairs, grp in todo:
                    g.wait_ge(T.sem[gsem[grp]], len(spare))
                    fused(dst, out, [(T[d["n"]][d["i"]], T[d["n"]][d["i"]]) for s, d in pairs], gsem[grp], "sent")
                g.wait_ge(T.sem["sent"], len(out) * len(todo))
        return
    prev, nxt = T.cores[(rank - 1) % n], T.cores[(rank + 1) % n]
    rid, pid = topo.addr(prev)[0:2]
    eng = topo.engines(core, prev)
    got = len(topo.engines(nxt, core))
    via = helper(core, prev)
    queue = {"g": g, "pe": g.tensor, "act": g.scalar, "dve": g.vector, "sync": g.sync}
    total = {}
    for name, ks in groups.items():
        kind = ops[ks[0]]["k"]
        total[gsem[name]] = 16 * len(ks) if kind == "dma" else (got if kind == "arrive" else len(eng))
    count = {}
    mark = {}
    clock = {}
    known = {e: {} for e in queue}

    def ap(r):
        a = T[r["n"]][r["i"]]
        if r["ind"] is not None:
            a = a.indirect(ap(r["ind"]))
        return a

    def val(s):
        return ap(s) if isinstance(s, dict) else s

    for k in seq:
        o = ops[k]
        e, kind, a = o["e"], o["k"], o["a"]
        if kind == "arrive":
            mark[k] = (gsem[o["g"]], got)
            clock[k] = {}
            continue
        q = queue[e]
        need = {}
        for m in o["d"]:
            if e == "pe" and ops[m]["e"] == "pe":
                continue
            s, v = mark[m]
            assert s != "sent"
            if known[e].get(s, 0) < v:
                need[s] = max(need.get(s, 0), v)
        for m in o["d"]:
            if mark[m][0] in need and mark[m][1] <= need[mark[m][0]]:
                for s, v in clock[m].items():
                    if s in need and need[s] <= v and s != mark[m][0]:
                        need[s] = 0
        for s in sorted(need):
            if need[s]:
                q.wait_ge(T.sem[s], need[s])
        for m in o["d"]:
            if e == "pe" and ops[m]["e"] == "pe":
                continue
            for s, v in list(clock[m].items()) + [mark[m]]:
                if known[e].get(s, 0) < v:
                    known[e][s] = v
        clock[k] = dict(known[e])
        if kind == "dma":
            if a[2]:
                ins = q.dma_start(ap(a[0]), ap(a[1]), accum_op=AL.add)
            else:
                ins = q.dma_start(ap(a[0]), ap(a[1]))
            ins.then_inc(T.sem[gsem[o["g"]]], 16)
            mark[k] = (gsem[o["g"]], total[gsem[o["g"]]])
            continue
        if kind == "send":
            pairs, grp = a
            loc = gsem[o["g"]] if o["g"] is not None else "sent"
            per = len(eng) // len(pairs)
            masks = [sum(1 << x for x in eng[m * per:(m + 1) * per]) for m in range(len(pairs))]
            if grp in OPT["VIA"] and via is not None:
                spare = [x for x in topo.engines(core, via) if x not in eng]
                assert len(spare) == len(eng)
                fused(via, spare, [(ap(s), ap(d)) for s, d in pairs], gsem[grp], loc)
            elif len(pairs) == 1:
                g.remote_dma(ap(pairs[0][1]), ap(pairs[0][0]), T.sem[gsem[grp]], T.sem[loc], pid, rid, masks[0])
            else:
                g.remote_dma_fused([RemoteDMATransfer(dst_ids=[DstId(rid=rid, pnc=pid)], dma_engine_mask=masks[m],
                                                      remote_sem=T.sem[gsem[grp]], src=ap(s), dst=ap(d))
                                    for m, (s, d) in enumerate(pairs)], local_sem=T.sem[loc])
            if loc == "sent":
                total["sent"] = total.get("sent", 0) + len(eng)
            mark[k] = (loc, len(eng))
            continue
        if kind == "tt":
            ins = q.tensor_tensor(ap(a[0]), ap(a[1]), ap(a[2]), a[3])
        elif kind == "ts":
            if a[5] is None:
                ins = q.tensor_scalar(ap(a[0]), ap(a[1]), val(a[2]), None, a[4])
            else:
                ins = q.tensor_scalar(ap(a[0]), ap(a[1]), val(a[2]), val(a[3]), a[4], a[5])
        elif kind == "cp":
            ins = q.tensor_copy(ap(a[0]), ap(a[1]))
        elif kind == "ms":
            ins = q.memset(ap(a[0]), a[1])
        elif kind == "act":
            f = {"Sigmoid": AF.Sigmoid, "Identity": AF.Identity, "Sign": AF.Sign, "Relu": AF.Relu, "Abs": AF.Abs}[a[2]]
            ins = q.activation(ap(a[0]), ap(a[1]), f, bias=a[3], scale=a[4])
        elif kind == "mm":
            ins = q.matmul(ap(a[0]), ap(a[1]), ap(a[2]), a[3], a[4])
        elif kind == "mms":
            for c in a:
                ins = q.matmul(ap(c[0]), ap(c[1]), ap(c[2]), c[3], c[4])
        else:
            if SCRATCH[a[0]["n"]][2] == "int32":
                ins = q.iota(ap(a[0]), a[1], a[2], a[3])
            else:
                ins = q.iota(ap(a[0]), a[1], a[2], a[3], allow_small_or_imprecise_dtypes=True)
        s = "pool" if e == "g" else e
        count[s] = count.get(s, 0) + 1
        ins.then_inc(T.sem[s], 1)
        mark[k] = (s, count[s])
    total.update(count)
    for s in sorted(total):
        g.wait_ge(T.sem[s], total[s])
